import numpy as np, ml_dtypes
CORES = [40,64,80,88,96,104,120,144]
N = 8
BF = ml_dtypes.bfloat16
def gentries(a):
    return np.ascontiguousarray(a.reshape(8, 16, -1).transpose(0, 2, 1)).reshape(8, -1)
def gtable(e):
    e = np.asarray(e); return np.ascontiguousarray(e.reshape(8, -1, 16).transpose(0, 2, 1)).reshape(128, -1).astype(np.int32)
P, LG, I, K, M, RO = 4096, 12, 128, 48, 32, 4
RHO, KA, KB, LIGHT, HALF = 68, 17, 5, 48, 7168
def lists(rng):
    return np.argsort(rng.random((N, 8, 4, P)), axis=-1)
def parts(rng):
    x = rng.integers(0, 256, (N, 8, 16, P)); z = rng.integers(0, 256, (N, 8, 16, 4 * I))
    lev = rng.permuted(np.tile(np.array([0.95, 0.83, 0.74, 0.69, 0.65, 0.6, 0.53, 0.42]), (N, 1)), axis=1)
    w = np.minimum(rng.geometric(lev[:, :, None], (N, 8, P)), 8)
    return x, w, z, lists(rng)
def pack(x, w, z, mem):
    return {"pt": np.ascontiguousarray(x.reshape(N, 128, P)).astype(np.float32).astype(BF), "w0": np.ascontiguousarray(w).astype(np.float32).astype(BF),
            "z0": np.ascontiguousarray(z.reshape(N, 128, 4 * I)).astype(np.float32).astype(BF), "lm": np.stack([gtable(a.reshape(8, -1)) for a in mem])}
def total(rng, s):
    e = (s - P) >> 4; w = np.ones(P, np.int64); w[:e] = 8; w[e:e + s - P - 7 * e] = 2
    return rng.permutation(w)
def setup_inputs(rng):
    return pack(*parts(rng))
def setup_inputs_spread(rng):
    def uneven(n):
        v = np.floor(np.exp2(8 * rng.random((N, 8, 1, n))) * rng.random((N, 8, 16, n))).astype(np.int64)
        return np.where(rng.random(v.shape) < 0.5, v, 255 - v)
    x, z = uneven(P), uneven(4 * I)
    ex = rng.permuted(np.tile(np.array([1.0, 2.0, 3.0, 5.0, 8.0, 12.0, 16.0, 24.0]), (N, 1)), axis=1)
    w = 1 + np.minimum(np.floor(8 * rng.random((N, 8, P)) ** ex[:, :, None]).astype(np.int64), 7)
    return pack(x, w, z, lists(rng))
def setup_inputs_ends(rng):
    def two(n):
        e = 255 * rng.integers(0, 2, (N, 8, 16, n)); m = rng.integers(0, 7, (N, 8, 1, n))
        return np.where(m == 0, 0, np.where(m == 1, 255, e))
    x, z = two(P), two(4 * I); w = np.ones((N, 8, P), np.int64)
    s = rng.permuted(np.tile(np.array([0.02, 0.06, 0.1, 0.15, 0.3, 0.5]), (N, 1)), axis=1)
    w[:, 1:7] = np.where(rng.random((N, 6, P)) < s[:, :, None], 8, 1); w[:, 1:7, 0] = 8; w[:, 1:7, P - 1] = 8
    w[0::2, 0] = 8; w[1::2, 7] = 8
    z[:, 1:6:2, :, I - 1::I] = 255; z[:, 0:7:2, :, I - 1::I] = 0
    for r in (0, N - 1): x[r, 7] = 255 * (rng.random((16, P)) < 0.03125)
    z[0, 7] = 255; z[1, 7] = 255
    inner = np.arange(4 * I) % I < I - 1; coin = rng.random((2, 4 * I)) < 0.5
    z[0:2, 7, 7] = np.where(inner & coin, 254, 255); z[0:2, 7, 15] = np.where(inner & ~coin, 254, 255)
    h = np.arange(P >> 1); seq = np.stack([h, P - 1 - h], axis=1).reshape(I, M)
    lan = np.argsort(rng.random((N, 4, 4, I)), axis=-1)
    lan[:, :, 0] = np.concatenate([1 + np.argsort(rng.random((N, 4, I - 1)), axis=-1), np.zeros((N, 4, 1), np.int64)], axis=-1)
    mem = lists(rng); mem[:, 0::2] = seq[lan].reshape(N, 4, 4, P)
    return pack(x, w, z, mem)
def setup_inputs_corners(rng):
    x, w, z, mem = parts(rng); o = [int(a) for a in rng.permutation(8)]
    x[:, o[0]] = rng.integers(100, 101 + (RHO >> 1), (N, 16, P)); z[:, o[0]] = rng.integers(100, 101 + (RHO >> 1), (N, 16, 4 * I))
    b = rng.integers(110, 141, (1, 16, 1)); x[:, o[1]] = b
    n = rng.choice(np.array([11, 12, 13, 16]), (N, 1, 4 * I)); pl = np.argsort(rng.random((N, 16, 4 * I)), axis=1)
    z[:, o[1]] = b + np.where(pl < n, RHO, RHO + 1) * rng.choice(np.array([-1, 1]), (N, 16, 4 * I))
    x[:, o[2]] = rng.integers(200, 256, (N, 16, P)); z[:, o[2]] = rng.integers(0, 21, (N, 16, 4 * I))
    for r in range(N):
        w[r, o[0]] = total(rng, (HALF, HALF + 1, 2 * P, 2 * P - 1)[r % 4]); w[r, o[3]] = total(rng, (2 * P + 1, 2 * P, 2 * P - 1, P)[r % 4])
        k = rng.integers(0, 4, (I, 1)); k[:4, 0] = rng.permutation(4); k[I - 1, 0] = 1 + r % 2
        twos = np.where(k == 0, 0, np.where(k == 1, (M >> 1) - 1, M >> 1))
        v = np.where(k == 3, 8, np.where(np.arange(M)[None, :] < twos, 2, 1))
        w[r, o[2], mem[r, o[2], 0]] = v.reshape(-1)
    w[:, o[4]] = 8; w[:, o[5]] = 1; w[:, o[6]] = 1; w[:, o[6], :P >> 2] = 8
    m = rng.integers(0, 3, (N, 1, 4 * I)); z[:, o[7]] = np.where(m == 0, 0, np.where(m == 1, 255, z[:, o[7]]))
    return pack(x, w, z, mem)
def setup_inputs_crowd(rng):
    x, w, z, mem = parts(rng); o = [int(a) for a in rng.permutation(8)]
    j = o.index(7 - o[0]); o[j], o[7] = o[7], o[j]
    for g in o[:5]:
        x[:, g] = rng.integers(200, 256, (N, 16, P)); z[:, g] = rng.integers(0, 21, (N, 16, 4 * I))
    w[:, o[0]] = rng.integers(2, 9, (N, P)); w[:, o[1]] = rng.integers(2, 9, (N, P)); w[:, o[2]] = 1; w[:, o[3]] = 1
    for r in range(N):
        a = int(rng.integers(0, I)); a = I - 1 if r == 0 else 0 if r == 1 else a
        z[r, o[1], :, a::I] = 227
        a = int(rng.integers(0, I)); a = I - 1 if r == N - 1 else a
        w[r, o[3], mem[r, o[3], 0, a * M:(a + 1) * M]] = 8
    mem[:, o[4], 1] = mem[:, o[4], 0].reshape(N, -1, 2, M)[:, :, ::-1].reshape(N, P)
    z[:, o[4], :, 1:I:2] = 227; w[:, o[4]] = np.minimum(rng.geometric(0.9, (N, P)), 8)
    z[:, o[5]] = 0
    x[:, o[6]] = rng.integers(200, 256, (N, 16, P)); z[:, o[6]] = 227; w[:, o[6]] = 1
    for r in range(N):
        n = int(rng.integers(7 * I >> 4, (17 * I >> 5) + 1)); a = rng.permutation(I)[:n]
        zv = z[(r + 1) % N, o[6]]; zv[:, a] = rng.integers(0, 21, (16, n))
        wv = w[r, o[6]]; wv[mem[r, o[6], 0].reshape(I, M)[a, :M >> 4]] = 8
    x[:, o[7]] = rng.integers(200, 256, (N, 16, P)); z[:, o[7]] = rng.integers(0, 21, (N, 16, 4 * I)); w[:, o[7]] = rng.integers(2, 9, (N, P))
    z[:, o[7], :, :I] = 227; z[:, o[7], :, 2 * I:3 * I] = 227
    for r in range(1, N, 2):
        a = int(rng.integers(0, I)); a = I - 1 if r == N - 1 else 0 if r == 1 else a
        z[r, o[7], :, I + a] = 227
    return pack(x, w, z, mem)
def check_inputs(d):
    bad = []
    for k, lo, hi in (("pt", 0, 255), ("w0", 1, 8), ("z0", 0, 255), ("lm", 0, P - 1)):
        a = np.asarray(d[k]).astype(np.float64)
        if not np.all((a >= lo) & (a <= hi)): bad.append("range of " + k)
        if np.any(a != np.floor(a)): bad.append("whole numbers of " + k)
    e = np.sort(np.stack([gentries(a) for a in np.asarray(d["lm"])]).reshape(-1, P), axis=1)
    if np.any(e != np.arange(P)[None, :]): bad.append("lm: the members of a class are all different")
    return bad
def reference(pt, w0, z0, lm):
    x = pt.astype(np.float32).astype(np.int64).reshape(N, 8, 16, P); w = w0.astype(np.float32).astype(np.int64).reshape(N, 8, P)
    z = z0.astype(np.float32).astype(np.int64).reshape(N, 8, 16, 4 * I); mem = np.stack([gentries(a) for a in lm]).astype(np.int64).reshape(N, 8, 4, I, M)
    kap = KA + KB * np.arange(K); cof = 2 * np.arange(16) + 1
    A = np.zeros((N, 8), np.int64); tally = np.zeros((N, 8, RO), np.int64)
    for t in range(RO):
        c = (t % 4, (t + 1) % 4); zn = z.copy()
        for r in range(N):
            q = (r + 1 + t % (N - 1)) % N
            for g in range(8):
                zz = [z[q, g, :, a * I:(a + 1) * I] for a in c]
                wg = w[r, g].copy(); T = min(int(np.sum(wg)), 2 * P); E = np.repeat(np.arange(P), wg)[:T]
                u = np.dot(cof, zz[0])
                h = (((u[:, None] * kap[None, :]) >> 4) + 61 * np.arange(I)[:, None] + A[r, g]) & (P - 1)
                net = E[(h * (T >> 1)) >> (LG - 1)]
                p = x[r, g][:, net]
                miss = [~np.any(np.sum(np.abs(p - b[:, :, None]) <= RHO, axis=0) >= 12, axis=1) for b in zz]
                y = (np.max(p, axis=2) + np.min(p, axis=2)) >> 1
                mark = np.zeros(P, bool); heavy = 0
                for m in (0, 1):
                    sel = miss[0] if m == 0 else miss[1] & ~miss[0]
                    s = np.sum(wg[mem[r, g, c[m]]], axis=1); light = sel & (s < LIGHT)
                    mark[mem[r, g, c[m]][light]] = True; heavy = heavy + int(np.sum(sel & ~light))
                    zn[q, g, :, c[m] * I:(c[m] + 1) * I] = np.where(sel[None, :], (zz[m] + y) >> 1, zz[m])
                wg = np.where(mark, np.minimum(2 * wg, 8), wg)
                if int(np.sum(wg)) > HALF: wg = (wg + 1) >> 1
                w[r, g] = wg; A[r, g] = heavy; tally[r, g, t] = heavy
        z = zn
    return {"yw": w.astype(np.float32), "yz": z.reshape(N, 128, 4 * I).astype(np.float32).astype(BF), "ya": tally.astype(np.float32)}

@@ -1,0 +1,568 @@
+from concourse.bass import DstId, RemoteDMATransfer
+from concourse.mybir import dt, AluOpType, AxisListType, ActivationFunctionType
+
+OP = AluOpType
+AF = ActivationFunctionType
+NR = 8
+ROUNDS = 4
+BLK = 1024
+OD0, OA0, OA1, OMX, OMN = 8192, 14336, 18432, 22528, 28672
+WDMA = (1, 2)
+VO = (0, 1, 2, 3)
+
+MSG = [
+    ("i01", "z0s", 0, 256, -1, "zin0", 0), ("i2", "z0s", 256, 384, -2, "zin1", 1), ("i3", "z0s", 384, 512, -3, "zin2", 1),
+    ("u0", "zo0", 128, 256, -1, "zr1", 0), ("c0", "zo0", 0, 128, -3, "zc0", 1),
+    ("u1", "zo1", 128, 256, -1, "zr2", 0), ("f1", "zo1", 0, 128, 2, "zf1", 1),
+    ("u2", "zo2", 128, 256, -1, "zr3", 0), ("f2", "zo2", 0, 128, 3, "zf2", 1),
+    ("f3", "zo3", 0, 256, 4, "zf3", 0)]
+
+_B, _F, _I, _U = "bfloat16", "float32", "int32", "uint16"
+SCRATCH = {}
+for _n, _w, _d in [
+        ("big", 32768, _B), ("ptb", 4112, _B), ("diffp", 4096, _B), ("pE", 8192, _B), ("zeros", 8192, _B),
+        ("wrep", 4096, _B), ("b0r", 2048, _B), ("sg1", 4096, _B), ("invw", 4096, _F), ("vals", 4096, _F),
+        ("zrep", 2048, _B), ("ind", 2048, _B), ("mkx", 2048, _B), ("mkn", 2048, _B),
+        ("lmI", 1024, _I), ("lm16", 1024, _U), ("inv16", 1024, _U), ("invt", 256, _F),
+        ("dg", 2048, _B), ("rp", 2048, _B), ("ident", 128, _B), ("nident", 128, _B), ("bo", 128, _B), ("bot", 128, _B),
+        ("lt", 128, _B), ("bo32", 128, _F), ("lt32", 128, _F), ("one32", 128, _F), ("row0", 128, _F), ("i976", 128, _F),
+        ("kl", 384, _F), ("pI", 8, _I), ("aF", 8, _F), ("gq", 128, _F), ("orl", 128, _B), ("cb", 248, _B), ("ncb", 248, _B),
+        ("m128", 272, _F), ("wt", 256, _B), ("woff", 272, _B), ("ex", 264, _F), ("off16", 256, _U), ("w2", 256, _B), ("wf", 256, _B),
+        ("w1", 256, _F), ("smv", 8, _F), ("smi", 8, _I), ("a16", 8, _F), ("thf", 8, _F), ("yab", 4, _F), ("ywb", 256, _F),
+        ("acc", 8, _F), ("jk", 256, _B), ("zf32", 128, _F), ("z0T", 128, _B), ("dzT", 128, _B),
+        ("hI", 384, _I), ("pos16", 384, _U), ("hb0", 384, _B), ("hb1", 384, _B), ("thr", 256, _F), ("sel", 256, _F), ("nh0", 128, _F),
+        ("m1", 128, _F), ("x1", 128, _F), ("L01", 256, _B), ("mx", 128, _B), ("mn", 128, _B), ("q01", 256, _I), ("e01", 256, _B),
+        ("z0s", 512, _B), ("zin0", 256, _B), ("zin1", 128, _B), ("zin2", 128, _B), ("zr1", 128, _B), ("zr2", 128, _B),
+        ("zr3", 128, _B), ("zc0", 128, _B), ("zf1", 128, _B), ("zf2", 128, _B), ("zf3", 256, _B),
+        ("zo0", 256, _B), ("zo1", 256, _B), ("zo2", 256, _B), ("zo3", 256, _B)]:
+    SCRATCH[_n] = ("sbuf", [128, _w], _d)
+for _m in MSG:
+    SCRATCH["y_" + _m[0]] = ("sbuf", [128, _m[3] - _m[2]], _B)
+for _n, _w in [("psA", 1024), ("psB", 1024), ("psC0", 512), ("psC1", 512), ("psM", 512), ("psS", 512)]:
+    SCRATCH[_n] = ("psum", [128, _w], _F)
+
+SEMAPHORES = ["kv", "ks", "kt", "kg", "ls"] + ["d%d" % i for i in range(40)] + ["m_" + m[0] for m in MSG] + ["q_" + m[0] for m in MSG]
+
+
+def relay_of(src, dst, which, T, topo):
+    if topo.may_write(src, dst):
+        return None
+    c = [x for x in topo.cores_of(src) if x != src and T.rank_of(x) is None and topo.may_write(x, dst) and topo.may_write(src, x)]
+    near = [x for x in c if topo.die(x) == topo.die(src)]
+    c = near if near else c
+    return c[which % len(c)]
+
+
+def mask_for(src, dst, far_src, far_dst, topo):
+    m = 0
+    ok = topo.engines(src, dst)
+    for e in topo.engines(far_src, far_dst):
+        if e in ok:
+            m |= 1 << e
+    return m
+
+
+def popcount(m):
+    return bin(m).count("1")
+
+
+def rank_program(g, core, T, topo):
+    rank = T.rank_of(core)
+    cores = list(T.cores)
+    if rank is not None:
+        rank_main(g, core, rank, cores, T, topo)
+        return
+    sent = 0
+    for kind, sbuf, lo, hi, off, land, which in MSG:
+        for r in range(NR):
+            src, dst = cores[r], cores[(r + off) % NR]
+            if relay_of(src, dst, which, T, topo) == core:
+                m = mask_for(core, dst, core, dst, topo)
+                g.wait_ge(T.sem["q_" + kind], popcount(mask_for(src, core, core, dst, topo)))
+                rid, pid = topo.addr(dst, core)
+                g.remote_dma(T[land][:], T["y_" + kind][:], T.sem["m_" + kind], T.sem.ls, pid, rid, m)
+                sent += popcount(m)
+    if sent:
+        g.wait_ge(T.sem.ls, sent)
+
+
+def rank_main(g, core, rank, cores, T, topo):
+    Q = {"v": g.vector, "s": g.scalar, "t": g.tensor, "g": g, "y": g.sync}
+    SEMOF = {"v": "kv", "s": "ks", "t": "kt", "g": "kg"}
+    count = {}
+    waited = {q: {} for q in Q}
+    hist = {}
+    nd = [0]
+
+    def need(q, name, lo, hi, write, toks):
+        ps = name.startswith("ps")
+        for (l, h, wr, sem, val, qq) in hist.get(name, []):
+            if qq == q and qq in SEMOF:
+                if not (l < hi and lo < h) or not wr or (ps and q == "t"):
+                    continue
+            elif ps:
+                if l // 512 > (hi - 1) // 512 or lo // 512 > (h - 1) // 512:
+                    continue
+            elif not (l < hi and lo < h) or not (wr or write):
+                continue
+            if toks.get(sem, 0) < val:
+                toks[sem] = val
+
+    def note(name, lo, hi, write, sem, val, q):
+        L = hist.get(name, [])
+        if write:
+            L = [e for e in L if not (lo <= e[0] and e[1] <= hi)]
+        else:
+            L = [e for e in L if not (not e[2] and e[5] == q and q in SEMOF and lo <= e[0] and e[1] <= hi)]
+        L.append((lo, hi, write, sem, val, q))
+        hist[name] = L
+
+    def waits(q, reads, writes):
+        toks = {}
+        for x in reads:
+            need(q, x[1], x[2], x[3], False, toks)
+        for x in writes:
+            need(q, x[1], x[2], x[3], True, toks)
+        for sem, val in toks.items():
+            if waited[q].get(sem, 0) < val:
+                Q[q].wait_ge(T.sem[sem], val)
+                waited[q][sem] = val
+
+    def b(name, lo, hi, step=1):
+        return (T[name][:, lo:hi:step] if step != 1 else T[name][:, lo:hi], name, lo, hi)
+
+    def ap(x):
+        return x[0] if isinstance(x, tuple) else x
+
+    def emit(q, fn, reads, writes):
+        reads = [x for x in reads if isinstance(x, tuple)]
+        waits(q, reads, writes)
+        sem = SEMOF[q]
+        count[sem] = count.get(sem, 0) + 1
+        fn().then_inc(T.sem[sem], 1)
+        for x in reads:
+            note(x[1], x[2], x[3], False, sem, count[sem], q)
+        for x in writes:
+            note(x[1], x[2], x[3], True, sem, count[sem], q)
+
+    def dma(q, pairs):
+        sem = "d%d" % nd[0]
+        nd[0] += 1
+        n = 16 * len(pairs)
+        waits(q, [p[1] for p in pairs if isinstance(p[1], tuple)], [p[0] for p in pairs if isinstance(p[0], tuple)])
+        for o, i in pairs:
+            Q[q].dma_start(ap(o), ap(i)).then_inc(T.sem[sem], 16)
+        for o, i in pairs:
+            if isinstance(i, tuple):
+                note(i[1], i[2], i[3], False, sem, n, q + "dma")
+        for o, i in pairs:
+            if isinstance(o, tuple):
+                note(o[1], o[2], o[3], True, sem, n, q + "dma")
+        count[sem] = n
+
+    def tt(o, x, y, op):
+        emit("v", lambda: g.vector.tensor_tensor(o[0], x[0], y[0], op), [x, y], [o])
+
+    def ts(o, x, s1, op0, s2=None, op1=None):
+        if op1 is None:
+            emit("v", lambda: g.vector.tensor_scalar(o[0], x[0], ap(s1), None, op0), [x, s1], [o])
+        else:
+            emit("v", lambda: g.vector.tensor_scalar(o[0], x[0], ap(s1), ap(s2), op0, op1), [x, s1, s2], [o])
+
+    def cp(o, x):
+        emit("v", lambda: g.vector.tensor_copy(o[0], x[0]), [x], [o])
+
+    def ms(o, c):
+        emit("v", lambda: g.vector.memset(o[0], c), [], [o])
+
+    def red(o, x):
+        emit("v", lambda: g.vector.tensor_reduce(o[0], x[0], AxisListType.X, OP.add), [x], [o])
+
+    def scan(o, d0, d1, op0, op1):
+        emit("v", lambda: g.vector.tensor_tensor_scan(o[0], d0[0], d1[0], 0.0, op0, op1), [d0, d1], [o])
+
+    def act(o, x, func, bias=0.0, scale=1.0):
+        emit("s", lambda: g.scalar.activation(o[0], x[0], func, bias=bias, scale=ap(scale)), [x, scale], [o])
+
+    def total(o, x):
+        j = b("jk", 0, 256)
+        emit("s", lambda: g.scalar.activation(j[0], x[0], AF.Copy, accum_out=o[0]), [x], [j, o])
+
+    def mm(o, l, r, start, stop):
+        emit("t", lambda: g.tensor.matmul(o[0], l[0], r[0], start, stop), [l, r], [o])
+
+    def asel(o, i, pattern, op, base, cm):
+        emit("g", lambda: g.affine_select(o[0], i[0], pattern, op, 0.0, base, cm), [i], [o])
+
+    def iota(o, pattern, base, cm, flag=True):
+        if flag:
+            emit("g", lambda: g.iota(o[0], pattern, base, cm, allow_small_or_imprecise_dtypes=True), [], [o])
+        else:
+            emit("g", lambda: g.iota(o[0], pattern, base, cm), [], [o])
+
+    def gath(q, o, win, off):
+        if q == "s":
+            emit("s", lambda: g.scalar.activation(o[0], win[0].indirect(off[0]), AF.Copy), [win, off], [o])
+        else:
+            emit("v", lambda: g.vector.tensor_copy(o[0], win[0].indirect(off[0])), [win, off], [o])
+
+    for kind, sbuf, lo, hi, off, land, which in MSG:
+        src = cores[(rank - off) % NR]
+        rel = relay_of(src, core, which, T, topo)
+        far = src if rel is None else rel
+        count["m_" + kind] = popcount(mask_for(far, core, far, core, topo))
+        note(land, 0, hi - lo, True, "m_" + kind, count["m_" + kind], "net")
+
+    def send(kind):
+        for k, sbuf, lo, hi, off, land, which in MSG:
+            if k == kind:
+                dst = cores[(rank + off) % NR]
+                rel = relay_of(core, dst, which, T, topo)
+                src = b(sbuf, lo, hi)
+                waits("g", [src], [])
+                if rel is None:
+                    m, to, out, sem = mask_for(core, dst, core, dst, topo), dst, T[land][:], "m_" + kind
+                else:
+                    m, to, out, sem = mask_for(core, rel, rel, dst, topo), rel, T["y_" + kind][:], "q_" + kind
+                rid, pid = topo.addr(to, core)
+                g.remote_dma(out, src[0], T.sem[sem], T.sem.ls, pid, rid, m)
+                count["ls"] = count.get("ls", 0) + popcount(m)
+
+    dma("y", [(b("wt", 0, 256), T.w0[:])])
+    dma("s", [(b("z0s", 0, 512), T.z0[:])])
+    for k in range(4):
+        dma("y", [(b("ptb", 16 + 1024 * k, 1040 + 1024 * k), T.pt[:, 1024 * k:1024 * k + 1024])])
+    dma("y", [(b("lmI", 0, 1024), T.lm[:])])
+    ms(b("zrep", 0, 2048), 1.0)
+    ms(b("ptb", 0, 16), 0.0)
+    ms(b("one32", 0, 128), 1.0)
+    ms(b("m128", 0, 272), -128.0)
+    ms(b("woff", 0, 8), 128.0)
+    ms(b("a16", 0, 8), 0.0)
+    ms(b("cb", 0, 248), 0.0)
+
+    iota(b("pI", 0, 1), [[0, 1]], 0, 1, False)
+    asel(b("ident", 0, 128), b("zrep", 0, 128), [[-1, 128]], OP.is_equal, 0, 1)
+    asel(b("bot", 0, 128), b("zrep", 0, 128), [[-16, 8], [0, 16]], OP.is_ge, 0, 1)
+    asel(b("bo", 0, 128), b("bot", 0, 128), [[16, 8], [0, 16]], OP.is_ge, 15, -1)
+    asel(b("lt", 0, 128), b("bo", 0, 128), [[1, 128]], OP.is_ge, -1, -1)
+    ts(b("nident", 0, 128), b("ident", 0, 128), -1.0, OP.mult)
+    send("i01")
+    asel(b("rp", 0, 2048), b("zrep", 0, 2048), [[-1, 16], [-16, 8], [0, 16]], OP.is_equal, 0, 1)
+    send("i2")
+    send("i3")
+    kl = b("kl", 0, 384)
+    iota(kl, [[80, 3], [0, 8], [5, 16]], 17, 0)
+    asel(kl, kl, [[0, 3], [-16, 8], [0, 16]], OP.is_ge, 0, 1)
+    asel(kl, kl, [[0, 3], [16, 8], [0, 16]], OP.is_ge, 15, -1)
+    asel(b("row0", 0, 128), b("one32", 0, 128), [[0, 128]], OP.is_equal, 0, 1)
+    iota(b("i976", 0, 128), [[976, 128]], 0, 0)
+    iota(b("gq", 0, 128), [[1, 8], [0, 16]], 0, 0)
+    iota(b("vals", 0, 4096), [[1, 128], [0, 32]], 64, 0)
+    asel(b("ind", 0, 2048), b("zrep", 0, 2048), [[-1, 128], [0, 16]], OP.is_equal, 0, 1)
+    asel(b("dg", 0, 2048), b("rp", 0, 2048), [[-1, 16], [0, 8], [1, 16]], OP.is_equal, 0, 0)
+    iota(b("zeros", 0, 8192), [[0, 8192]], 0, 0)
+
+    ms(b("big", 0, 8192), 0.0)
+    cp(b("bo32", 0, 128), b("bo", 0, 128))
+    cp(b("lt32", 0, 128), b("lt", 0, 128))
+    ts(b("woff", 8, 264), b("wt", 0, 256), 128.0, OP.add)
+
+    def prefix_scan():
+        scan(b("ex", 0, 257), b("m128", 0, 257), b("woff", 7, 264), OP.add, OP.add)
+
+    def prefix_sums():
+        mm(b("psM", 1, 2), b("lt32", 0, 128), b("ex", 256, 257), True, True)
+        mm(b("psM", 2, 3), b("bo32", 0, 128), b("ex", 256, 257), True, True)
+
+    def prefix_end():
+        ts(b("off16", 0, 256), b("ex", 0, 256), b("psM", 1, 2), OP.add)
+
+    prefix_scan()
+    banks = (("psA", 0), ("psA", 512), ("psB", 0), ("psB", 512), ("psC0", 0), ("psC1", 0))
+    for a in range(16):
+        p = b(banks[a % 6][0], banks[a % 6][1], banks[a % 6][1] + 256)
+        mm(p, b("ident", 0, 128), b("ptb", 16 + 256 * a, 272 + 256 * a), True, False)
+        mm(p, b("nident", 0, 128), b("ptb", 15 + 256 * a, 271 + 256 * a), False, True)
+        act(b("diffp", a, 4096, 16), p, AF.Copy, 0.0, 0.5)
+    ms(b("mkx", 0, 2048), 512.0)
+    ms(b("mkn", 0, 2048), -512.0)
+    ms(b("mkx", 0, 2048, 16), -512.0)
+    ms(b("mkn", 0, 2048, 16), 512.0)
+    cp(b("lm16", 0, 1024), b("lmI", 0, 1024))
+    cp(b("cb", 120, 128), b("bo", 0, 128, 16))
+    ts(b("ncb", 0, 248), b("cb", 0, 248), -1.0, OP.mult)
+    prefix_sums()
+    prefix_end()
+    ts(b("pI", 2, 3), b("pI", 0, 1), 7, OP.bitwise_and)
+    cp(b("aF", 1, 2), b("pI", 2, 3))
+    ts(b("pI", 1, 2), b("pI", 0, 1), 15, OP.bitwise_and)
+    ts(b("aF", 2, 3), b("pI", 1, 2), 2.0, OP.mult, 1.0, OP.add)
+
+    def inverse(c, k, n):
+        m = 4096 // n
+        w, v, off = b("invw", 0, 4096), b("vals", m * k, m * k + m), b("lm16", 256 * c + m // 16 * k, 256 * c + m // 16 * (k + 1))
+        emit("s", lambda: g.scalar.activation(w[0].indirect(off[0]), v[0], AF.Silu), [v, off], [w])
+
+    def inverse_table():
+        dma("y", [((T.invt[a::16, 0:256], "invt", 0, 256), (T.invw[a::16, 256 * a:256 * a + 256], "invw", 0, 4096)) for a in range(16)])
+
+    def inverse_list(c):
+        ts(b("inv16", 256 * c, 256 * c + 256), b("invt", 0, 256), -63.75, OP.add)
+
+    ZSRC = [(("zin0", 0), ("zin0", 128)), (("zr1", 0), ("zin1", 0)), (("zr2", 0), ("zin2", 0)), (("zr3", 0), ("zc0", 0))]
+    MB, MO = ("ptb", "sg1"), (16, 0)
+    MP = (("psA", 0), ("psA", 512), ("psC0", 0), ("psC1", 0))
+    MXB = (("big", OMX), ("big", OMX + 2048), ("big", OMX + 4096))
+    MNB = (("big", OMN), ("big", OMN + 2048), ("pE", 0))
+    for t in range(ROUNDS):
+        c0, c1 = t % 4, (t + 1) % 4
+        last = t == ROUNDS - 1
+        z0 = b(ZSRC[t][0][0], ZSRC[t][0][1], ZSRC[t][0][1] + 128)
+        z1 = b(ZSRC[t][1][0], ZSRC[t][1][1], ZSRC[t][1][1] + 128)
+        bigw, offs, dif = b("big", 0, 32768), b("off16", 0, 256), b("diffp", 0, 4096)
+        emit("v", lambda: g.vector.tensor_copy(bigw[0].indirect(offs[0]), dif[0]), [dif, offs], [bigw])
+        if t in WDMA:
+            dma("y", [((T.wrep[a::16, :], "wrep", 0, 4096), b("woff", 8, 264)) for a in range(16)])
+            inverse_table()
+        else:
+            for q in range(4):
+                ps = ("psA", "psB")[q % 2]
+                for k in range(4):
+                    a = 4 * q + k
+                    mm(b(ps, 256 * k, 256 * k + 256), b("rp", 128 * a, 128 * a + 128), b("woff", 8, 264), True, True)
+                act(b("wrep", 1024 * q, 1024 * q + 1024), b(ps, 0, 1024), AF.Copy)
+        if t == 0:
+            act(kl, kl, AF.Copy, 0.0, b("aF", 2, 3))
+        gath("s", b("ptb", 16, 4112), b("wrep", 0, 4096), b("lm16", 256 * c0, 256 * c0 + 256))
+        if t == 0:
+            inverse(0, 0, 1)
+        act(b("wf", 0, 256), b("woff", 8, 264), AF.Copy, -128.0)
+        act(b("zf32", 0, 128), z0, AF.Copy)
+        mm(b("psC1", 0, 128), z0, b("ident", 0, 128), True, True)
+        mm(b("psC1", 128, 256), z0, b("ident", 0, 128), True, False)
+        mm(b("psC1", 128, 256), z1, b("nident", 0, 128), False, True)
+        for k2 in range(3):
+            p = b("psC0", 128 * k2, 128 * k2 + 128)
+            mm(p, b("kl", 128 * k2, 128 * k2 + 128), b("zf32", 0, 128), True, False)
+            mm(p, b("row0", 0, 128), b("i976", 0, 128), False, True)
+        act(b("z0T", 0, 128), b("psC1", 0, 128), AF.Copy)
+        act(b("dzT", 0, 128), b("psC1", 128, 256), AF.Copy)
+        for q in range(4):
+            mm(b(("psA", "psB")[q // 2], 512 * (q % 2), 512 * (q % 2) + 512), b("z0T", 0, 128), b("ind", 512 * q, 512 * q + 512), True, True)
+        act(b("zrep", 0, 1024), b("psA", 0, 1024), AF.Copy)
+        act(b("zrep", 1024, 2048), b("psB", 0, 1024), AF.Copy)
+        for i in range(32):
+            mm(b("psS", 0, 128), b("ident", 0, 128), b("ptb", 16 + i, 4112, 32), i == 0, i == 31)
+        if t == 0:
+            inverse_table()
+            ts(b("orl", 0, 128), b("gq", 0, 128), b("aF", 1, 2), OP.is_equal)
+        ts(b("smi", 0, 1), b("psM", 2, 3), 0.5, OP.mult, -0.25, OP.add)
+        ts(b("thf", 0, 1), b("smi", 0, 1), 4096.0, OP.min, 1.0 / 2048.0, OP.mult)
+
+        def heavy(r):
+            ts(b("smv", 4, 5), b("acc", 1, 2), -16.0, OP.mult)
+            ts(b("a16", 0, 1), b("acc", 0, 1), 16.0, OP.mult, b("smv", 4, 5), OP.add)
+            ts(b("yab", r, r + 1), b("a16", 0, 1), 0.0625, OP.mult)
+
+        if t > 0:
+            heavy(t - 1)
+        scan(b("pE", 0, 8192), b("big", 0, 8192), b("big", 0, 8192), OP.add, OP.add)
+        if not last:
+            dma("y", [(b("big", 0, 8192), b("zeros", 0, 8192))])
+        else:
+            dma("y", [(T.yz[:, 128:256], b("zf1", 0, 128)), (T.yz[:, 256:384], b("zf2", 0, 128))])
+        if t == 0:
+            gath("v", b("sg1", 0, 4096), b("wrep", 0, 4096), b("lm16", 256 * c1, 256 * c1 + 256))
+        hI = b("hI", 0, 384)
+        ts(hI, b("psC0", 0, 384), b("a16", 0, 1), OP.add)
+        ts(hI, hI, 4, OP.arith_shift_right, 4095, OP.bitwise_and)
+        ts(hI, hI, b("thf", 0, 1), OP.mult, -4095.5 + 1.0 / 4096.0, OP.add)
+        ts(b("pos16", 0, 384), hI, 4095.0, OP.add)
+
+        def two_sided(bk):
+            return t == 0 and bk in VO
+
+        def ring(m, bk, lo=0, step=1):
+            base = (OA0, OA1)[m] + BLK * (bk % 4)
+            return b("big", base + lo, base + BLK, step)
+
+        def gather(bk):
+            o, win, off = b("big", OD0 + bk * BLK, OD0 + bk * BLK + BLK), b("pE", 0, 8192), b("pos16", 64 * bk, 64 * bk + 64)
+            zz = b("zrep", BLK * (bk % 2), BLK * (bk % 2) + BLK)
+            emit("v", lambda: g.vector.tensor_tensor(o[0], win[0].indirect(off[0]), zz[0], OP.subtract), [win, off, zz], [o])
+            if not two_sided(bk):
+                act(ring(0, bk), o, AF.Abs)
+            ps = ("psA", "psB")[bk % 2]
+            for h in range(2):
+                p = b(ps, 512 * h, 512 * h + 512)
+                mm(p, b("ident", 0, 128), b("big", OD0 + bk * BLK + 512 * h, OD0 + bk * BLK + 512 * h + 512), True, False)
+                mm(p, b("dzT", 0, 128), b("ind", BLK * (bk % 2) + 512 * h, BLK * (bk % 2) + 512 * h + 512), False, True)
+            act(ring(1, bk), b(ps, 0, 1024), AF.Abs)
+            if bk < 4:
+                if t == 0:
+                    inverse(1, bk, 4)
+                else:
+                    gath("s", b("sg1", BLK * bk, BLK * bk + BLK), b("wrep", 0, 4096), b("lm16", 256 * c1 + 64 * bk, 256 * c1 + 64 * bk + 64))
+
+        def compare(bk):
+            k2, half = bk // 2, bk % 2
+            for m in range(2):
+                two = m == 0 and two_sided(bk)
+                o = b("psC%d" % m, 128 * k2 + 64 * half, 128 * k2 + 64 * half + 64)
+                lo = BLK * half
+                if two:
+                    d = b("big", OD0 + bk * BLK, OD0 + bk * BLK + BLK)
+                    ts(ring(0, bk), d, -68.0, OP.is_ge)
+                    ts(b("b0r", lo, lo + BLK), d, 68.0, OP.is_gt)
+                else:
+                    ts(ring(m, bk), ring(m, bk), 68.0, OP.is_le)
+                for a in range(16):
+                    mm(o, b("cb", 120 - 8 * a, 248 - 8 * a), ring(m, bk, a, 16), a == 0, a == 15 and not two)
+                if two:
+                    for a in range(16):
+                        mm(o, b("ncb", 120 - 8 * a, 248 - 8 * a), b("b0r", lo + a, lo + BLK, 16), False, a == 15)
+
+        def extremes(k2, part=2):
+            d = b("big", OD0 + 2048 * k2, OD0 + 2048 * k2 + 2048)
+            if part != 1:
+                scan(b(MXB[k2][0], MXB[k2][1], MXB[k2][1] + 2048), b("mkx", 0, 2048), d, OP.min, OP.max)
+            if part != 0:
+                scan(b(MNB[k2][0], MNB[k2][1], MNB[k2][1] + 2048), b("mkn", 0, 2048), d, OP.max, OP.min)
+
+        def second_sums(h):
+            for i in range(32):
+                mm(b("psS", 128 + 64 * h, 192 + 64 * h), b("ident", 0, 128), b("sg1", 2048 * h + i, 2048 * h + 2048, 32), i == 0, i == 31)
+
+        gather(0)
+        gather(1)
+        gather(2)
+        if t == 0:
+            inverse_list(0)
+        compare(0)
+        gather(3)
+        compare(1)
+        extremes(0)
+        second_sums(0)
+        gather(4)
+        compare(2)
+        gather(5)
+        second_sums(1)
+        extremes(1)
+        compare(3)
+        if t in (1, 2):
+            inverse_list(t + 1)
+        if t == 0:
+            inverse_table()
+        compare(4)
+        extremes(2, 0)
+        compare(5)
+        ts(b("thr", 0, 256), b("psS", 0, 256), 4143.5, OP.is_lt, 0.5, OP.mult)
+        extremes(2, 1)
+        hits = (b("psM", 128, 256), b("psS", 256, 384))
+        for m in range(2):
+            act(b("hb%d" % m, 0, 384), b("psC%d" % m, 0, 384), AF.Relu, -11.0)
+            for k2 in range(3):
+                mm(hits[m], b("orl", 0, 128), b("hb%d" % m, 128 * k2, 128 * k2 + 128), k2 == 0, k2 == 2)
+        tt(b("L01", 0, 128), hits[0], b("thr", 0, 128), OP.is_lt)
+        ts(b("nh0", 0, 128), hits[0], 0.5, OP.is_ge)
+        tt(b("x1", 0, 128), hits[1], b("thr", 128, 256), OP.is_lt)
+        tt(b("L01", 128, 256), b("x1", 0, 128), b("nh0", 0, 128), OP.mult)
+
+        def mark_gather(q, m, k0, k1):
+            c = (c0, c1)[m]
+            gath(q, b(MB[m], MO[m] + 512 * k0, MO[m] + 512 * k1), b("L01", 128 * m, 128 * m + 128),
+                 b("inv16", 256 * c + 32 * k0, 256 * c + 32 * k1))
+
+        def marks(m, h, first):
+            p = b(MP[h][0], MP[h][1], MP[h][1] + 64)
+            for a in range(16):
+                mm(p, b("dg", 128 * a, 128 * a + 128), b(MB[m], MO[m] + 1024 * h + a, MO[m] + 1024 * h + 1024, 16),
+                   first and a == 0, not first and a == 15)
+
+        def extremes_end():
+            for buf, o, op in ((MXB, "mx", OP.max), (MNB, "mn", OP.min)):
+                e = [b(n, lo + 15, lo + 2048, 16) for n, lo in buf]
+                tt(b(o, 0, 128), e[0], e[1], op)
+                tt(b(o, 0, 128), b(o, 0, 128), e[2], op)
+            ts(b("sel", 0, 128), hits[0], 0.5, OP.is_lt)
+            ts(b("m1", 0, 128), hits[1], 0.5, OP.is_lt)
+            tt(b("sel", 128, 256), b("m1", 0, 128), b("nh0", 0, 128), OP.mult)
+            one, neg, mx, mn = b("ident", 0, 128), b("nident", 0, 128), b("mx", 0, 128), b("mn", 0, 128)
+            for k, x in enumerate((mx, mn)):
+                mm(b("psB", 0, 128), one, x, k == 0, k == 1)
+            for k, (l, x) in enumerate(((one, mx), (one, mn), (one, z0), (one, z0), (neg, z1), (neg, z1))):
+                mm(b("psB", 128, 256), l, x, k == 0, k == 5)
+
+        def quarter():
+            ts(b("q01", 0, 256), b("psB", 0, 256), 0.25, OP.mult, -0.375, OP.add)
+
+        def move():
+            tt(b("e01", 0, 256), b("q01", 0, 256), b("sel", 0, 256), OP.mult)
+            for m, z in ((0, z0), (1, z1)):
+                mm(b("psB", 512 + 128 * m, 640 + 128 * m), b("ident", 0, 128), b("e01", 128 * m, 128 * m + 128), True, False)
+                mm(b("psB", 512 + 128 * m, 640 + 128 * m), b("ident", 0, 128), z, False, True)
+
+        def hand_over():
+            if t == 2:
+                act(b("zo%d" % t, 0, 256), b("psB", 512, 768), AF.Copy)
+            else:
+                cp(b("zo%d" % t, 0, 256), b("psB", 512, 768))
+            for kind in (("u0", "c0"), ("u1", "f1"), ("u2", "f2"), ("f3",))[t]:
+                send(kind)
+
+        if t == 0:
+            ts(b("dg", 0, 2048), b("dg", 0, 2048), 8.0, OP.mult)
+            inverse_list(1)
+        mark_gather("s", 0, 0, 4)
+        mark_gather("s", 0, 4, 8)
+        if last:
+            extremes_end()
+            quarter()
+            move()
+            hand_over()
+        marks(0, 0, True)
+        marks(0, 1, True)
+        mark_gather("v", 1, 0, 4)
+        marks(1, 0, False)
+        marks(1, 1, False)
+        mark_gather("v", 1, 4, 6)
+        marks(1, 2, True)
+        marks(0, 2, False)
+        marks(0, 3, True)
+        mark_gather("s", 1, 6, 8)
+        marks(1, 3, False)
+        ts(b("w2", 0, 256), b("wf", 0, 256), 2.0, OP.mult, 8.0, OP.min)
+        if not last:
+            extremes_end()
+        total(b("acc", 0, 1), b("sel", 0, 256))
+        total(b("acc", 1, 2), b("L01", 0, 256))
+        if t < 2:
+            inverse(t + 2, 0, 1)
+        for h in range(4):
+            w1 = b("w1", 64 * h, 64 * h + 64)
+            tt(w1, b(MP[h][0], MP[h][1], MP[h][1] + 64), b("w2", 64 * h, 64 * h + 64), OP.min)
+            tt(w1, w1, b("wf", 64 * h, 64 * h + 64), OP.max)
+        red(b("smv", 0, 1), b("w1", 0, 256))
+        mm(b("psM", 0, 1), b("bo32", 0, 128), b("smv", 0, 1), True, True)
+        if not last:
+            quarter()
+        ts(b("smv", 1, 2), b("psM", 0, 1), 7168.5, OP.is_gt, -0.5, OP.mult)
+        ts(b("smv", 2, 3), b("smv", 1, 2), 1.0, OP.add)
+        ts(b("smv", 3, 4), b("smv", 1, 2), -0.5, OP.mult, 128.0, OP.add)
+        ts(b("woff", 8, 264), b("w1", 0, 256), b("smv", 2, 3), OP.mult, b("smv", 3, 4), OP.add)
+        if not last:
+            prefix_scan()
+            prefix_sums()
+            move()
+            prefix_end()
+            hand_over()
+
+    ts(b("ywb", 0, 256), b("woff", 8, 264), -128.0, OP.add)
+    dma("y", [(T.yw[:], b("ywb", 0, 256))])
+    heavy(ROUNDS - 1)
+    dma("y", [(T.ya[:], (T.yab[0::16, 0:4], "yab", 0, 4))])
+    dma("s", [(T.yz[:, 384:512], b("zf3", 0, 128)), (T.yz[:, 0:128], b("zf3", 128, 256))])
+    for sem, val in count.items():
+        if waited["g"].get(sem, 0) < val:
+            g.wait_ge(T.sem[sem], val)

@@ -6,9 +6,22 @@ AF = ActivationFunctionType
 NR = 8
 ROUNDS = 4
 BLK = 1024
-OD0, OA0, OA1, OMX, OMN = 8192, 14336, 18432, 22528, 28672
-WDMA = (1, 2)
-VO = (0, 1, 2, 3)
+OP_, OI0, OI1, OMX, OMN = 8192, 14336, 18432, 22528, 28672
+BIG = 1.5 * 2.0 ** 34
+EARLY = ("i i i i i i i i factors cen ms00 cend ms01 rep ms02 ms03",
+         "i ms00 ms01 ms02 ms03 cen ms10 i i cend ms11 sum0 rep ms12",
+         "i ms00 ms01 ms02 ms03 cen ms10 i i cend ms11 sum0 rep ms12",
+         "ms00 ms01 ms02 ms03 cen ms10 cend sum0 ms11 rep ms12 ms13")
+_H = ("g0 g1 f01 g2 A00 f10 T10 f21 C00 ms13 g3 f11 T01 T11 c00 f31 g4 A20 C20 f30 T30 sum1 c01 g5 T21 x00 f50 A40 c10 f41 C40 A31 C31 "
+      "T50 c20 x10 x01 L0 f51 c11 w0 A51 C51 T41 i x11 k0 c21 first L1 w1 k1 x20 i r0 r1 j0 cho x21 j1 d0 d1 i spr mid whole q halve "
+      "move hea i pre end i hand")
+HIT = ("g0 g1 f01 f10 f11 A00 g2 sum0 g3 T01 f21 i T10 f30 C00 c00 A20 T11 f31 c01 i i g4 g5 T21 f41 C20 i T30 f50 c10 A40 T31 f51 c11 "
+       "i i i i C40 T50 c20 ms10 ms11 x00 L0 w0 T41 ms12 T51 c21 k0 ms13 sum1 first x01 x10 x11 L1 w1 r0 k1 cho i d0 spr x20 r1 hea i "
+       "x21 i j0 j1 mid d1 whole i q halve pre move hand i end",
+       _H, _H.replace(" i ", " "),
+       "sum1 g0 g1 f01 f10 f11 A00 g2 g3 T10 f21 C00 c00 A01 f30 A11 f31 g4 C01 A20 C11 c01 g5 x00 C20 A21 f41 T30 f50 c10 A31 f51 C21 "
+       "A40 x01 C31 c11 A50 C40 C50 c20 A41 x10 A51 L0 w0 k0 C41 C51 c21 first x11 L1 w1 cho k1 spr x20 x21 j0 j1 mid r0 q move hand "
+       "r1 hea d0 d1 whole halve")
 
 MSG = [
     ("i01", "z0s", 0, 256, -1, "zin0", 0), ("i2", "z0s", 256, 384, -2, "zin1", 1), ("i3", "z0s", 384, 512, -3, "zin2", 1),
@@ -20,25 +33,28 @@ MSG = [
 _B, _F, _I, _U = "bfloat16", "float32", "int32", "uint16"
 SCRATCH = {}
 for _n, _w, _d in [
-        ("big", 32768, _B), ("ptb", 4112, _B), ("diffp", 4096, _B), ("pE", 8192, _B), ("zeros", 8192, _B),
-        ("wrep", 4096, _B), ("b0r", 2048, _B), ("sg1", 4096, _B), ("invw", 4096, _F), ("vals", 4096, _F),
-        ("zrep", 2048, _B), ("ind", 2048, _B), ("mkx", 2048, _B), ("mkn", 2048, _B),
-        ("lmI", 1024, _I), ("lm16", 1024, _U), ("inv16", 1024, _U), ("invt", 256, _F),
-        ("dg", 2048, _B), ("rp", 2048, _B), ("ident", 128, _B), ("nident", 128, _B), ("bo", 128, _B), ("bot", 128, _B),
-        ("lt", 128, _B), ("bo32", 128, _F), ("lt32", 128, _F), ("one32", 128, _F), ("row0", 128, _F), ("i976", 128, _F),
-        ("kl", 384, _F), ("pI", 8, _I), ("aF", 8, _F), ("gq", 128, _F), ("orl", 128, _B), ("cb", 248, _B), ("ncb", 248, _B),
+        ("big", 32768, _B), ("ptb", 4112, _B), ("diffp", 4096, _B), ("pE", 8192, _B), ("zeros", 2048, _B),
+        ("wg0", 4096, _B), ("wg1", 4096, _B), ("rf", 4096, _F), ("vals", 4096, _F), ("rr", 16384, _B),
+        ("ind", 2048, _B), ("mkx", 2048, _B), ("mkn", 2048, _B), ("amk", 384, _B),
+        ("lmI", 1024, _I), ("lm16", 1024, _U), ("pat", 256, _F), ("mI", 16, _I), ("mF", 16, _F),
+        ("zero", 128, _B), ("one", 128, _B), ("ident", 128, _B), ("nident", 128, _B), ("id15", 128, _B), ("n2id", 128, _B),
+        ("p2id", 128, _B), ("zh", 128, _B), ("zrep", 1024, _B),
+        ("bo32", 128, _F), ("lt32", 128, _F), ("one32", 128, _F), ("bi8", 8, _B), ("rs8", 8, _B), ("sgn", 8, _F),
+        ("cst", 384, _B), ("lane", 128, _B), ("crep", 128, _B), ("em", 512, _B), ("bw0", 144, _B), ("bw1", 144, _B),
+        ("kl", 384, _F), ("aF", 8, _F),
         ("m128", 272, _F), ("wt", 256, _B), ("woff", 272, _B), ("ex", 264, _F), ("off16", 256, _U), ("w2", 256, _B), ("wf", 256, _B),
-        ("w1", 256, _F), ("smv", 8, _F), ("smi", 8, _I), ("a16", 8, _F), ("thf", 8, _F), ("yab", 4, _F), ("ywb", 256, _F),
-        ("acc", 8, _F), ("jk", 256, _B), ("zf32", 128, _F), ("z0T", 128, _B), ("dzT", 128, _B),
-        ("hI", 384, _I), ("pos16", 384, _U), ("hb0", 384, _B), ("hb1", 384, _B), ("thr", 256, _F), ("sel", 256, _F), ("nh0", 128, _F),
-        ("m1", 128, _F), ("x1", 128, _F), ("L01", 256, _B), ("mx", 128, _B), ("mn", 128, _B), ("q01", 256, _I), ("e01", 256, _B),
+        ("wa", 256, _B), ("w1", 256, _B), ("r0", 256, _B), ("r1", 256, _B),
+        ("smv", 8, _F), ("smi", 8, _I), ("a16", 8, _F), ("thf", 8, _F), ("yab", 4, _F), ("ywb", 256, _F),
+        ("jk", 128, _B), ("zf32", 128, _F), ("zT", 256, _B), ("hI", 384, _I), ("pos16", 384, _U),
+        ("am0", 384, _B), ("am1", 384, _B), ("thr", 32, _F), ("xs", 32, _B), ("xT", 128, _B),
+        ("mx", 128, _B), ("mn", 128, _B), ("q01", 256, _I), ("e01", 256, _B),
         ("z0s", 512, _B), ("zin0", 256, _B), ("zin1", 128, _B), ("zin2", 128, _B), ("zr1", 128, _B), ("zr2", 128, _B),
         ("zr3", 128, _B), ("zc0", 128, _B), ("zf1", 128, _B), ("zf2", 128, _B), ("zf3", 256, _B),
         ("zo0", 256, _B), ("zo1", 256, _B), ("zo2", 256, _B), ("zo3", 256, _B)]:
     SCRATCH[_n] = ("sbuf", [128, _w], _d)
 for _m in MSG:
     SCRATCH["y_" + _m[0]] = ("sbuf", [128, _m[3] - _m[2]], _B)
-for _n, _w in [("psA", 1024), ("psB", 1024), ("psC0", 512), ("psC1", 512), ("psM", 512), ("psS", 512)]:
+for _n, _w in [("psA", 1024), ("psB", 1024), ("psD", 1024), ("psC0", 512), ("psC1", 512)]:
     SCRATCH[_n] = ("psum", [128, _w], _F)
 
 SEMAPHORES = ["kv", "ks", "kt", "kg", "ls"] + ["d%d" % i for i in range(40)] + ["m_" + m[0] for m in MSG] + ["q_" + m[0] for m in MSG]
@@ -93,17 +109,18 @@ def rank_main(g, core, rank, cores, T, topo):
     waited = {q: {} for q in Q}
     hist = {}
     nd = [0]
+    apart = [False]
 
     def need(q, name, lo, hi, write, toks):
         ps = name.startswith("ps")
         for (l, h, wr, sem, val, qq) in hist.get(name, []):
             if qq == q and qq in SEMOF:
-                if not (l < hi and lo < h) or not wr or (ps and q == "t"):
+                if not (l < hi and lo < h) or not wr or (ps and q == "t") or (write and apart[0]):
                     continue
             elif ps:
                 if l // 512 > (hi - 1) // 512 or lo // 512 > (h - 1) // 512:
                     continue
-            elif not (l < hi and lo < h) or not (wr or write):
+            elif not (l < hi and lo < h) or not (wr or write) or (write and wr and apart[0]):
                 continue
             if toks.get(sem, 0) < val:
                 toks[sem] = val
@@ -111,7 +128,7 @@ def rank_main(g, core, rank, cores, T, topo):
     def note(name, lo, hi, write, sem, val, q):
         L = hist.get(name, [])
         if write:
-            L = [e for e in L if not (lo <= e[0] and e[1] <= hi)]
+            L = [e for e in L if not (lo <= e[0] and e[1] <= hi and (e[5] == q or not apart[0]))]
         else:
             L = [e for e in L if not (not e[2] and e[5] == q and q in SEMOF and lo <= e[0] and e[1] <= hi)]
         L.append((lo, hi, write, sem, val, q))
@@ -128,8 +145,9 @@ def rank_main(g, core, rank, cores, T, topo):
                 Q[q].wait_ge(T.sem[sem], val)
                 waited[q][sem] = val
 
-    def b(name, lo, hi, step=1):
-        return (T[name][:, lo:hi:step] if step != 1 else T[name][:, lo:hi], name, lo, hi)
+    def b(name, lo, hi, step=1, rows=None):
+        cols = slice(lo, hi, step) if step != 1 else slice(lo, hi)
+        return (T[name][:, cols] if rows is None else T[name][0:rows, cols], name, lo, hi)
 
     def ap(x):
         return x[0] if isinstance(x, tuple) else x
@@ -184,15 +202,15 @@ def rank_main(g, core, rank, cores, T, topo):
     def act(o, x, func, bias=0.0, scale=1.0):
         emit("s", lambda: g.scalar.activation(o[0], x[0], func, bias=bias, scale=ap(scale)), [x, scale], [o])
 
-    def total(o, x):
-        j = b("jk", 0, 256)
-        emit("s", lambda: g.scalar.activation(j[0], x[0], AF.Copy, accum_out=o[0]), [x], [j, o])
+    def total(o, x, scale):
+        j = b("jk", 0, 128)
+        emit("s", lambda: g.scalar.activation(j[0], x[0], AF.Copy, scale=scale, accum_out=o[0]), [x], [j, o])
 
     def mm(o, l, r, start, stop):
         emit("t", lambda: g.tensor.matmul(o[0], l[0], r[0], start, stop), [l, r], [o])
 
-    def asel(o, i, pattern, op, base, cm):
-        emit("g", lambda: g.affine_select(o[0], i[0], pattern, op, 0.0, base, cm), [i], [o])
+    def asel(o, i, pattern, op, base, cm, fill=0.0):
+        emit("g", lambda: g.affine_select(o[0], i[0], pattern, op, fill, base, cm), [i], [o])
 
     def iota(o, pattern, base, cm, flag=True):
         if flag:
@@ -228,339 +246,331 @@ def rank_main(g, core, rank, cores, T, topo):
                 g.remote_dma(out, src[0], T.sem[sem], T.sem.ls, pid, rid, m)
                 count["ls"] = count.get("ls", 0) + popcount(m)
 
+    zero, one, one32 = b("zero", 0, 128), b("one", 0, 128), b("one32", 0, 128)
+    ident, nident, id15, n2id = b("ident", 0, 128), b("nident", 0, 128), b("id15", 0, 128), b("n2id", 0, 128)
     dma("y", [(b("wt", 0, 256), T.w0[:])])
     dma("s", [(b("z0s", 0, 512), T.z0[:])])
     for k in range(4):
         dma("y", [(b("ptb", 16 + 1024 * k, 1040 + 1024 * k), T.pt[:, 1024 * k:1024 * k + 1024])])
     dma("y", [(b("lmI", 0, 1024), T.lm[:])])
-    ms(b("zrep", 0, 2048), 1.0)
+    iota(b("mI", 0, 16), [[-1, 16]], 16, 1, False)
+    ms(zero, 0.0)
+    ms(one32, 1.0)
+    for lo in range(8):
+        ms(b("pat", 32 * lo, 32 * lo + 32), 2.0 ** (13 - lo))
+    ts(b("mI", 0, 16), b("mI", 0, 16), 15, OP.bitwise_and)
+    ts(b("mF", 0, 16), b("mI", 0, 16), 0.0, OP.is_equal)
     ms(b("ptb", 0, 16), 0.0)
-    ms(b("one32", 0, 128), 1.0)
     ms(b("m128", 0, 272), -128.0)
     ms(b("woff", 0, 8), 128.0)
-    ms(b("a16", 0, 8), 0.0)
-    ms(b("cb", 0, 248), 0.0)
 
-    iota(b("pI", 0, 1), [[0, 1]], 0, 1, False)
-    asel(b("ident", 0, 128), b("zrep", 0, 128), [[-1, 128]], OP.is_equal, 0, 1)
-    asel(b("bot", 0, 128), b("zrep", 0, 128), [[-16, 8], [0, 16]], OP.is_ge, 0, 1)
-    asel(b("bo", 0, 128), b("bot", 0, 128), [[16, 8], [0, 16]], OP.is_ge, 15, -1)
-    asel(b("lt", 0, 128), b("bo", 0, 128), [[1, 128]], OP.is_ge, -1, -1)
-    ts(b("nident", 0, 128), b("ident", 0, 128), -1.0, OP.mult)
+    asel(ident, zero, [[-1, 128]], OP.not_equal, 0, 1, 1.0)
+    asel(nident, zero, [[-1, 128]], OP.not_equal, 0, 1, -1.0)
+    asel(b("lt32", 0, 128), one32, [[-16, 8], [0, 16]], OP.is_ge, 0, 1)
+    asel(b("bo32", 0, 128), b("lt32", 0, 128), [[16, 8], [0, 16]], OP.is_ge, 15, -1)
+    asel(b("lt32", 0, 128), b("bo32", 0, 128), [[1, 128]], OP.is_ge, -1, -1)
     send("i01")
-    asel(b("rp", 0, 2048), b("zrep", 0, 2048), [[-1, 16], [-16, 8], [0, 16]], OP.is_equal, 0, 1)
-    send("i2")
-    send("i3")
     kl = b("kl", 0, 384)
     iota(kl, [[80, 3], [0, 8], [5, 16]], 17, 0)
     asel(kl, kl, [[0, 3], [-16, 8], [0, 16]], OP.is_ge, 0, 1)
     asel(kl, kl, [[0, 3], [16, 8], [0, 16]], OP.is_ge, 15, -1)
-    asel(b("row0", 0, 128), b("one32", 0, 128), [[0, 128]], OP.is_equal, 0, 1)
-    iota(b("i976", 0, 128), [[976, 128]], 0, 0)
-    iota(b("gq", 0, 128), [[1, 8], [0, 16]], 0, 0)
-    iota(b("vals", 0, 4096), [[1, 128], [0, 32]], 64, 0)
-    asel(b("ind", 0, 2048), b("zrep", 0, 2048), [[-1, 128], [0, 16]], OP.is_equal, 0, 1)
-    asel(b("dg", 0, 2048), b("rp", 0, 2048), [[-1, 16], [0, 8], [1, 16]], OP.is_equal, 0, 0)
-    iota(b("zeros", 0, 8192), [[0, 8192]], 0, 0)
+    iota(b("lane", 0, 128), [[1, 128]], 0, 0)
+    send("i2")
+    send("i3")
+    iota(b("zeros", 0, 2048), [[0, 2048]], 0, 0)
+    asel(b("ind", 0, 2048), b("zeros", 0, 2048), [[-1, 128], [0, 16]], OP.not_equal, 0, 1, -15.0)
+    asel(id15, zero, [[-1, 128]], OP.not_equal, 0, 1, 15.0)
+    asel(b("rs8", 0, 8), b("zero", 0, 8), [[-16, 8]], OP.not_equal, 0, 1, 1.0)
 
+    iota(b("zh", 0, 128), [[0, 128]], 0, 0)
+    iota(b("mkx", 0, 2048), [[0, 128], [1024, 16]], -512, 0)
+
+    def late_constants():
+        iota(b("mkn", 0, 2048), [[0, 128], [-1024, 16]], 512, 0)
+        asel(b("p2id", 0, 128), zero, [[-1, 128]], OP.not_equal, 0, 1, 2.0)
+        iota(b("amk", 0, 384), [[0, 8], [16, 48]], 0, 0)
+        asel(n2id, zero, [[-1, 128]], OP.not_equal, 0, 1, -2.0)
+        for lo in range(8):
+            asel(b("crep", 0, 128), zero if lo == 0 else b("crep", 0, 128), [[0, 8], [-8, 16]], OP.not_equal, -lo, 1, 2.0 ** (lo - 14))
+        asel(b("em", 0, 512), b("zeros", 0, 512), [[-8, 4], [-1, 8], [0, 16]], OP.not_equal, 0, 1, 1.0)
+        asel(b("sgn", 0, 1), b("one32", 0, 1), [[0, 1]], OP.is_ge, 15, -1, -1.0)
+        iota(b("bw0", 0, 144), [[0, 144]], 0, 0)
+        iota(b("bw1", 0, 144), [[0, 144]], 0, 0)
+
+    for a in range(16):
+        act(b("vals", 256 * a, 256 * a + 256), b("pat", 0, 256), AF.Copy, 0.0, b("mF", a, a + 1))
     ms(b("big", 0, 8192), 0.0)
-    cp(b("bo32", 0, 128), b("bo", 0, 128))
-    cp(b("lt32", 0, 128), b("lt", 0, 128))
     ts(b("woff", 8, 264), b("wt", 0, 256), 128.0, OP.add)
 
     def prefix_scan():
         scan(b("ex", 0, 257), b("m128", 0, 257), b("woff", 7, 264), OP.add, OP.add)
 
     def prefix_sums():
-        mm(b("psM", 1, 2), b("lt32", 0, 128), b("ex", 256, 257), True, True)
-        mm(b("psM", 2, 3), b("bo32", 0, 128), b("ex", 256, 257), True, True)
+        mm(b("psC0", 401, 402), b("lt32", 0, 128), b("ex", 256, 257), True, True)
+        mm(b("psC0", 402, 403), b("bo32", 0, 128), b("ex", 256, 257), True, True)
 
     def prefix_end():
-        ts(b("off16", 0, 256), b("ex", 0, 256), b("psM", 1, 2), OP.add)
+        ts(b("off16", 0, 256), b("ex", 0, 256), b("psC0", 401, 402), OP.add)
 
     prefix_scan()
-    banks = (("psA", 0), ("psA", 512), ("psB", 0), ("psB", 512), ("psC0", 0), ("psC1", 0))
-    for a in range(16):
-        p = b(banks[a % 6][0], banks[a % 6][1], banks[a % 6][1] + 256)
-        mm(p, b("ident", 0, 128), b("ptb", 16 + 256 * a, 272 + 256 * a), True, False)
-        mm(p, b("nident", 0, 128), b("ptb", 15 + 256 * a, 271 + 256 * a), False, True)
-        act(b("diffp", a, 4096, 16), p, AF.Copy, 0.0, 0.5)
-    ms(b("mkx", 0, 2048), 512.0)
-    ms(b("mkn", 0, 2048), -512.0)
-    ms(b("mkx", 0, 2048, 16), -512.0)
-    ms(b("mkn", 0, 2048, 16), 512.0)
-    cp(b("lm16", 0, 1024), b("lmI", 0, 1024))
-    cp(b("cb", 120, 128), b("bo", 0, 128, 16))
-    ts(b("ncb", 0, 248), b("cb", 0, 248), -1.0, OP.mult)
     prefix_sums()
     prefix_end()
-    ts(b("pI", 2, 3), b("pI", 0, 1), 7, OP.bitwise_and)
-    cp(b("aF", 1, 2), b("pI", 2, 3))
-    ts(b("pI", 1, 2), b("pI", 0, 1), 15, OP.bitwise_and)
-    ts(b("aF", 2, 3), b("pI", 1, 2), 2.0, OP.mult, 1.0, OP.add)
+    banks = (("psB", 0), ("psB", 512), ("psD", 0), ("psD", 512), ("psA", 0), ("psA", 512))
+    apart[0] = True
+    for a in range(16):
+        p = b(banks[a % 6][0], banks[a % 6][1], banks[a % 6][1] + 256)
+        mm(p, ident, b("ptb", 16 + 256 * a, 272 + 256 * a), True, False)
+        mm(p, nident, b("ptb", 15 + 256 * a, 271 + 256 * a), False, True)
+        if a % 8 < 5:
+            ts(b("diffp", a, 4096, 16), p, 0.5, OP.mult)
+        else:
+            act(b("diffp", a, 4096, 16), p, AF.Copy, 0.0, 0.5)
+        if a == 9:
+            cp(b("lm16", 0, 256), b("lmI", 0, 256))
+    apart[0] = False
 
-    def inverse(c, k, n):
-        m = 4096 // n
-        w, v, off = b("invw", 0, 4096), b("vals", m * k, m * k + m), b("lm16", 256 * c + m // 16 * k, 256 * c + m // 16 * (k + 1))
+    def rest_of_setup():
+        cp(b("lm16", 256, 1024), b("lmI", 256, 1024))
+        ts(b("aF", 2, 3), b("mI", 0, 1), 2.0, OP.mult, 1.0, OP.add)
+        ms(b("cst", 0, 128), 976.0)
+        ms(b("cst", 128, 384), 128.0)
+        ms(one, 1.0)
+        ms(b("a16", 0, 8), 0.0)
+        cp(b("bi8", 0, 8), b("bo32", 0, 128, 16))
+
+    def inverse(c, k):
+        w, v, off = b("rf", 0, 4096), b("vals", 512 * k, 512 * k + 512), b("lm16", 256 * c + 32 * k, 256 * c + 32 * k + 32)
         emit("s", lambda: g.scalar.activation(w[0].indirect(off[0]), v[0], AF.Silu), [v, off], [w])
-
-    def inverse_table():
-        dma("y", [((T.invt[a::16, 0:256], "invt", 0, 256), (T.invw[a::16, 256 * a:256 * a + 256], "invw", 0, 4096)) for a in range(16)])
-
-    def inverse_list(c):
-        ts(b("inv16", 256 * c, 256 * c + 256), b("invt", 0, 256), -63.75, OP.add)
+        if k == 7:
+            dma("g", [(b("rr", 4096 * c, 4096 * c + 4096), w)])
 
     ZSRC = [(("zin0", 0), ("zin0", 128)), (("zr1", 0), ("zin1", 0)), (("zr2", 0), ("zin2", 0)), (("zr3", 0), ("zc0", 0))]
-    MB, MO = ("ptb", "sg1"), (16, 0)
-    MP = (("psA", 0), ("psA", 512), ("psC0", 0), ("psC1", 0))
+    TILE = ("psA", "psB", "psD")
+    pieces = [0]
     MXB = (("big", OMX), ("big", OMX + 2048), ("big", OMX + 4096))
     MNB = (("big", OMN), ("big", OMN + 2048), ("pE", 0))
     for t in range(ROUNDS):
-        c0, c1 = t % 4, (t + 1) % 4
+        cc = (t % 4, (t + 1) % 4)
         last = t == ROUNDS - 1
-        z0 = b(ZSRC[t][0][0], ZSRC[t][0][1], ZSRC[t][0][1] + 128)
-        z1 = b(ZSRC[t][1][0], ZSRC[t][1][1], ZSRC[t][1][1] + 128)
+        zz = [b(n, lo, lo + 128) for n, lo in ZSRC[t]]
+        wrow = b("ptb", 16, 4112)
+        tile, free, tail = {}, list(TILE), []
+        dma("y", [((T.ptb[0::16, 16:4112], "ptb", 16, 4112), b("woff", 8, 264))])
+        ts(b("smi", 0, 1), b("psC0", 402, 403), 0.5, OP.mult, -0.25, OP.add)
         bigw, offs, dif = b("big", 0, 32768), b("off16", 0, 256), b("diffp", 0, 4096)
         emit("v", lambda: g.vector.tensor_copy(bigw[0].indirect(offs[0]), dif[0]), [dif, offs], [bigw])
-        if t in WDMA:
-            dma("y", [((T.wrep[a::16, :], "wrep", 0, 4096), b("woff", 8, 264)) for a in range(16)])
-            inverse_table()
-        else:
-            for q in range(4):
-                ps = ("psA", "psB")[q % 2]
-                for k in range(4):
-                    a = 4 * q + k
-                    mm(b(ps, 256 * k, 256 * k + 256), b("rp", 128 * a, 128 * a + 128), b("woff", 8, 264), True, True)
-                act(b("wrep", 1024 * q, 1024 * q + 1024), b(ps, 0, 1024), AF.Copy)
-        if t == 0:
+
+        def members(q, m, k):
+            gath(q, b("wg%d" % m, BLK * k, BLK * k + BLK), wrow, b("lm16", 256 * cc[m] + 64 * k, 256 * cc[m] + 64 * k + 64))
+
+        def sums(m):
+            for i in range(32):
+                mm(b("psC%d" % m, 384, 392), b("wg%d" % m, i, 4096, 32), b("rs8", 0, 8), i == 0, i == 31)
+
+        def centres():
+            act(b("zf32", 0, 128), zz[0], AF.Copy)
+            for k2 in range(3):
+                p = b("psA", 128 * k2, 128 * k2 + 128)
+                mm(p, b("kl", 128 * k2, 128 * k2 + 128), b("zf32", 0, 128), True, False)
+                mm(p, b("cst", 0, 128, 1, 1), b("lane", 0, 128, 1, 1), False, True)
+            mm(b("psB", 0, 128), zz[0], ident, True, True)
+            act(b("zh", 0, 64), b(ZSRC[t][0][0], ZSRC[t][0][1], ZSRC[t][0][1] + 64), AF.Copy)
+            mm(b("psB", 128, 256), zz[1], ident, True, False)
+            mm(b("psB", 128, 256), b("zh", 0, 128), nident, False, True)
+
+        def centres_end():
+            act(b("zT", 0, 256), b("psB", 0, 256), AF.Copy)
+            for h in range(2):
+                mm(b("psD", 512 * h, 512 * h + 512), b("zT", 0, 128), b("ind", 512 * h, 512 * h + 512), True, True)
+            act(b("wf", 0, 256), b("woff", 8, 264), AF.Copy, -128.0)
+
+        def repeated():
+            act(b("zrep", 0, 1024), b("psD", 0, 1024), AF.Copy, 0.0, -1.0 / 15.0)
+
+        def factors():
+            late_constants()
             act(kl, kl, AF.Copy, 0.0, b("aF", 2, 3))
-        gath("s", b("ptb", 16, 4112), b("wrep", 0, 4096), b("lm16", 256 * c0, 256 * c0 + 256))
+
+        def next_inverse():
+            inverse(pieces[0] // 8, pieces[0] % 8)
+            pieces[0] += 1
+
+        def play(order, steps):
+            for word in order.split():
+                name = word.rstrip("0123456789")
+                steps[name](*[int(x) for x in word[len(name):]])
+
+        steps = {"i": next_inverse, "ms": lambda m, k: members("s", m, k), "mv": lambda m, k: members("v", m, k), "sum": sums,
+                 "cen": centres, "cend": centres_end, "rep": repeated, "factors": factors}
         if t == 0:
-            inverse(0, 0, 1)
-        act(b("wf", 0, 256), b("woff", 8, 264), AF.Copy, -128.0)
-        act(b("zf32", 0, 128), z0, AF.Copy)
-        mm(b("psC1", 0, 128), z0, b("ident", 0, 128), True, True)
-        mm(b("psC1", 128, 256), z0, b("ident", 0, 128), True, False)
-        mm(b("psC1", 128, 256), z1, b("nident", 0, 128), False, True)
-        for k2 in range(3):
-            p = b("psC0", 128 * k2, 128 * k2 + 128)
-            mm(p, b("kl", 128 * k2, 128 * k2 + 128), b("zf32", 0, 128), True, False)
-            mm(p, b("row0", 0, 128), b("i976", 0, 128), False, True)
-        act(b("z0T", 0, 128), b("psC1", 0, 128), AF.Copy)
-        act(b("dzT", 0, 128), b("psC1", 128, 256), AF.Copy)
-        for q in range(4):
-            mm(b(("psA", "psB")[q // 2], 512 * (q % 2), 512 * (q % 2) + 512), b("z0T", 0, 128), b("ind", 512 * q, 512 * q + 512), True, True)
-        act(b("zrep", 0, 1024), b("psA", 0, 1024), AF.Copy)
-        act(b("zrep", 1024, 2048), b("psB", 0, 1024), AF.Copy)
-        for i in range(32):
-            mm(b("psS", 0, 128), b("ident", 0, 128), b("ptb", 16 + i, 4112, 32), i == 0, i == 31)
-        if t == 0:
-            inverse_table()
-            ts(b("orl", 0, 128), b("gq", 0, 128), b("aF", 1, 2), OP.is_equal)
-        ts(b("smi", 0, 1), b("psM", 2, 3), 0.5, OP.mult, -0.25, OP.add)
+            rest_of_setup()
+        play(EARLY[t], steps)
         ts(b("thf", 0, 1), b("smi", 0, 1), 4096.0, OP.min, 1.0 / 2048.0, OP.mult)
-
-        def heavy(r):
-            ts(b("smv", 4, 5), b("acc", 1, 2), -16.0, OP.mult)
-            ts(b("a16", 0, 1), b("acc", 0, 1), 16.0, OP.mult, b("smv", 4, 5), OP.add)
-            ts(b("yab", r, r + 1), b("a16", 0, 1), 0.0625, OP.mult)
-
-        if t > 0:
-            heavy(t - 1)
         scan(b("pE", 0, 8192), b("big", 0, 8192), b("big", 0, 8192), OP.add, OP.add)
         if not last:
-            dma("y", [(b("big", 0, 8192), b("zeros", 0, 8192))])
+            dma("y", [(b("big", 2048 * k, 2048 * k + 2048), b("zeros", 0, 2048)) for k in range(4)])
         else:
             dma("y", [(T.yz[:, 128:256], b("zf1", 0, 128)), (T.yz[:, 256:384], b("zf2", 0, 128))])
-        if t == 0:
-            gath("v", b("sg1", 0, 4096), b("wrep", 0, 4096), b("lm16", 256 * c1, 256 * c1 + 256))
         hI = b("hI", 0, 384)
-        ts(hI, b("psC0", 0, 384), b("a16", 0, 1), OP.add)
+        ts(hI, b("psA", 0, 384), b("a16", 0, 1), OP.add)
         ts(hI, hI, 4, OP.arith_shift_right, 4095, OP.bitwise_and)
         ts(hI, hI, b("thf", 0, 1), OP.mult, -4095.5 + 1.0 / 4096.0, OP.add)
         ts(b("pos16", 0, 384), hI, 4095.0, OP.add)
 
-        def two_sided(bk):
-            return t == 0 and bk in VO
-
-        def ring(m, bk, lo=0, step=1):
-            base = (OA0, OA1)[m] + BLK * (bk % 4)
-            return b("big", base + lo, base + BLK, step)
-
         def gather(bk):
-            o, win, off = b("big", OD0 + bk * BLK, OD0 + bk * BLK + BLK), b("pE", 0, 8192), b("pos16", 64 * bk, 64 * bk + 64)
-            zz = b("zrep", BLK * (bk % 2), BLK * (bk % 2) + BLK)
-            emit("v", lambda: g.vector.tensor_tensor(o[0], win[0].indirect(off[0]), zz[0], OP.subtract), [win, off, zz], [o])
-            if not two_sided(bk):
-                act(ring(0, bk), o, AF.Abs)
-            ps = ("psA", "psB")[bk % 2]
+            o, win, off, zr = b("big", OP_ + bk * BLK, OP_ + bk * BLK + BLK), b("pE", 0, 8192), b("pos16", 64 * bk, 64 * bk + 64), b("zrep", 0, BLK)
+            if bk % 2:
+                gath("s", o, win, off)
+            else:
+                emit("v", lambda: g.vector.tensor_tensor(o[0], win[0].indirect(off[0]), zr[0], OP.subtract), [win, off, zr], [o])
+
+        def fill(bk, m):
+            tile[bk, m] = free.pop(0)
             for h in range(2):
-                p = b(ps, 512 * h, 512 * h + 512)
-                mm(p, b("ident", 0, 128), b("big", OD0 + bk * BLK + 512 * h, OD0 + bk * BLK + 512 * h + 512), True, False)
-                mm(p, b("dzT", 0, 128), b("ind", BLK * (bk % 2) + 512 * h, BLK * (bk % 2) + 512 * h + 512), False, True)
-            act(ring(1, bk), b(ps, 0, 1024), AF.Abs)
-            if bk < 4:
-                if t == 0:
-                    inverse(1, bk, 4)
-                else:
-                    gath("s", b("sg1", BLK * bk, BLK * bk + BLK), b("wrep", 0, 4096), b("lm16", 256 * c1 + 64 * bk, 256 * c1 + 64 * bk + 64))
+                p = b(tile[bk, m], 512 * h, 512 * h + 512)
+                rep = b("ind", BLK * (bk % 2) + 512 * h, BLK * (bk % 2) + 512 * h + 512)
+                mm(p, id15, b("big", OP_ + bk * BLK + 512 * h, OP_ + bk * BLK + 512 * h + 512), True, False)
+                mm(p, b("zT", 128 * m, 128 * m + 128), rep, False, True)
 
-        def compare(bk):
-            k2, half = bk // 2, bk % 2
-            for m in range(2):
-                two = m == 0 and two_sided(bk)
-                o = b("psC%d" % m, 128 * k2 + 64 * half, 128 * k2 + 64 * half + 64)
-                lo = BLK * half
-                if two:
-                    d = b("big", OD0 + bk * BLK, OD0 + bk * BLK + BLK)
-                    ts(ring(0, bk), d, -68.0, OP.is_ge)
-                    ts(b("b0r", lo, lo + BLK), d, 68.0, OP.is_gt)
-                else:
-                    ts(ring(m, bk), ring(m, bk), 68.0, OP.is_le)
-                for a in range(16):
-                    mm(o, b("cb", 120 - 8 * a, 248 - 8 * a), ring(m, bk, a, 16), a == 0, a == 15 and not two)
-                if two:
-                    for a in range(16):
-                        mm(o, b("ncb", 120 - 8 * a, 248 - 8 * a), b("b0r", lo + a, lo + BLK, 16), False, a == 15)
+        def ring(m, bk):
+            base = (OI0, OI1)[m] + BLK * (bk % 4)
+            return b("big", base, base + BLK)
 
-        def extremes(k2, part=2):
-            d = b("big", OD0 + 2048 * k2, OD0 + 2048 * k2 + 2048)
-            if part != 1:
+        def absolute(bk, m):
+            if (bk, m) in tile:
+                act(ring(m, bk), b(tile[bk, m], 0, 1024), AF.Abs)
+                free.append(tile[bk, m])
+            else:
+                act(ring(m, bk), b("big", OP_ + bk * BLK, OP_ + bk * BLK + BLK), AF.Abs, 0.0, 15.0)
+
+        def compare(bk, m):
+            ts(ring(m, bk), ring(m, bk), 1024.0, OP.is_le)
+
+        def test(bk, m):
+            ts(ring(m, bk), b(tile[bk, m], 0, 1024), BIG, OP.add, BIG, OP.is_equal)
+            free.append(tile[bk, m])
+
+        def counts(k2, m):
+            base = (OI0, OI1)[m] + 2048 * (k2 % 2)
+            for a in range(16):
+                mm(b("psC%d" % m, 16 * k2 + a, 384, 48), b("big", base + a, base + 2048, 16), b("bi8", 0, 8), True, True)
+
+        def extremes(k2, part):
+            d = b("big", OP_ + 2048 * k2, OP_ + 2048 * k2 + 2048)
+            if part == 0:
                 scan(b(MXB[k2][0], MXB[k2][1], MXB[k2][1] + 2048), b("mkx", 0, 2048), d, OP.min, OP.max)
-            if part != 0:
+            else:
                 scan(b(MNB[k2][0], MNB[k2][1], MNB[k2][1] + 2048), b("mkn", 0, 2048), d, OP.max, OP.min)
 
-        def second_sums(h):
-            for i in range(32):
-                mm(b("psS", 128 + 64 * h, 192 + 64 * h), b("ident", 0, 128), b("sg1", 2048 * h + i, 2048 * h + 2048, 32), i == 0, i == 31)
+        def best(m):
+            scan(b("am%d" % m, 0, 384), b("amk", 0, 384), b("psC%d" % m, 0, 384), OP.min, OP.max)
 
-        gather(0)
-        gather(1)
-        gather(2)
-        if t == 0:
-            inverse_list(0)
-        compare(0)
-        gather(3)
-        compare(1)
-        extremes(0)
-        second_sums(0)
-        gather(4)
-        compare(2)
-        gather(5)
-        second_sums(1)
-        extremes(1)
-        compare(3)
-        if t in (1, 2):
-            inverse_list(t + 1)
-        if t == 0:
-            inverse_table()
-        compare(4)
-        extremes(2, 0)
-        compare(5)
-        ts(b("thr", 0, 256), b("psS", 0, 256), 4143.5, OP.is_lt, 0.5, OP.mult)
-        extremes(2, 1)
-        hits = (b("psM", 128, 256), b("psS", 256, 384))
-        for m in range(2):
-            act(b("hb%d" % m, 0, 384), b("psC%d" % m, 0, 384), AF.Relu, -11.0)
-            for k2 in range(3):
-                mm(hits[m], b("orl", 0, 128), b("hb%d" % m, 128 * k2, 128 * k2 + 128), k2 == 0, k2 == 2)
-        tt(b("L01", 0, 128), hits[0], b("thr", 0, 128), OP.is_lt)
-        ts(b("nh0", 0, 128), hits[0], 0.5, OP.is_ge)
-        tt(b("x1", 0, 128), hits[1], b("thr", 128, 256), OP.is_lt)
-        tt(b("L01", 128, 256), b("x1", 0, 128), b("nh0", 0, 128), OP.mult)
+        def words(m):
+            if m == 0:
+                tail.append(free.pop(0))
+                tail.extend(x for x in TILE if x != tail[0])
+            p = b(tail[0], 512 + 8 * m, 520 + 8 * m)
+            mm(p, b("crep", 0, 128), b("xs", 16 + 8 * m, 24 + 8 * m), True, True)
+            tt(b("bw%d" % m, 15, 143, 16), p, b("bi8", 0, 8), OP.mult)
 
-        def mark_gather(q, m, k0, k1):
-            c = (c0, c1)[m]
-            gath(q, b(MB[m], MO[m] + 512 * k0, MO[m] + 512 * k1), b("L01", 128 * m, 128 * m + 128),
-                 b("inv16", 256 * c + 32 * k0, 256 * c + 32 * k1))
-
-        def marks(m, h, first):
-            p = b(MP[h][0], MP[h][1], MP[h][1] + 64)
+        def marks(m):
+            p = b(tail[0], 768 * m, 768 * m + 256)
+            mm(p, b("one", 0, 128, 1, 1), b("cst", 128, 384, 1, 1), True, False)
             for a in range(16):
-                mm(p, b("dg", 128 * a, 128 * a + 128), b(MB[m], MO[m] + 1024 * h + a, MO[m] + 1024 * h + 1024, 16),
-                   first and a == 0, not first and a == 15)
+                lo = 4096 * cc[m] + 256 * a
+                mm(p, b("bw%d" % m, 15 - a, 143 - a), b("rr", lo, lo + 256), False, a == 15)
 
-        def extremes_end():
-            for buf, o, op in ((MXB, "mx", OP.max), (MNB, "mn", OP.min)):
-                e = [b(n, lo + 15, lo + 2048, 16) for n, lo in buf]
-                tt(b(o, 0, 128), e[0], e[1], op)
-                tt(b(o, 0, 128), b(o, 0, 128), e[2], op)
-            ts(b("sel", 0, 128), hits[0], 0.5, OP.is_lt)
-            ts(b("m1", 0, 128), hits[1], 0.5, OP.is_lt)
-            tt(b("sel", 128, 256), b("m1", 0, 128), b("nh0", 0, 128), OP.mult)
-            one, neg, mx, mn = b("ident", 0, 128), b("nident", 0, 128), b("mx", 0, 128), b("mn", 0, 128)
-            for k, x in enumerate((mx, mn)):
-                mm(b("psB", 0, 128), one, x, k == 0, k == 1)
-            for k, (l, x) in enumerate(((one, mx), (one, mn), (one, z0), (one, z0), (neg, z1), (neg, z1))):
-                mm(b("psB", 128, 256), l, x, k == 0, k == 5)
+        def rounded(m):
+            act(b("r%d" % m, 0, 256), b(tail[0], 768 * m, 768 * m + 256), AF.Copy, 2.0 ** -9)
+
+        def double(m):
+            p = b(tail[0], 768 * m, 768 * m + 256)
+            tt(p, b("r%d" % m, 0, 256), p, OP.is_gt)
+            tt(p, p, b("w2", 0, 256), OP.mult)
+            tt(b(("wa", "w1")[m], 0, 256), p, b(("wf", "wa")[m], 0, 256), OP.max)
+
+        def joint(part):
+            buf, o, op = ((MXB, "mx", OP.max), (MNB, "mn", OP.min))[part]
+            e = [b(n, lo + 15, lo + 2048, 16) for n, lo in buf]
+            tt(b(o, 0, 128), e[0], e[1], op)
+            tt(b(o, 0, 128), b(o, 0, 128), e[2], op)
+
+        def choices():
+            mm(b(tail[1], 0, 128, 1, 32), b("xs", 0, 32), ident, True, True)
+            act(b("xT", 0, 128, 1, 32), b(tail[1], 0, 128, 1, 32), AF.Copy, 0.0, b("sgn", 0, 1, 1, 32))
+
+        def spread():
+            xT = b("xT", 0, 128, 1, 32)
+            for m in range(2):
+                mm(b(tail[2], 128 * m, 128 * m + 128), b("em", 128 * m, 128 * m + 128, 1, 32), xT, True, True)
+            for k in range(4):
+                mm(b(tail[1], 128, 256), b("em", 128 * k, 128 * k + 128, 1, 32), xT, k == 0, k == 3)
+
+        def heavy():
+            total(b("a16", 0, 1), b(tail[1], 128, 256), 16.0)
+            act(b("yab", t, t + 1), b("a16", 0, 1), AF.Copy, 0.0, 0.0625)
+
+        def middle():
+            for m in range(2):
+                terms = ((n2id, zz[m]), (b("p2id", 0, 128), b("zh", 0, 128)), (ident, b("mx", 0, 128)), (ident, b("mn", 0, 128)))
+                for k, (l, x) in enumerate(terms):
+                    mm(b(tail[2], 512 + 128 * m, 640 + 128 * m), l, x, k == 0, k == 3)
 
         def quarter():
-            ts(b("q01", 0, 256), b("psB", 0, 256), 0.25, OP.mult, -0.375, OP.add)
+            ts(b("q01", 0, 256), b(tail[2], 512, 768), 0.25, OP.mult, -0.375, OP.add)
 
         def move():
-            tt(b("e01", 0, 256), b("q01", 0, 256), b("sel", 0, 256), OP.mult)
-            for m, z in ((0, z0), (1, z1)):
-                mm(b("psB", 512 + 128 * m, 640 + 128 * m), b("ident", 0, 128), b("e01", 128 * m, 128 * m + 128), True, False)
-                mm(b("psB", 512 + 128 * m, 640 + 128 * m), b("ident", 0, 128), z, False, True)
+            tt(b("e01", 0, 256), b("q01", 0, 256), b(tail[2], 0, 256), OP.mult)
+            for m in range(2):
+                mm(b(tail[1], 512 + 128 * m, 640 + 128 * m), ident, b("e01", 128 * m, 128 * m + 128), True, False)
+                mm(b(tail[1], 512 + 128 * m, 640 + 128 * m), ident, zz[m], False, True)
 
         def hand_over():
-            if t == 2:
-                act(b("zo%d" % t, 0, 256), b("psB", 512, 768), AF.Copy)
-            else:
-                cp(b("zo%d" % t, 0, 256), b("psB", 512, 768))
+            act(b("zo%d" % t, 0, 256), b(tail[1], 512, 768), AF.Copy)
             for kind in (("u0", "c0"), ("u1", "f1"), ("u2", "f2"), ("f3",))[t]:
                 send(kind)
 
-        if t == 0:
-            ts(b("dg", 0, 2048), b("dg", 0, 2048), 8.0, OP.mult)
-            inverse_list(1)
-        mark_gather("s", 0, 0, 4)
-        mark_gather("s", 0, 4, 8)
-        if last:
-            extremes_end()
-            quarter()
-            move()
-            hand_over()
-        marks(0, 0, True)
-        marks(0, 1, True)
-        mark_gather("v", 1, 0, 4)
-        marks(1, 0, False)
-        marks(1, 1, False)
-        mark_gather("v", 1, 4, 6)
-        marks(1, 2, True)
-        marks(0, 2, False)
-        marks(0, 3, True)
-        mark_gather("s", 1, 6, 8)
-        marks(1, 3, False)
-        ts(b("w2", 0, 256), b("wf", 0, 256), 2.0, OP.mult, 8.0, OP.min)
-        if not last:
-            extremes_end()
-        total(b("acc", 0, 1), b("sel", 0, 256))
-        total(b("acc", 1, 2), b("L01", 0, 256))
-        if t < 2:
-            inverse(t + 2, 0, 1)
-        for h in range(4):
-            w1 = b("w1", 64 * h, 64 * h + 64)
-            tt(w1, b(MP[h][0], MP[h][1], MP[h][1] + 64), b("w2", 64 * h, 64 * h + 64), OP.min)
-            tt(w1, w1, b("wf", 64 * h, 64 * h + 64), OP.max)
-        red(b("smv", 0, 1), b("w1", 0, 256))
-        mm(b("psM", 0, 1), b("bo32", 0, 128), b("smv", 0, 1), True, True)
-        if not last:
-            quarter()
-        ts(b("smv", 1, 2), b("psM", 0, 1), 7168.5, OP.is_gt, -0.5, OP.mult)
-        ts(b("smv", 2, 3), b("smv", 1, 2), 1.0, OP.add)
-        ts(b("smv", 3, 4), b("smv", 1, 2), -0.5, OP.mult, 128.0, OP.add)
-        ts(b("woff", 8, 264), b("w1", 0, 256), b("smv", 2, 3), OP.mult, b("smv", 3, 4), OP.add)
-        if not last:
+        m0, m1 = b("am0", 47, 384, 48), b("am1", 47, 384, 48)
+
+        def light(m):
+            if m == 0:
+                ts(b("thr", 0, 8), b("psC0", 384, 392), 4143.5, OP.is_lt, 11.5, OP.mult)
+                best(0)
+                tt(b("xs", 16, 24), m0, b("thr", 0, 8), OP.is_lt)
+            else:
+                ts(b("thr", 16, 24), b("psC1", 384, 392), 4143.5, OP.is_lt)
+                best(1)
+                tt(b("thr", 24, 32), b("thr", 8, 16), b("thr", 16, 24), OP.mult)
+                tt(b("xs", 8, 16), m1, b("thr", 8, 16), OP.is_lt)
+                tt(b("xs", 24, 32), m1, b("thr", 24, 32), OP.is_lt)
+
+        def first():
+            ts(b("xs", 0, 8), m0, 11.5, OP.is_lt)
+            ts(b("thr", 8, 16), m0, 11.5, OP.is_ge, 11.5, OP.mult)
+            ts(b("w2", 0, 256), b("wf", 0, 256), 2.0, OP.mult, 8.0, OP.min)
+
+        def whole():
+            red(b("smv", 0, 1), b("w1", 0, 256))
+            mm(b("psC0", 400, 401), b("bo32", 0, 128), b("smv", 0, 1), True, True)
+
+        def halve():
+            ts(b("smv", 1, 2), b("psC0", 400, 401), 7168.5, OP.is_gt, -0.5, OP.mult)
+            ts(b("smv", 2, 3), b("smv", 1, 2), 1.0, OP.add)
+            ts(b("smv", 3, 4), b("smv", 1, 2), -0.5, OP.mult, 128.0, OP.add)
+            ts(b("woff", 8, 264), b("w1", 0, 256), b("smv", 2, 3), OP.mult, b("smv", 3, 4), OP.add)
+
+        def prefix():
             prefix_scan()
             prefix_sums()
-            move()
-            prefix_end()
-            hand_over()
+
+        steps.update({"g": gather, "f": fill, "A": absolute, "C": compare, "T": test,
+                      "c": counts, "x": extremes, "L": light, "first": first, "w": words, "k": marks, "r": rounded, "d": double,
+                      "j": joint, "cho": choices, "spr": spread, "hea": heavy, "hand": hand_over, "mid": middle, "q": quarter, "move": move, "whole": whole, "halve": halve,
+                      "pre": prefix, "end": prefix_end})
+        play(HIT[t], steps)
 
     ts(b("ywb", 0, 256), b("woff", 8, 264), -128.0, OP.add)
     dma("y", [(T.yw[:], b("ywb", 0, 256))])
-    heavy(ROUNDS - 1)
     dma("y", [(T.ya[:], (T.yab[0::16, 0:4], "yab", 0, 4))])
     dma("s", [(T.yz[:, 384:512], b("zf3", 0, 128)), (T.yz[:, 0:128], b("zf3", 128, 256))])
     for sem, val in count.items():

@@ -8,20 +8,19 @@ ROUNDS = 4
 BLK = 1024
 OP_, OI0, OI1, OMX, OMN = 8192, 14336, 18432, 22528, 28672
 BIG = 1.5 * 2.0 ** 34
-EARLY = ("i i i i i i i i factors cen ms00 cend ms01 rep ms02 ms03",
-         "i ms00 ms01 ms02 ms03 cen ms10 i i cend ms11 sum0 rep ms12",
-         "i ms00 ms01 ms02 ms03 cen ms10 i i cend ms11 sum0 rep ms12",
-         "ms00 ms01 ms02 ms03 cen ms10 cend sum0 ms11 rep ms12 ms13")
-_H = ("g0 g1 f01 g2 A00 f10 T10 f21 C00 ms13 g3 f11 T01 T11 c00 f31 g4 A20 C20 f30 T30 sum1 c01 g5 T21 x00 f50 A40 c10 f41 C40 A31 C31 "
-      "T50 c20 x10 x01 L0 f51 c11 w0 A51 C51 T41 i x11 k0 c21 first L1 w1 k1 x20 i r0 r1 j0 cho x21 j1 d0 d1 i spr mid whole q halve "
-      "move hea i pre end i hand")
-HIT = ("g0 g1 f01 f10 f11 A00 g2 sum0 g3 T01 f21 i T10 f30 C00 c00 A20 T11 f31 c01 i i g4 g5 T21 f41 C20 i T30 f50 c10 A40 T31 f51 c11 "
-       "i i i i C40 T50 c20 ms10 ms11 x00 L0 w0 T41 ms12 T51 c21 k0 ms13 sum1 first x01 x10 x11 L1 w1 r0 k1 cho i d0 spr x20 r1 hea i "
-       "x21 i j0 j1 mid d1 whole i q halve pre move hand i end",
-       _H, _H.replace(" i ", " "),
-       "sum1 g0 g1 f01 f10 f11 A00 g2 g3 T10 f21 C00 c00 A01 f30 A11 f31 g4 C01 A20 C11 c01 g5 x00 C20 A21 f41 T30 f50 c10 A31 f51 C21 "
-       "A40 x01 C31 c11 A50 C40 C50 c20 A41 x10 A51 L0 w0 k0 C41 C51 c21 first x11 L1 w1 cho k1 spr x20 x21 j0 j1 mid r0 q move hand "
-       "r1 hea d0 d1 whole halve")
+_EARLY = "i row sc0 i ms01 ms02 ms11 sc1 cen seq ms03 i ms10 cend ms00 rep sum0 i pos "
+_HITS = ("g1 g0 f01 f10 g2 g4 f21 T10 f11 T01 g3 A00 g5 A20 ms13 ms12 f30 C00 T21 c00 fold A40 f50 T11 T30 f41 f31 T50 c01 C20 i C40 "
+         "sum1 T41 T31 c20 c10 f51 i L0 T51 w0 first c11 c21 L1 k0 w1 cho x0 k1 x1 spr r0 mid r1 d0 i d1 q turn dbl whole move halve "
+         "hea pre i end hand")
+ORDER = (
+    "i i rest sc0 i i sc1 i i row ms01 i i factors cen ms00 seq ms03 cend pos g3 rep g0 g1 f10 ms02 g5 i g2 A00 f01 sum0 T01 f21 g4 "
+    "f11 T10 f31 T11 c01 fold i C00 A20 C20 f30 T31 T30 T21 c00 f50 f51 i i c10 i i i T50 c11 A40 T51 C40 f41 i c20 T41 L0 ms10 c21 "
+    "ms12 w0 k0 first ms11 ms13 x0 sum1 L1 r0 i w1 d0 cho k1 r1 x1 i d1 i mid q turn i spr dbl whole move hand halve pre hea end",
+    _EARLY + _HITS,
+    _EARLY + _HITS.replace(" i ", " "),
+    "row ms13 ms02 ms00 sc0 ms01 sc1 ms03 cen fin ms12 sum0 ms11 cend ms10 sum1 seq pos rep g1 g0 f01 f10 f11 g2 g4 g3 A00 T10 f21 C00 "
+    "c00 T01 T11 g5 f30 A20 A40 T21 fold A30 f31 f41 C20 A31 C31 c01 f50 f51 C30 c10 C40 T50 A41 C41 T51 c20 L0 c11 first w0 x0 c21 "
+    "k0 L1 w1 r0 cho x1 k1 mid r1 q spr move d1 hand d0 turn dbl hea whole halve")
 
 MSG = [
     ("i01", "z0s", 0, 256, -1, "zin0", 0), ("i2", "z0s", 256, 384, -2, "zin1", 1), ("i3", "z0s", 384, 512, -3, "zin2", 1),
@@ -40,14 +39,14 @@ for _n, _w, _d in [
         ("zero", 128, _B), ("one", 128, _B), ("ident", 128, _B), ("nident", 128, _B), ("id15", 128, _B), ("n2id", 128, _B),
         ("p2id", 128, _B), ("zh", 128, _B), ("zrep", 1024, _B),
         ("bo32", 128, _F), ("lt32", 128, _F), ("one32", 128, _F), ("bi8", 8, _B), ("rs8", 8, _B), ("sgn", 8, _F),
-        ("cst", 384, _B), ("lane", 128, _B), ("crep", 128, _B), ("em", 512, _B), ("bw0", 144, _B), ("bw1", 144, _B),
+        ("cst", 384, _B), ("lane", 128, _B), ("crep", 128, _B), ("em", 512, _B), ("bw", 16, _B), ("bok", 128, _F),
         ("kl", 384, _F), ("aF", 8, _F),
         ("m128", 272, _F), ("wt", 256, _B), ("woff", 272, _B), ("ex", 264, _F), ("off16", 256, _U), ("w2", 256, _B), ("wf", 256, _B),
-        ("wa", 256, _B), ("w1", 256, _B), ("r0", 256, _B), ("r1", 256, _B),
+        ("mk", 512, _B), ("w1", 264, _B), ("r0", 256, _B), ("r1", 256, _B),
         ("smv", 8, _F), ("smi", 8, _I), ("a16", 8, _F), ("thf", 8, _F), ("yab", 4, _F), ("ywb", 256, _F),
         ("jk", 128, _B), ("zf32", 128, _F), ("zT", 256, _B), ("hI", 384, _I), ("pos16", 384, _U),
         ("am0", 384, _B), ("am1", 384, _B), ("thr", 32, _F), ("xs", 32, _B), ("xT", 128, _B),
-        ("mx", 128, _B), ("mn", 128, _B), ("q01", 256, _I), ("e01", 256, _B),
+        ("q01", 256, _I), ("e01", 256, _B),
         ("z0s", 512, _B), ("zin0", 256, _B), ("zin1", 128, _B), ("zin2", 128, _B), ("zr1", 128, _B), ("zr2", 128, _B),
         ("zr3", 128, _B), ("zc0", 128, _B), ("zf1", 128, _B), ("zf2", 128, _B), ("zf3", 256, _B),
         ("zo0", 256, _B), ("zo1", 256, _B), ("zo2", 256, _B), ("zo3", 256, _B)]:
@@ -58,6 +57,8 @@ for _n, _w in [("psA", 1024), ("psB", 1024), ("psD", 1024), ("psC0", 512), ("psC
     SCRATCH[_n] = ("psum", [128, _w], _F)
 
 SEMAPHORES = ["kv", "ks", "kt", "kg", "ls"] + ["d%d" % i for i in range(40)] + ["m_" + m[0] for m in MSG] + ["q_" + m[0] for m in MSG]
+SEMAPHORES += [x + "%d%d" % (t, part) for x in "hb" for t in range(ROUNDS) for part in range(2)]
+SEMAPHORES += ["hz"] + ["lf%d" % t for t in range(ROUNDS)] + [x + "z%d" % t for x in "hb" for t in range(ROUNDS - 1)]
 
 
 def relay_of(src, dst, which, T, topo):
@@ -67,6 +68,13 @@ def relay_of(src, dst, which, T, topo):
     near = [x for x in c if topo.die(x) == topo.die(src)]
     c = near if near else c
     return c[which % len(c)]
+
+
+def helper_of(src, cores, T, topo):
+    r = cores.index(src)
+    busy = [relay_of(src, cores[(r + m[4]) % NR], w, T, topo) for m in MSG for w in range(2)]
+    busy += [x for x in topo.cores_of(src) if all(topo.may_write(x, y) for y in cores if y != x)]
+    return [x for x in topo.cores_of(src) if T.rank_of(x) is None and topo.die(x) == topo.die(src) and x not in busy][0]
 
 
 def mask_for(src, dst, far_src, far_dst, topo):
@@ -89,6 +97,23 @@ def rank_program(g, core, T, topo):
         rank_main(g, core, rank, cores, T, topo)
         return
     sent = 0
+    for src in cores:
+        if helper_of(src, cores, T, topo) == core:
+            rid, pid = topo.addr(src, core)
+            g.wait_ge(T.sem.hz, popcount(topo.mask(src, core)))
+            for t in range(ROUNDS):
+                if t < ROUNDS - 1:
+                    g.wait_ge(T.sem["hz%d" % t], 1)
+                    g.remote_dma_fused([RemoteDMATransfer(dst_ids=[DstId(rid=rid, pnc=pid)] * 4, dma_engine_mask=topo.mask(core, src),
+                                                          remote_sem=T.sem["bz%d" % t], srcs=[T.zeros[:]],
+                                                          dsts=[T.big[:, 2048 * k:2048 * k + 2048] for k in range(4)])], local_sem=T.sem.ls)
+                    sent += popcount(topo.mask(core, src))
+                for part in range(2):
+                    at, name = 4096 * t + 2048 * part, "%d%d" % (t, part)
+                    g.wait_ge(T.sem["h" + name], popcount(topo.mask(src, core)))
+                    g.remote_dma(T.pE[:, 2048 * part:2048 * part + 2048], T.big[:, at:at + 2048], T.sem["b" + name], T.sem.ls, pid, rid,
+                                 topo.mask(core, src))
+                    sent += popcount(topo.mask(core, src))
     for kind, sbuf, lo, hi, off, land, which in MSG:
         for r in range(NR):
             src, dst = cores[r], cores[(r + off) % NR]
@@ -278,6 +303,10 @@ def rank_main(g, core, rank, cores, T, topo):
     send("i2")
     send("i3")
     iota(b("zeros", 0, 2048), [[0, 2048]], 0, 0)
+    helper = helper_of(core, cores, T, topo)
+    waits("g", [b("zeros", 0, 2048)], [])
+    g.remote_dma(T.zeros[:], T.zeros[:], T.sem.hz, T.sem.ls, topo.addr(helper, core)[1], topo.addr(helper, core)[0], topo.mask(core, helper))
+    count["ls"] += popcount(topo.mask(core, helper))
     asel(b("ind", 0, 2048), b("zeros", 0, 2048), [[-1, 128], [0, 16]], OP.not_equal, 0, 1, -15.0)
     asel(id15, zero, [[-1, 128]], OP.not_equal, 0, 1, 15.0)
     asel(b("rs8", 0, 8), b("zero", 0, 8), [[-16, 8]], OP.not_equal, 0, 1, 1.0)
@@ -294,8 +323,8 @@ def rank_main(g, core, rank, cores, T, topo):
             asel(b("crep", 0, 128), zero if lo == 0 else b("crep", 0, 128), [[0, 8], [-8, 16]], OP.not_equal, -lo, 1, 2.0 ** (lo - 14))
         asel(b("em", 0, 512), b("zeros", 0, 512), [[-8, 4], [-1, 8], [0, 16]], OP.not_equal, 0, 1, 1.0)
         asel(b("sgn", 0, 1), b("one32", 0, 1), [[0, 1]], OP.is_ge, 15, -1, -1.0)
-        iota(b("bw0", 0, 144), [[0, 144]], 0, 0)
-        iota(b("bw1", 0, 144), [[0, 144]], 0, 0)
+        asel(b("w1", 256, 258), b("zero", 0, 2), [[1, 2]], OP.not_equal, 0, 0, -448.0)
+        asel(b("w1", 256, 258), b("w1", 256, 258), [[1, 2]], OP.not_equal, -1, 0, -1.0 / 32.0)
 
     for a in range(16):
         act(b("vals", 256 * a, 256 * a + 256), b("pat", 0, 256), AF.Copy, 0.0, b("mF", a, a + 1))
@@ -347,18 +376,21 @@ def rank_main(g, core, rank, cores, T, topo):
     ZSRC = [(("zin0", 0), ("zin0", 128)), (("zr1", 0), ("zin1", 0)), (("zr2", 0), ("zin2", 0)), (("zr3", 0), ("zc0", 0))]
     TILE = ("psA", "psB", "psD")
     pieces = [0]
-    MXB = (("big", OMX), ("big", OMX + 2048), ("big", OMX + 4096))
-    MNB = (("big", OMN), ("big", OMN + 2048), ("pE", 0))
-    for t in range(ROUNDS):
+
+    def round_steps(t):
         cc = (t % 4, (t + 1) % 4)
-        last = t == ROUNDS - 1
         zz = [b(n, lo, lo + 128) for n, lo in ZSRC[t]]
         wrow = b("ptb", 16, 4112)
         tile, free, tail = {}, list(TILE), []
-        dma("y", [((T.ptb[0::16, 16:4112], "ptb", 16, 4112), b("woff", 8, 264))])
-        ts(b("smi", 0, 1), b("psC0", 402, 403), 0.5, OP.mult, -0.25, OP.add)
-        bigw, offs, dif = b("big", 0, 32768), b("off16", 0, 256), b("diffp", 0, 4096)
-        emit("v", lambda: g.vector.tensor_copy(bigw[0].indirect(offs[0]), dif[0]), [dif, offs], [bigw])
+
+        def row():
+            dma("y", [((T.ptb[0::16, 16:4112], "ptb", 16, 4112), b("woff", 8, 264))])
+
+        def scatter(h):
+            if h == 0:
+                ts(b("smi", 0, 1), b("psC0", 402, 403), 0.5, OP.mult, -0.25, OP.add)
+            bigw, offs, dif = b("big", 0, 32768), b("off16", 128 * h, 128 * h + 128), b("diffp", 2048 * h, 2048 * h + 2048)
+            emit("v", lambda: g.vector.tensor_copy(bigw[0].indirect(offs[0]), dif[0]), [dif, offs], [bigw])
 
         def members(q, m, k):
             gath(q, b("wg%d" % m, BLK * k, BLK * k + BLK), wrow, b("lm16", 256 * cc[m] + 64 * k, 256 * cc[m] + 64 * k + 64))
@@ -390,32 +422,32 @@ def rank_main(g, core, rank, cores, T, topo):
         def factors():
             late_constants()
             act(kl, kl, AF.Copy, 0.0, b("aF", 2, 3))
+            act(b("bok", 0, 128), b("bo32", 0, 128), AF.Copy, 0.0, 1024.0)
 
         def next_inverse():
             inverse(pieces[0] // 8, pieces[0] % 8)
             pieces[0] += 1
 
-        def play(order, steps):
-            for word in order.split():
-                name = word.rstrip("0123456789")
-                steps[name](*[int(x) for x in word[len(name):]])
+        def sequence():
+            ts(b("thf", 0, 1), b("smi", 0, 1), 4096.0, OP.min, 1.0 / 2048.0, OP.mult)
+            scan(b("pE", 0, 8192), b("big", 0, 8192), b("big", 0, 8192), OP.add, OP.add)
+            if t < ROUNDS - 1:
+                waits("g", [], [b("big", 0, 8192)])
+                rid, pid = topo.addr(helper, core)
+                g.remote_sem_update(T.sem["hz%d" % t], T.sem.ls, pid, rid, 1 << topo.engines(core, helper)[0])
+                count["ls"] += 1
+                count["bz%d" % t] = 4 * popcount(topo.mask(helper, core))
+                note("big", 0, 8192, True, "bz%d" % t, count["bz%d" % t], "net")
 
-        steps = {"i": next_inverse, "ms": lambda m, k: members("s", m, k), "mv": lambda m, k: members("v", m, k), "sum": sums,
-                 "cen": centres, "cend": centres_end, "rep": repeated, "factors": factors}
-        if t == 0:
-            rest_of_setup()
-        play(EARLY[t], steps)
-        ts(b("thf", 0, 1), b("smi", 0, 1), 4096.0, OP.min, 1.0 / 2048.0, OP.mult)
-        scan(b("pE", 0, 8192), b("big", 0, 8192), b("big", 0, 8192), OP.add, OP.add)
-        if not last:
-            dma("y", [(b("big", 2048 * k, 2048 * k + 2048), b("zeros", 0, 2048)) for k in range(4)])
-        else:
+        def places():
+            hI = b("hI", 0, 384)
+            ts(hI, b("psA", 0, 384), b("a16", 0, 1), OP.add)
+            ts(hI, hI, 4, OP.arith_shift_right, 4095, OP.bitwise_and)
+            ts(hI, hI, b("thf", 0, 1), OP.mult, -4095.5 + 1.0 / 4096.0, OP.add)
+            ts(b("pos16", 0, 384), hI, 4095.0, OP.add)
+
+        def finished():
             dma("y", [(T.yz[:, 128:256], b("zf1", 0, 128)), (T.yz[:, 256:384], b("zf2", 0, 128))])
-        hI = b("hI", 0, 384)
-        ts(hI, b("psA", 0, 384), b("a16", 0, 1), OP.add)
-        ts(hI, hI, 4, OP.arith_shift_right, 4095, OP.bitwise_and)
-        ts(hI, hI, b("thf", 0, 1), OP.mult, -4095.5 + 1.0 / 4096.0, OP.add)
-        ts(b("pos16", 0, 384), hI, 4095.0, OP.add)
 
         def gather(bk):
             o, win, off, zr = b("big", OP_ + bk * BLK, OP_ + bk * BLK + BLK), b("pE", 0, 8192), b("pos16", 64 * bk, 64 * bk + 64), b("zrep", 0, BLK)
@@ -455,12 +487,27 @@ def rank_main(g, core, rank, cores, T, topo):
             for a in range(16):
                 mm(b("psC%d" % m, 16 * k2 + a, 384, 48), b("big", base + a, base + 2048, 16), b("bi8", 0, 8), True, True)
 
-        def extremes(k2, part):
-            d = b("big", OP_ + 2048 * k2, OP_ + 2048 * k2 + 2048)
+        def fold():
+            thirds = [b("big", OP_ + 2048 * k2, OP_ + 2048 * k2 + 2048) for k2 in range(3)]
+            waits("g", thirds, [b("pE", 0, 4096)])
+            mask = topo.mask(core, helper)
+            rid, pid = topo.addr(helper, core)
+            for part in range(2):
+                at, name = 4096 * t + 2048 * part, "%d%d" % (t, part)
+                g.remote_dma_fused([RemoteDMATransfer(dst_ids=[DstId(rid=rid, pnc=pid)], dma_engine_mask=mask, remote_sem=T.sem["h" + name],
+                                                      srcs=[x[0] for x in thirds], dsts=[T.big[:, at:at + 2048]], alu_op=2 + part)],
+                                   local_sem=T.sem["lf%d" % t])
+                count["b" + name] = popcount(topo.mask(helper, core))
+                note("pE", 2048 * part, 2048 * part + 2048, True, "b" + name, count["b" + name], "net")
+            count["lf%d" % t] = 2 * popcount(mask)
+            note("big", OP_, OP_ + 6144, False, "lf%d" % t, count["lf%d" % t], "net")
+
+        def extremes(part):
+            d, o = b("pE", 2048 * part, 2048 * part + 2048), b("pE", 4096 + 2048 * part, 6144 + 2048 * part)
             if part == 0:
-                scan(b(MXB[k2][0], MXB[k2][1], MXB[k2][1] + 2048), b("mkx", 0, 2048), d, OP.min, OP.max)
+                scan(o, b("mkx", 0, 2048), d, OP.min, OP.max)
             else:
-                scan(b(MNB[k2][0], MNB[k2][1], MNB[k2][1] + 2048), b("mkn", 0, 2048), d, OP.max, OP.min)
+                scan(o, b("mkn", 0, 2048), d, OP.max, OP.min)
 
         def best(m):
             scan(b("am%d" % m, 0, 384), b("amk", 0, 384), b("psC%d" % m, 0, 384), OP.min, OP.max)
@@ -471,29 +518,30 @@ def rank_main(g, core, rank, cores, T, topo):
                 tail.extend(x for x in TILE if x != tail[0])
             p = b(tail[0], 512 + 8 * m, 520 + 8 * m)
             mm(p, b("crep", 0, 128), b("xs", 16 + 8 * m, 24 + 8 * m), True, True)
-            tt(b("bw%d" % m, 15, 143, 16), p, b("bi8", 0, 8), OP.mult)
+            tt(b("bw", 8 * m, 8 * m + 8), p, b("bi8", 0, 8), OP.mult)
 
         def marks(m):
-            p = b(tail[0], 768 * m, 768 * m + 256)
-            mm(p, b("one", 0, 128, 1, 1), b("cst", 128, 384, 1, 1), True, False)
-            for a in range(16):
-                lo = 4096 * cc[m] + 256 * a
-                mm(p, b("bw%d" % m, 15 - a, 143 - a), b("rr", lo, lo + 256), False, a == 15)
+            lo = 768 * m
+            mm(b(tail[0], lo, lo + 256), b("one", 0, 128, 1, 1), b("cst", 128, 384, 1, 1), True, False)
+            for ch in range(32):
+                at = 4096 * cc[m] + 128 * ch
+                mm(b(tail[0], lo + ch, lo + 256, 32), b("rr", at, at + 128), b("bw", 8 * m, 8 * m + 8), False, ch == 31)
 
         def rounded(m):
             act(b("r%d" % m, 0, 256), b(tail[0], 768 * m, 768 * m + 256), AF.Copy, 2.0 ** -9)
 
-        def double(m):
-            p = b(tail[0], 768 * m, 768 * m + 256)
-            tt(p, b("r%d" % m, 0, 256), p, OP.is_gt)
-            tt(p, p, b("w2", 0, 256), OP.mult)
-            tt(b(("wa", "w1")[m], 0, 256), p, b(("wf", "wa")[m], 0, 256), OP.max)
+        def marked(m):
+            tt(b("mk", 256 * m, 256 * m + 256), b("r%d" % m, 0, 256), b(tail[0], 768 * m, 768 * m + 256), OP.is_gt)
 
-        def joint(part):
-            buf, o, op = ((MXB, "mx", OP.max), (MNB, "mn", OP.min))[part]
-            e = [b(n, lo + 15, lo + 2048, 16) for n, lo in buf]
-            tt(b(o, 0, 128), e[0], e[1], op)
-            tt(b(o, 0, 128), b(o, 0, 128), e[2], op)
+        def turn():
+            for h in range(2):
+                for m in range(2):
+                    mm(b(tail[0], 256 + 128 * h, 384 + 128 * h), b("mk", 256 * m + h, 256 * m + 256, 2), id15, m == 0, m == 1)
+
+        def double():
+            p = b(tail[0], 256, 512)
+            tt(p, p, b("w2", 0, 256), OP.min)
+            tt(b("w1", 0, 256), p, b("wf", 0, 256), OP.max)
 
         def choices():
             mm(b(tail[1], 0, 128, 1, 32), b("xs", 0, 32), ident, True, True)
@@ -512,7 +560,8 @@ def rank_main(g, core, rank, cores, T, topo):
 
         def middle():
             for m in range(2):
-                terms = ((n2id, zz[m]), (b("p2id", 0, 128), b("zh", 0, 128)), (ident, b("mx", 0, 128)), (ident, b("mn", 0, 128)))
+                terms = ((n2id, zz[m]), (b("p2id", 0, 128), b("zh", 0, 128)), (ident, b("pE", 4111, 6144, 16)),
+                         (ident, b("pE", 6159, 8192, 16)))
                 for k, (l, x) in enumerate(terms):
                     mm(b(tail[2], 512 + 128 * m, 640 + 128 * m), l, x, k == 0, k == 3)
 
@@ -550,24 +599,31 @@ def rank_main(g, core, rank, cores, T, topo):
             ts(b("w2", 0, 256), b("wf", 0, 256), 2.0, OP.mult, 8.0, OP.min)
 
         def whole():
-            red(b("smv", 0, 1), b("w1", 0, 256))
-            mm(b("psC0", 400, 401), b("bo32", 0, 128), b("smv", 0, 1), True, True)
+            red(b("smv", 0, 1), b("w1", 0, 258))
+            mm(b("psC0", 400, 401), b("bok", 0, 128), b("smv", 0, 1), True, True)
 
         def halve():
-            ts(b("smv", 1, 2), b("psC0", 400, 401), 7168.5, OP.is_gt, -0.5, OP.mult)
-            ts(b("smv", 2, 3), b("smv", 1, 2), 1.0, OP.add)
-            ts(b("smv", 3, 4), b("smv", 1, 2), -0.5, OP.mult, 128.0, OP.add)
-            ts(b("woff", 8, 264), b("w1", 0, 256), b("smv", 2, 3), OP.mult, b("smv", 3, 4), OP.add)
+            ts(b("smv", 2, 3), b("psC0", 400, 401), 128.0, OP.max, 256.5, OP.min)
+            ts(b("smv", 3, 4), b("psC0", 400, 401), 0.0, OP.is_lt, 0.5, OP.max)
+            ts(b("woff", 8, 264), b("w1", 0, 256), b("smv", 2, 3), OP.add, b("smv", 3, 4), OP.mult)
 
         def prefix():
             prefix_scan()
             prefix_sums()
 
-        steps.update({"g": gather, "f": fill, "A": absolute, "C": compare, "T": test,
-                      "c": counts, "x": extremes, "L": light, "first": first, "w": words, "k": marks, "r": rounded, "d": double,
-                      "j": joint, "cho": choices, "spr": spread, "hea": heavy, "hand": hand_over, "mid": middle, "q": quarter, "move": move, "whole": whole, "halve": halve,
-                      "pre": prefix, "end": prefix_end})
-        play(HIT[t], steps)
+        return {"row": row, "sc": scatter, "rest": rest_of_setup, "seq": sequence, "pos": places, "fin": finished, "i": next_inverse,
+                "ms": lambda m, k: members("s", m, k), "mv": lambda m, k: members("v", m, k), "sum": sums, "cen": centres,
+                "cend": centres_end, "rep": repeated, "factors": factors, "g": gather, "f": fill, "A": absolute, "C": compare,
+                "T": test, "c": counts, "x": extremes, "L": light, "first": first, "w": words, "k": marks, "r": rounded,
+                "d": marked, "turn": turn, "dbl": double, "fold": fold, "cho": choices, "spr": spread, "hea": heavy,
+                "hand": hand_over, "mid": middle, "q": quarter, "move": move, "whole": whole, "halve": halve, "pre": prefix,
+                "end": prefix_end}
+
+    steps = [round_steps(t) for t in range(ROUNDS)]
+    for t in range(ROUNDS):
+        for word in ORDER[t].split():
+            name = word.lstrip("-").rstrip("0123456789")
+            steps[t - word.count("-")][name](*[int(x) for x in word.lstrip("-")[len(name):]])
 
     ts(b("ywb", 0, 256), b("woff", 8, 264), -128.0, OP.add)
     dma("y", [(T.yw[:], b("ywb", 0, 256))])

@@ -1,3 +1,4 @@
+import numpy as np
 from concourse.bass import DstId, RemoteDMATransfer
 from concourse.mybir import dt, AluOpType, AxisListType, ActivationFunctionType
 
@@ -6,59 +7,73 @@ AF = ActivationFunctionType
 NR = 8
 ROUNDS = 4
 BLK = 1024
-OP_, OI0, OI1, OMX, OMN = 8192, 14336, 18432, 22528, 28672
+OP_, OI0, OI1, OI2 = 8192, 14336, 20480, 26624
 BIG = 1.5 * 2.0 ** 34
-_EARLY = "i row sc0 i ms01 ms02 ms11 sc1 cen seq ms03 i ms10 cend ms00 rep sum0 i pos "
-_HITS = ("g1 g0 f01 f10 g2 g4 f21 T10 f11 T01 g3 A00 g5 A20 ms13 ms12 f30 C00 T21 c00 fold A40 f50 T11 T30 f41 f31 T50 c01 C20 i C40 "
-         "sum1 T41 T31 c20 c10 f51 i L0 T51 w0 first c11 c21 L1 k0 w1 cho x0 k1 x1 spr r0 mid r1 d0 i d1 q turn dbl whole move halve "
-         "hea pre i end hand")
-ORDER = (
-    "i i rest sc0 i i sc1 i i row ms01 i i factors cen ms00 seq ms03 cend pos g3 rep g0 g1 f10 ms02 g5 i g2 A00 f01 sum0 T01 f21 g4 "
-    "f11 T10 f31 T11 c01 fold i C00 A20 C20 f30 T31 T30 T21 c00 f50 f51 i i c10 i i i T50 c11 A40 T51 C40 f41 i c20 T41 L0 ms10 c21 "
-    "ms12 w0 k0 first ms11 ms13 x0 sum1 L1 r0 i w1 d0 cho k1 r1 x1 i d1 i mid q turn i spr dbl whole move hand halve pre hea end",
-    _EARLY + _HITS,
-    _EARLY + _HITS.replace(" i ", " "),
-    "row ms13 ms02 ms00 sc0 ms01 sc1 ms03 cen fin ms12 sum0 ms11 cend ms10 sum1 seq pos rep g1 g0 f01 f10 f11 g2 g4 g3 A00 T10 f21 C00 "
-    "c00 T01 T11 g5 f30 A20 A40 T21 fold A30 f31 f41 C20 A31 C31 c01 f50 f51 C30 c10 C40 T50 A41 C41 T51 c20 L0 c11 first w0 x0 c21 "
-    "k0 L1 w1 r0 cho x1 k1 mid r1 q spr move d1 hand d0 turn dbl hea whole halve")
+ROUND = 1.5 * 2.0 ** 23
+PIECES = 2
+FILLS = 2
+CUTS = ((0, 2, 4, 6, 8), (0, 2, 4, 6, 8), (0, 1, 2, 3, 4, 5, 6, 7, 8), (0, 1, 2, 3, 4, 5, 6, 7, 8))
+FIRST = 11.0
+TAKEN = ()
+WEIGHT = (1.0, 1.0, 1.0, 1.0)
+SHARE = 5
+TESTS = ("ATATATATATAT", "ATAAATAAATAA", "TATATATATATA", "TATATATATATA")
+LANES = (128, 128, 64, 64)
+FOLD = (6, 6, 6, 4)
+MEMBERS = ("ssssssvv", "ssssssss", "ssssssss", "ssssssss")
+CYCLE, COLUMN = np.array([0.83e-3, 0.83e-3, 1.1e-3, 0.95e-3]), np.array([0.52e-3, 0.52e-3, 0.7e-3, 0.6e-3])
+GATHER, SCATTER = np.array([1.1, 1.4, 1.6, 2.0]), np.array([1.8, 3.0, 5.0, 2.2])
+CALL, WAKE = {"v": 0.06, "s": 0.1, "t": 0.006, "g": 0.15, "y": 0.05}, 0.06
+WAKES = (0.06, 0.06, 0.12, 0.1)
+ROUNDER = "ss"
+PARTS = ((0, 384, 0),)
+SEED = 6
+SWAPS = 18000
+SLACK = 0.0015
+SHAKE = 8.0
+REACH = 12.0
+PASSES = 30
+CASES = (0, 1)
 
 MSG = [
     ("i01", "z0s", 0, 256, -1, "zin0", 0), ("i2", "z0s", 256, 384, -2, "zin1", 1), ("i3", "z0s", 384, 512, -3, "zin2", 1),
     ("u0", "zo0", 128, 256, -1, "zr1", 0), ("c0", "zo0", 0, 128, -3, "zc0", 1),
     ("u1", "zo1", 128, 256, -1, "zr2", 0), ("f1", "zo1", 0, 128, 2, "zf1", 1),
     ("u2", "zo2", 128, 256, -1, "zr3", 0), ("f2", "zo2", 0, 128, 3, "zf2", 1),
-    ("f3", "zo3", 0, 256, 4, "zf3", 0)]
+    ("f3", "zo3", 0, 128, 4, "zf3", 1), ("f0", "zo3", 128, 256, 4, "zf0", 0)]
 
 _B, _F, _I, _U = "bfloat16", "float32", "int32", "uint16"
 SCRATCH = {}
 for _n, _w, _d in [
-        ("big", 32768, _B), ("ptb", 4112, _B), ("diffp", 4096, _B), ("pE", 8192, _B), ("zeros", 2048, _B),
-        ("wg0", 4096, _B), ("wg1", 4096, _B), ("rf", 4096, _F), ("vals", 4096, _F), ("rr", 16384, _B),
-        ("ind", 2048, _B), ("mkx", 2048, _B), ("mkn", 2048, _B), ("amk", 384, _B),
+        ("big", 32768, _B), ("ptb", 4112, _B), ("diffp", 4096, _B), ("pE", 8192, _B), ("zeros", 1024, _B),
+        ("wg0", 4096, _B), ("wg1", 4096, _B), ("rf", 8192, _F), ("vals", 4096, _F), ("rr", 12288, _B),
+        ("ind", 1024, _B), ("mkx", 1024, _B), ("mkn", 1024, _B), ("amk", 384, _B),
         ("lmI", 1024, _I), ("lm16", 1024, _U), ("pat", 256, _F), ("mI", 16, _I), ("mF", 16, _F),
         ("zero", 128, _B), ("one", 128, _B), ("ident", 128, _B), ("nident", 128, _B), ("id15", 128, _B), ("n2id", 128, _B),
-        ("p2id", 128, _B), ("zh", 128, _B), ("zrep", 1024, _B),
+        ("p2id", 128, _B), ("zrep", 1024, _B), ("zh", 256, _B),
         ("bo32", 128, _F), ("lt32", 128, _F), ("one32", 128, _F), ("bi8", 8, _B), ("rs8", 8, _B), ("sgn", 8, _F),
-        ("cst", 384, _B), ("lane", 128, _B), ("crep", 128, _B), ("em", 512, _B), ("bw", 16, _B), ("bok", 128, _F),
-        ("kl", 384, _F), ("aF", 8, _F),
+        ("cst", 384, _B), ("lane", 64, _B), ("crep", 128, _B), ("em", 512, _B), ("bw", 16, _B), ("bok", 128, _F),
+        ("kl", 1536, _F), ("aF", 8, _F),
         ("m128", 272, _F), ("wt", 256, _B), ("woff", 272, _B), ("ex", 264, _F), ("off16", 256, _U), ("w2", 256, _B), ("wf", 256, _B),
         ("mk", 512, _B), ("w1", 264, _B), ("r0", 256, _B), ("r1", 256, _B),
         ("smv", 8, _F), ("smi", 8, _I), ("a16", 8, _F), ("thf", 8, _F), ("yab", 4, _F), ("ywb", 256, _F),
         ("jk", 128, _B), ("zf32", 128, _F), ("zT", 256, _B), ("hI", 384, _I), ("pos16", 384, _U),
         ("am0", 384, _B), ("am1", 384, _B), ("thr", 32, _F), ("xs", 32, _B), ("xT", 128, _B),
-        ("q01", 256, _I), ("e01", 256, _B),
+        ("q01", 256, _I), ("mx", 256, _B),
         ("z0s", 512, _B), ("zin0", 256, _B), ("zin1", 128, _B), ("zin2", 128, _B), ("zr1", 128, _B), ("zr2", 128, _B),
-        ("zr3", 128, _B), ("zc0", 128, _B), ("zf1", 128, _B), ("zf2", 128, _B), ("zf3", 256, _B),
+        ("zr3", 128, _B), ("zc0", 128, _B), ("zf1", 128, _B), ("zf2", 128, _B), ("zf3", 128, _B), ("zf0", 128, _B),
         ("zo0", 256, _B), ("zo1", 256, _B), ("zo2", 256, _B), ("zo3", 256, _B)]:
     SCRATCH[_n] = ("sbuf", [128, _w], _d)
 for _m in MSG:
     SCRATCH["y_" + _m[0]] = ("sbuf", [128, _m[3] - _m[2]], _B)
-for _n, _w in [("psA", 1024), ("psB", 1024), ("psD", 1024), ("psC0", 512), ("psC1", 512)]:
+TILE = ("psA", "psB", "psD")
+for _n, _w in [("psT", 3072), ("psC0", 512), ("psC1", 512)]:
     SCRATCH[_n] = ("psum", [128, _w], _F)
 
 SEMAPHORES = ["kv", "ks", "kt", "kg", "ls"] + ["d%d" % i for i in range(40)] + ["m_" + m[0] for m in MSG] + ["q_" + m[0] for m in MSG]
 SEMAPHORES += [x + "%d%d" % (t, part) for x in "hb" for t in range(ROUNDS) for part in range(2)]
 SEMAPHORES += ["hz"] + ["lf%d" % t for t in range(ROUNDS)] + [x + "z%d" % t for x in "hb" for t in range(ROUNDS - 1)]
+PLAN = []
 
 
 def relay_of(src, dst, which, T, topo):
@@ -70,11 +85,15 @@ def relay_of(src, dst, which, T, topo):
     return c[which % len(c)]
 
 
-def helper_of(src, cores, T, topo):
-    r = cores.index(src)
-    busy = [relay_of(src, cores[(r + m[4]) % NR], w, T, topo) for m in MSG for w in range(2)]
-    busy += [x for x in topo.cores_of(src) if all(topo.may_write(x, y) for y in cores if y != x)]
-    return [x for x in topo.cores_of(src) if T.rank_of(x) is None and topo.die(x) == topo.die(src) and x not in busy][0]
+def helpers_of(src, cores, T, topo):
+    busy = [x for x in topo.cores_of(src) if all(topo.may_write(x, y) for y in cores if y != x)]
+    idle = [x for x in topo.cores_of(src) if T.rank_of(x) is None and x not in busy]
+    return sorted(idle, key=lambda x: topo.die(x) != topo.die(src))[:2]
+
+
+def landing(t, part):
+    name, lo = ("pE", 0) if FOLD[t] == 6 else ("big", OI2 + 2 * BLK)
+    return name, lo + BLK * part, lo + BLK * part + BLK
 
 
 def mask_for(src, dst, far_src, far_dst, topo):
@@ -98,20 +117,25 @@ def rank_program(g, core, T, topo):
         return
     sent = 0
     for src in cores:
-        if helper_of(src, cores, T, topo) == core:
+        pair = helpers_of(src, cores, T, topo)
+        if core in pair:
             rid, pid = topo.addr(src, core)
             g.wait_ge(T.sem.hz, popcount(topo.mask(src, core)))
+            g.sync.wait_ge(T.sem.hz, popcount(topo.mask(src, core)))
+            for k in range(4):
+                g.sync.dma_start(T.pE[:, BLK * k:BLK * k + BLK], T.zeros[:]).then_inc(T.sem.d0, 16)
+            g.wait_ge(T.sem.d0, 64)
+            half = 4096 * pair.index(core)
             for t in range(ROUNDS):
                 if t < ROUNDS - 1:
                     g.wait_ge(T.sem["hz%d" % t], 1)
-                    g.remote_dma_fused([RemoteDMATransfer(dst_ids=[DstId(rid=rid, pnc=pid)] * 4, dma_engine_mask=topo.mask(core, src),
-                                                          remote_sem=T.sem["bz%d" % t], srcs=[T.zeros[:]],
-                                                          dsts=[T.big[:, 2048 * k:2048 * k + 2048] for k in range(4)])], local_sem=T.sem.ls)
+                    g.remote_dma(T.big[:, half:half + 4096], T.pE[:, 0:4096], T.sem["bz%d" % t], T.sem.ls, pid, rid, topo.mask(core, src))
                     sent += popcount(topo.mask(core, src))
-                for part in range(2):
-                    at, name = 4096 * t + 2048 * part, "%d%d" % (t, part)
+                for part in range(2 if core == pair[0] else 0):
+                    at, name = BLK * (2 * t + part), "%d%d" % (t, part)
                     g.wait_ge(T.sem["h" + name], popcount(topo.mask(src, core)))
-                    g.remote_dma(T.pE[:, 2048 * part:2048 * part + 2048], T.big[:, at:at + 2048], T.sem["b" + name], T.sem.ls, pid, rid,
+                    buf, lo, hi = landing(t, part)
+                    g.remote_dma(T[buf][:, lo:hi], T.big[:, at:at + BLK], T.sem["b" + name], T.sem.ls, pid, rid,
                                  topo.mask(core, src))
                     sent += popcount(topo.mask(core, src))
     for kind, sbuf, lo, hi, off, land, which in MSG:
@@ -127,157 +151,333 @@ def rank_program(g, core, T, topo):
         g.wait_ge(T.sem.ls, sent)
 
 
+def plan(calls):
+    n = len(calls)
+    before, after, seen = [set() for _ in calls], [[] for _ in calls], {}
+    for i, c in enumerate(calls):
+        for write, xs in ((False, c[2]), (True, c[3])):
+            for x in xs:
+                for lo, hi, wr, j in seen.get(x[1], []):
+                    if lo < x[3] and x[2] < hi and (wr or write) and j != i and not (wr and write and c[6] and calls[j][6]):
+                        before[i].add(j)
+        for write, xs in ((False, c[2]), (True, c[3])):
+            for x in xs:
+                old = [e for e in seen.get(x[1], []) if not (write and not c[6] and x[2] <= e[0] and e[1] <= x[3])]
+                seen[x[1]] = old + [(x[2], x[3], write, i)]
+        before[i] -= {k for j in before[i] if not calls[j][5] + calls[j][7] for k in before[j] if not calls[k][5] + calls[k][7]}
+        for j in before[i]:
+            after[j].append(i)
+    times = [[float((c[4] + 0.0 * CYCLE)[case]) for c in calls] for case in range(len(CYCLE))]
+    way = [0.0] * n
+    for i in range(n - 1, -1, -1):
+        way[i] = times[1][i] + calls[i][5] + max([way[k] + WAKE for k in after[i]], default=0.0)
+    banks = [sorted({(x[1], k) for x in c[2] + c[3] if x[1].startswith("ps") for k in range(x[2] // 512, (x[3] - 1) // 512 + 1)})
+             for c in calls]
+
+    def gap(j, k):
+        return 0.0 if calls[k][0] == "-" or calls[j][0] == calls[k][0] == "t" else WAKE + late[j]
+
+    late = [c[5] + c[7] for c in calls]
+    edges = [[(j, gap(j, i) > 0.0) for j in sorted(before[i])] for i in range(n)]
+
+    def replay(order, time):
+        wake = WAKES[times.index(time)]
+        done, free, held, engines = [0.0] * n, {}, {}, (0.0, -1)
+        for i in order:
+            q = calls[i][0]
+            at, cause[i] = free.get(q, (0.0, -1))
+            for j, waits in edges[i]:
+                x = done[j] + late[j] + wake if waits else done[j]
+                if x >= at:
+                    at, cause[i] = x, j
+            for k in banks[i]:
+                if k in held and held[k][1] != q and held[k][0] > at:
+                    at, cause[i] = held[k][0], held[k][2]
+            done[i] = at + time[i]
+            free[q] = (done[i], i)
+            if calls[i][7]:
+                if engines[0] > done[i]:
+                    cause[i] = engines[1]
+                engines = (max(engines[0], done[i]) + calls[i][7], i)
+                late[i] = engines[0] - done[i] + calls[i][5]
+            for k in banks[i]:
+                held[k] = (done[i] + wake, q, i)
+        cause[n] = max(order[-24:], key=lambda i: done[i] + late[i])
+        return done[cause[n]] + late[cause[n]]
+
+    cause = [-1] * (n + 1)
+
+    def sweep(forward, rank, times):
+        pre, post = (before, after) if forward else (after, before)
+        done, busy, left, placed = [0.0] * n, {}, [len(x) for x in pre], []
+        ready = {i: 0.0 if forward else late[i] for i in range(n) if not left[i]}
+        while ready:
+            i = max(ready, key=lambda k: (rank[k], -k))
+            at, time, moved = ready.pop(i), times[i], True
+            rooms = [busy.setdefault(k, []) for k in banks[i] + [calls[i][0]]]
+            while moved:
+                moved = False
+                for room in rooms:
+                    k = len(room)
+                    while k and room[k - 1][1] > at:
+                        k -= 1
+                    while k < len(room) and room[k][0] < at + time:
+                        at, moved, k = room[k][1], True, k + 1
+            done[i] = at + time
+            for room in rooms:
+                k = len(room)
+                while k and room[k - 1][0] > at:
+                    k -= 1
+                room.insert(k, (at, done[i]))
+            placed.append((at, len(placed), i))
+            for k in post[i]:
+                left[k] -= 1
+                if not left[k]:
+                    ready[k] = max(done[j] + (gap(j, k) if forward else gap(k, j)) for j in pre[k])
+        return [i for at, k, i in sorted(placed)], done
+
+    share = [w / sum(x) for w, x in zip(WEIGHT, times)]
+
+    def worth(order):
+        return sum(share[case] * replay(order, times[case]) for case in reversed(range(len(times))))
+
+    best, seed = None, SEED
+    for k in range(PASSES):
+        for _ in range(2):
+            order, done = sweep(True, way, times[CASES[k % len(CASES)]])
+            span = worth(order)
+            way = sweep(False, done, times[CASES[k % len(CASES)]])[1]
+            if best is None or span < best[0]:
+                best = (span, order, way)
+        way, lo = [], max(best[2]) * (k * 0.382 % 1.0)
+        for x in best[2]:
+            seed = (seed * 1103515245 + 12345) % 2 ** 31
+            way.append(x + SHAKE * (seed / 2 ** 31 - 0.5) * (abs(x - lo) < REACH))
+
+    def chain(order, case):
+        span, pairs, i = share[case] * replay(order, times[case]), [], cause[n]
+        while cause[i] >= 0:
+            if cause[i] not in before[i]:
+                pairs.append((cause[i], i))
+            i = cause[i]
+        return span, pairs
+
+    cases = range(len(times))
+    now = best
+    chains = [chain(now[1], case) for case in cases]
+    for k in range(SWAPS):
+        order, case, slack = now[1], k % len(times), SLACK * (1.0 - k / SWAPS)
+        pairs = chains[case][1]
+        seed = (seed * 1103515245 + 12345) % 2 ** 31
+        j, i = pairs[(seed >> 8) % len(pairs)]
+        a, z = order.index(j), order.index(i)
+        between, ahead = order[a:z + 1], {i}
+        for x in reversed(between):
+            if x in ahead:
+                ahead |= before[x]
+        if j in ahead:
+            continue
+        order = order[:a] + [x for x in between if x in ahead] + [x for x in between if x not in ahead] + order[z + 1:]
+        first = chain(order, case)
+        if first[0] > chains[case][0] + slack:
+            continue
+        tried = [first if x == case else chain(order, x) for x in cases]
+        span = sum(x[0] for x in tried)
+        if span < now[0] + slack:
+            now, chains = (span, order), tried
+            if span < best[0]:
+                best = now
+    return best[1]
+
+
 def rank_main(g, core, rank, cores, T, topo):
     Q = {"v": g.vector, "s": g.scalar, "t": g.tensor, "g": g, "y": g.sync}
     SEMOF = {"v": "kv", "s": "ks", "t": "kt", "g": "kg"}
-    count = {}
+    count = {"ls": 0}
     waited = {q: {} for q in Q}
     hist = {}
-    nd = [0]
+    nd = [0, 0]
+    calls = []
     apart = [False]
 
-    def need(q, name, lo, hi, write, toks):
+    def need(q, name, lo, hi, write, toks, loose):
         ps = name.startswith("ps")
         for (l, h, wr, sem, val, qq) in hist.get(name, []):
             if qq == q and qq in SEMOF:
-                if not (l < hi and lo < h) or not wr or (ps and q == "t") or (write and apart[0]):
+                if not (l < hi and lo < h) or not wr or (ps and q == "t") or (write and loose):
                     continue
             elif ps:
                 if l // 512 > (hi - 1) // 512 or lo // 512 > (h - 1) // 512:
                     continue
-            elif not (l < hi and lo < h) or not (wr or write) or (write and wr and apart[0]):
+            elif not (l < hi and lo < h) or not (wr or write) or (write and wr and loose):
                 continue
             if toks.get(sem, 0) < val:
                 toks[sem] = val
 
-    def note(name, lo, hi, write, sem, val, q):
+    def note(x, write, sem, val, q, loose=False):
+        name, lo, hi = x[1:4]
         L = hist.get(name, [])
         if write:
-            L = [e for e in L if not (lo <= e[0] and e[1] <= hi and (e[5] == q or not apart[0]))]
+            L = [e for e in L if not (lo <= e[0] and e[1] <= hi and (e[5] == q or not loose))]
         else:
             L = [e for e in L if not (not e[2] and e[5] == q and q in SEMOF and lo <= e[0] and e[1] <= hi)]
         L.append((lo, hi, write, sem, val, q))
         hist[name] = L
 
-    def waits(q, reads, writes):
+    def waits(q, reads, writes, loose=False):
         toks = {}
         for x in reads:
-            need(q, x[1], x[2], x[3], False, toks)
+            need(q, x[1], x[2], x[3], False, toks, loose)
         for x in writes:
-            need(q, x[1], x[2], x[3], True, toks)
+            need(q, x[1], x[2], x[3], True, toks, loose)
         for sem, val in toks.items():
             if waited[q].get(sem, 0) < val:
                 Q[q].wait_ge(T.sem[sem], val)
                 waited[q][sem] = val
 
     def b(name, lo, hi, step=1, rows=None):
+        if name in TILE:
+            name, lo, hi = "psT", lo + BLK * TILE.index(name), hi + BLK * TILE.index(name)
         cols = slice(lo, hi, step) if step != 1 else slice(lo, hi)
-        return (T[name][:, cols] if rows is None else T[name][0:rows, cols], name, lo, hi)
+        return (T[name][:, cols] if rows is None else T[name][0:rows, cols], name, lo, hi, (hi - lo + step - 1) // step)
 
     def ap(x):
         return x[0] if isinstance(x, tuple) else x
 
-    def emit(q, fn, reads, writes):
+    def emit(q, fn, reads, writes, time, joined=False):
         reads = [x for x in reads if isinstance(x, tuple)]
-        waits(q, reads, writes)
-        sem = SEMOF[q]
-        count[sem] = count.get(sem, 0) + 1
-        fn().then_inc(T.sem[sem], 1)
-        for x in reads:
-            note(x[1], x[2], x[3], False, sem, count[sem], q)
-        for x in writes:
-            note(x[1], x[2], x[3], True, sem, count[sem], q)
+        loose = apart[0]
 
-    def dma(q, pairs):
+        def issue():
+            waits(q, reads, writes, loose)
+            sem = SEMOF[q]
+            count[sem] = count.get(sem, 0) + 1
+            fn().then_inc(T.sem[sem], 1)
+            for x in reads:
+                note(x, False, sem, count[sem], q)
+            for x in writes:
+                note(x, True, sem, count[sem], q, loose)
+
+        if joined:
+            c = calls[-1]
+            assert c[0] == q
+            c[1].append(issue)
+            c[2:5] = [c[2] + reads, c[3] + writes, c[4] + CALL[q] + time]
+        else:
+            calls.append([q, [issue], reads, writes, CALL[q] + time, 0.0, loose, 0.0])
+
+    def dma(q, pairs, busy):
         sem = "d%d" % nd[0]
         nd[0] += 1
-        n = 16 * len(pairs)
-        waits(q, [p[1] for p in pairs if isinstance(p[1], tuple)], [p[0] for p in pairs if isinstance(p[0], tuple)])
-        for o, i in pairs:
-            Q[q].dma_start(ap(o), ap(i)).then_inc(T.sem[sem], 16)
-        for o, i in pairs:
-            if isinstance(i, tuple):
-                note(i[1], i[2], i[3], False, sem, n, q + "dma")
-        for o, i in pairs:
-            if isinstance(o, tuple):
-                note(o[1], o[2], o[3], True, sem, n, q + "dma")
-        count[sem] = n
+        reads, writes = [i for o, i in pairs if isinstance(i, tuple)], [o for o, i in pairs if isinstance(o, tuple)]
+
+        def issue():
+            waits(q, reads, writes)
+            count[sem] = 16 * len(pairs)
+            for o, i in pairs:
+                Q[q].dma_start(ap(o), ap(i)).then_inc(T.sem[sem], 16)
+            for x in reads:
+                note(x, False, sem, count[sem], q + "dma")
+            for x in writes:
+                note(x, True, sem, count[sem], q + "dma")
+
+        calls.append([q, [issue], reads, writes, 1.0 if q == "g" else CALL[q], 1.7, False, busy])
+
+    def remote(issue, reads, writes, late, busy):
+        calls.append(["g", [issue], reads, writes, 0.3 if nd[1] else 2.3, late, False, busy])
+        nd[1] += 1
+
+    def narrow(*xs):
+        return 0.5 if all(SCRATCH[x[1]][2] in (_B, _U) for x in xs) else 1.0
+
+    def cycles(k):
+        return max(k, 64) * CYCLE
 
     def tt(o, x, y, op):
-        emit("v", lambda: g.vector.tensor_tensor(o[0], x[0], y[0], op), [x, y], [o])
+        emit("v", lambda: g.vector.tensor_tensor(o[0], x[0], y[0], op), [x, y], [o], cycles(o[4] * (1 if "ps" in (x[1][:2], y[1][:2]) else 2)))
 
     def ts(o, x, s1, op0, s2=None, op1=None):
         if op1 is None:
-            emit("v", lambda: g.vector.tensor_scalar(o[0], x[0], ap(s1), None, op0), [x, s1], [o])
+            emit("v", lambda: g.vector.tensor_scalar(o[0], x[0], ap(s1), None, op0), [x, s1], [o], cycles(o[4] * narrow(o, x)))
         else:
-            emit("v", lambda: g.vector.tensor_scalar(o[0], x[0], ap(s1), ap(s2), op0, op1), [x, s1, s2], [o])
+            emit("v", lambda: g.vector.tensor_scalar(o[0], x[0], ap(s1), ap(s2), op0, op1), [x, s1, s2], [o], cycles(o[4] * narrow(o, x)))
 
     def cp(o, x):
-        emit("v", lambda: g.vector.tensor_copy(o[0], x[0]), [x], [o])
+        emit("v", lambda: g.vector.tensor_copy(o[0], x[0]), [x], [o], cycles(o[4] * narrow(o, x)))
 
-    def ms(o, c):
-        emit("v", lambda: g.vector.memset(o[0], c), [], [o])
+    def ms(o, c, behind=()):
+        emit("v", lambda: g.vector.memset(o[0], c), list(behind), [o], cycles(o[4] * narrow(o)))
 
     def red(o, x):
-        emit("v", lambda: g.vector.tensor_reduce(o[0], x[0], AxisListType.X, OP.add), [x], [o])
+        emit("v", lambda: g.vector.tensor_reduce(o[0], x[0], AxisListType.X, OP.add), [x], [o], cycles(x[4]))
 
     def scan(o, d0, d1, op0, op1):
-        emit("v", lambda: g.vector.tensor_tensor_scan(o[0], d0[0], d1[0], 0.0, op0, op1), [d0, d1], [o])
+        emit("v", lambda: g.vector.tensor_tensor_scan(o[0], d0[0], d1[0], 0.0, op0, op1), [d0, d1], [o], cycles(o[4] * narrow(o, d0, d1)))
 
     def act(o, x, func, bias=0.0, scale=1.0):
-        emit("s", lambda: g.scalar.activation(o[0], x[0], func, bias=bias, scale=ap(scale)), [x, scale], [o])
+        emit("s", lambda: g.scalar.activation(o[0], x[0], func, bias=bias, scale=ap(scale)), [x, scale], [o], o[4] * CYCLE)
 
     def total(o, x, scale):
         j = b("jk", 0, 128)
-        emit("s", lambda: g.scalar.activation(j[0], x[0], AF.Copy, scale=scale, accum_out=o[0]), [x], [j, o])
+        emit("s", lambda: g.scalar.activation(j[0], x[0], AF.Copy, scale=scale, accum_out=o[0]), [x], [j, o], x[4] * CYCLE)
 
-    def mm(o, l, r, start, stop):
-        emit("t", lambda: g.tensor.matmul(o[0], l[0], r[0], start, stop), [l, r], [o])
+    def mm(o, l, r, start, stop, joined=False):
+        emit("t", lambda: g.tensor.matmul(o[0], l[0], r[0], start, stop), [l, r], [o],
+             max(64, r[4]) * COLUMN * (4 if SCRATCH[l[1]][2] == _F else 1), joined or not start)
 
     def asel(o, i, pattern, op, base, cm, fill=0.0):
-        emit("g", lambda: g.affine_select(o[0], i[0], pattern, op, fill, base, cm), [i], [o])
+        emit("g", lambda: g.affine_select(o[0], i[0], pattern, op, fill, base, cm), [i], [o], 2 * o[4] * CYCLE)
 
     def iota(o, pattern, base, cm, flag=True):
         if flag:
-            emit("g", lambda: g.iota(o[0], pattern, base, cm, allow_small_or_imprecise_dtypes=True), [], [o])
+            emit("g", lambda: g.iota(o[0], pattern, base, cm, allow_small_or_imprecise_dtypes=True), [], [o], 2 * o[4] * CYCLE)
         else:
-            emit("g", lambda: g.iota(o[0], pattern, base, cm), [], [o])
+            emit("g", lambda: g.iota(o[0], pattern, base, cm), [], [o], 2 * o[4] * CYCLE)
 
     def gath(q, o, win, off):
         if q == "s":
-            emit("s", lambda: g.scalar.activation(o[0], win[0].indirect(off[0]), AF.Copy), [win, off], [o])
+            emit("s", lambda: g.scalar.activation(o[0], win[0].indirect(off[0]), AF.Copy), [win, off], [o], o[4] * GATHER * CYCLE)
         else:
-            emit("v", lambda: g.vector.tensor_copy(o[0], win[0].indirect(off[0])), [win, off], [o])
+            emit("v", lambda: g.vector.tensor_copy(o[0], win[0].indirect(off[0])), [win, off], [o], o[4] * GATHER * CYCLE)
 
     for kind, sbuf, lo, hi, off, land, which in MSG:
         src = cores[(rank - off) % NR]
         rel = relay_of(src, core, which, T, topo)
         far = src if rel is None else rel
         count["m_" + kind] = popcount(mask_for(far, core, far, core, topo))
-        note(land, 0, hi - lo, True, "m_" + kind, count["m_" + kind], "net")
+        note(b(land, 0, hi - lo), True, "m_" + kind, count["m_" + kind], "net")
 
     def send(kind):
-        for k, sbuf, lo, hi, off, land, which in MSG:
-            if k == kind:
-                dst = cores[(rank + off) % NR]
-                rel = relay_of(core, dst, which, T, topo)
-                src = b(sbuf, lo, hi)
-                waits("g", [src], [])
-                if rel is None:
-                    m, to, out, sem = mask_for(core, dst, core, dst, topo), dst, T[land][:], "m_" + kind
-                else:
-                    m, to, out, sem = mask_for(core, rel, rel, dst, topo), rel, T["y_" + kind][:], "q_" + kind
-                rid, pid = topo.addr(to, core)
-                g.remote_dma(out, src[0], T.sem[sem], T.sem.ls, pid, rid, m)
-                count["ls"] = count.get("ls", 0) + popcount(m)
+        k, sbuf, lo, hi, off, land, which = [m for m in MSG if m[0] == kind][0]
+        dst = cores[(rank + off) % NR]
+        rel = relay_of(core, dst, which, T, topo)
+        src = b(sbuf, lo, hi)
+
+        def issue():
+            waits("g", [src], [])
+            if rel is None:
+                m, to, out, sem = mask_for(core, dst, core, dst, topo), dst, T[land][:], "m_" + kind
+            else:
+                m, to, out, sem = mask_for(core, rel, rel, dst, topo), rel, T["y_" + kind][:], "q_" + kind
+            rid, pid = topo.addr(to, core)
+            g.remote_dma(out, src[0], T.sem[sem], T.sem.ls, pid, rid, m)
+            count["ls"] += popcount(m)
+
+        remote(issue, [src], [b(land, 0, hi - lo)], FIRST if kind[0] == "i" else 5.5, 0.8)
+
+    helper, sweeper = helpers_of(core, cores, T, topo)
+    hrid, hpid = topo.addr(helper, core)
+    aides = [DstId(rid=topo.addr(x, core)[0], pnc=topo.addr(x, core)[1]) for x in (helper, sweeper)]
+    there, back = topo.mask(core, helper), topo.mask(helper, core)
 
     zero, one, one32 = b("zero", 0, 128), b("one", 0, 128), b("one32", 0, 128)
     ident, nident, id15, n2id = b("ident", 0, 128), b("nident", 0, 128), b("id15", 0, 128), b("n2id", 0, 128)
-    dma("y", [(b("wt", 0, 256), T.w0[:])])
-    dma("s", [(b("z0s", 0, 512), T.z0[:])])
+    dma("y", [(b("wt", 0, 256), T.w0[:])], 0.5)
+    dma("s", [(b("lmI", 0, 256), T.lm[:, 0:256])], 0.7)
     for k in range(4):
-        dma("y", [(b("ptb", 16 + 1024 * k, 1040 + 1024 * k), T.pt[:, 1024 * k:1024 * k + 1024])])
-    dma("y", [(b("lmI", 0, 1024), T.lm[:])])
+        dma("y", [(b("ptb", 16 + 1024 * k, 1040 + 1024 * k), T.pt[:, 1024 * k:1024 * k + 1024])], 1.05)
+    dma("y", [(b("z0s", 0, 512), T.z0[:])], 0.7)
+    dma("y", [(b("lmI", 256, 1024), T.lm[:, 256:1024])], 1.4)
     iota(b("mI", 0, 16), [[-1, 16]], 16, 1, False)
     ms(zero, 0.0)
     ms(one32, 1.0)
@@ -288,347 +488,328 @@ def rank_main(g, core, rank, cores, T, topo):
     ms(b("ptb", 0, 16), 0.0)
     ms(b("m128", 0, 272), -128.0)
     ms(b("woff", 0, 8), 128.0)
+    ms(b("cst", 128, 384), 128.0)
+    ms(one, 1.0)
+    ms(b("a16", 0, 8), 0.0)
+    for k in range(FILLS):
+        iota(b("big", BLK * k, BLK * k + BLK), [[0, BLK]], 0, 0)
+    for k in range(FILLS, 8, 2):
+        ms(b("big", BLK * k, BLK * min(k + 2, 8)), 0.0, [b("mF", 0, 16), b("pat", 0, 256), zero])
 
     asel(ident, zero, [[-1, 128]], OP.not_equal, 0, 1, 1.0)
     asel(nident, zero, [[-1, 128]], OP.not_equal, 0, 1, -1.0)
     asel(b("lt32", 0, 128), one32, [[-16, 8], [0, 16]], OP.is_ge, 0, 1)
     asel(b("bo32", 0, 128), b("lt32", 0, 128), [[16, 8], [0, 16]], OP.is_ge, 15, -1)
     asel(b("lt32", 0, 128), b("bo32", 0, 128), [[1, 128]], OP.is_ge, -1, -1)
-    send("i01")
-    kl = b("kl", 0, 384)
-    iota(kl, [[80, 3], [0, 8], [5, 16]], 17, 0)
-    asel(kl, kl, [[0, 3], [-16, 8], [0, 16]], OP.is_ge, 0, 1)
-    asel(kl, kl, [[0, 3], [16, 8], [0, 16]], OP.is_ge, 15, -1)
-    iota(b("lane", 0, 128), [[1, 128]], 0, 0)
-    send("i2")
-    send("i3")
-    iota(b("zeros", 0, 2048), [[0, 2048]], 0, 0)
-    helper = helper_of(core, cores, T, topo)
-    waits("g", [b("zeros", 0, 2048)], [])
-    g.remote_dma(T.zeros[:], T.zeros[:], T.sem.hz, T.sem.ls, topo.addr(helper, core)[1], topo.addr(helper, core)[0], topo.mask(core, helper))
-    count["ls"] += popcount(topo.mask(core, helper))
-    asel(b("ind", 0, 2048), b("zeros", 0, 2048), [[-1, 128], [0, 16]], OP.not_equal, 0, 1, -15.0)
+    for kind in ("i01", "i2", "i3"):
+        send(kind)
+    kl = b("kl", 0, 768)
+    iota(kl, [[40, 6], [0, 16], [5, 8]], 17, 0)
+    asel(kl, kl, [[0, 6], [-16, 8], [0, 16]], OP.is_ge, 0, 1)
+    asel(kl, kl, [[0, 6], [16, 8], [0, 16]], OP.is_ge, 15, -1)
+    asel(b("kl", 768, 1536), kl, [[0, 48], [1, 16]], OP.is_ge, -8, 0)
+    asel(kl, kl, [[0, 48], [-1, 16]], OP.is_ge, 7, 0)
+    iota(b("cst", 0, 128), [[0, 8], [976, 2], [0, 8]], 0, 0)
+    asel(b("cst", 0, 128), b("cst", 0, 128), [[0, 128]], OP.not_equal, 0, 1, 1952.0)
+    iota(b("lane", 0, 64), [[1, 64]], 0, 0)
+    asel(b("lane", 0, 64), b("lane", 0, 64), [[0, 64]], OP.not_equal, -1, 1, 1.0)
+    iota(b("zeros", 0, BLK), [[0, BLK]], 0, 0)
+
+    def lend_zeros():
+        waits("g", [b("zeros", 0, BLK)], [])
+        g.remote_dma_fused([RemoteDMATransfer(dst_ids=aides, dma_engine_mask=there, remote_sem=T.sem.hz, srcs=[T.zeros[:]],
+                                              dsts=[T.zeros[:], T.zeros[:]])], local_sem=T.sem.ls)
+        count["ls"] += popcount(there)
+
+    lent = (None, "lent", 0, 1)
+    swept = (None, "swept", 0, 1)
+    remote(lend_zeros, [b("zeros", 0, BLK)], [swept], 8.0, 2.0)
+
+    def in_turn():
+        calls.append(["-", [], [], [lent], 0.0, 0.0, False, 0.0])
+
+    asel(b("ind", 0, BLK), b("zeros", 0, BLK), [[-1, 128], [0, 8]], OP.not_equal, 0, 1, -15.0)
     asel(id15, zero, [[-1, 128]], OP.not_equal, 0, 1, 15.0)
     asel(b("rs8", 0, 8), b("zero", 0, 8), [[-16, 8]], OP.not_equal, 0, 1, 1.0)
+    iota(b("zh", 0, 256), [[0, 256]], 0, 0)
+    iota(b("mkx", 0, BLK), [[0, 128], [1024, 8]], -512, 0)
+    iota(b("mkn", 0, BLK), [[0, 128], [-1024, 8]], 512, 0)
+    asel(b("p2id", 0, 128), zero, [[-1, 128]], OP.not_equal, 0, 1, 2.0)
+    iota(b("amk", 0, 384), [[0, 8], [16, 48]], 0, 0)
+    asel(n2id, zero, [[-1, 128]], OP.not_equal, 0, 1, -2.0)
+    for lo in range(8):
+        asel(b("crep", 0, 128), zero if lo == 0 else b("crep", 0, 128), [[0, 8], [-8, 16]], OP.not_equal, -lo, 1, 2.0 ** (lo - 14))
+    asel(b("em", 0, 512), b("zeros", 0, 512), [[-8, 4], [-1, 8], [0, 16]], OP.not_equal, 0, 1, 1.0)
+    asel(b("sgn", 0, 1), b("one32", 0, 1), [[0, 1]], OP.is_ge, 15, -1, -1.0)
 
-    iota(b("zh", 0, 128), [[0, 128]], 0, 0)
-    iota(b("mkx", 0, 2048), [[0, 128], [1024, 16]], -512, 0)
-
-    def late_constants():
-        iota(b("mkn", 0, 2048), [[0, 128], [-1024, 16]], 512, 0)
-        asel(b("p2id", 0, 128), zero, [[-1, 128]], OP.not_equal, 0, 1, 2.0)
-        iota(b("amk", 0, 384), [[0, 8], [16, 48]], 0, 0)
-        asel(n2id, zero, [[-1, 128]], OP.not_equal, 0, 1, -2.0)
-        for lo in range(8):
-            asel(b("crep", 0, 128), zero if lo == 0 else b("crep", 0, 128), [[0, 8], [-8, 16]], OP.not_equal, -lo, 1, 2.0 ** (lo - 14))
-        asel(b("em", 0, 512), b("zeros", 0, 512), [[-8, 4], [-1, 8], [0, 16]], OP.not_equal, 0, 1, 1.0)
-        asel(b("sgn", 0, 1), b("one32", 0, 1), [[0, 1]], OP.is_ge, 15, -1, -1.0)
-        asel(b("w1", 256, 258), b("zero", 0, 2), [[1, 2]], OP.not_equal, 0, 0, -448.0)
-        asel(b("w1", 256, 258), b("w1", 256, 258), [[1, 2]], OP.not_equal, -1, 0, -1.0 / 32.0)
+    ts(b("aF", 2, 3), b("mI", 0, 1), 2.0, OP.mult, 1.0, OP.add)
+    act(b("bok", 0, 128), b("bo32", 0, 128), AF.Copy, 0.0, 1024.0)
+    cp(b("bi8", 0, 8), b("bo32", 0, 128, 16))
+    for c in range(4):
+        cp(b("lm16", 256 * c, 256 * c + 256), b("lmI", 256 * c, 256 * c + 256))
+    ts(b("woff", 8, 264), b("wt", 0, 256), 128.0, OP.add)
 
     for a in range(16):
         act(b("vals", 256 * a, 256 * a + 256), b("pat", 0, 256), AF.Copy, 0.0, b("mF", a, a + 1))
-    ms(b("big", 0, 8192), 0.0)
-    ts(b("woff", 8, 264), b("wt", 0, 256), 128.0, OP.add)
+    SLOT = (0, 4096, 8192, 4096)
 
-    def prefix_scan():
+    def narrowed(c):
+        dma("g", [(b("rr", SLOT[c], SLOT[c] + 4096), b("rf", 4096 * (c % 2), 4096 * (c % 2) + 4096))], 3.5)
+
+    for c in range(4):
+        for lo, hi in zip(CUTS[c], CUTS[c][1:]):
+            w, v = b("rf", 4096 * (c % 2), 4096 * (c % 2) + 4096), b("vals", 512 * lo, 512 * hi)
+            off = b("lm16", 256 * c + 32 * lo, 256 * c + 32 * hi)
+            if (c, lo) in TAKEN:
+                emit("v", lambda w=w, v=v, off=off: g.vector.tensor_copy(w[0].indirect(off[0]), v[0]), [v, off], [w], v[4] * SCATTER * CYCLE)
+            else:
+                emit("s", lambda w=w, v=v, off=off: g.scalar.activation(w[0].indirect(off[0]), v[0], AF.Silu), [v, off],
+                     [w, (None, "class after class", 0, 1)], v[4] * SCATTER * CYCLE)
+        if c < 3:
+            narrowed(c)
+
+    def prefix():
         scan(b("ex", 0, 257), b("m128", 0, 257), b("woff", 7, 264), OP.add, OP.add)
-
-    def prefix_sums():
         mm(b("psC0", 401, 402), b("lt32", 0, 128), b("ex", 256, 257), True, True)
         mm(b("psC0", 402, 403), b("bo32", 0, 128), b("ex", 256, 257), True, True)
-
-    def prefix_end():
         ts(b("off16", 0, 256), b("ex", 0, 256), b("psC0", 401, 402), OP.add)
+        act(b("smv", 5, 6), b("ex", 256, 257), AF.Copy, -7168.5 / 16.0)
+        x = b("thf", 1, 2)
+        act(x, b("psC0", 402, 403), AF.Copy, -0.25, 0.5)
+        act(x, x, AF.Copy, ROUND)
+        act(x, x, AF.Relu, ROUND + 4096.0, -1.0)
+        act(b("thf", 0, 1), x, AF.Copy, 2.0, -1.0 / 2048.0)
 
-    prefix_scan()
-    prefix_sums()
-    prefix_end()
     banks = (("psB", 0), ("psB", 512), ("psD", 0), ("psD", 512), ("psA", 0), ("psA", 512))
-    apart[0] = True
     for a in range(16):
         p = b(banks[a % 6][0], banks[a % 6][1], banks[a % 6][1] + 256)
         mm(p, ident, b("ptb", 16 + 256 * a, 272 + 256 * a), True, False)
         mm(p, nident, b("ptb", 15 + 256 * a, 271 + 256 * a), False, True)
-        if a % 8 < 5:
-            ts(b("diffp", a, 4096, 16), p, 0.5, OP.mult)
-        else:
+        apart[0] = True
+        if a < SHARE:
             act(b("diffp", a, 4096, 16), p, AF.Copy, 0.0, 0.5)
-        if a == 9:
-            cp(b("lm16", 0, 256), b("lmI", 0, 256))
-    apart[0] = False
-
-    def rest_of_setup():
-        cp(b("lm16", 256, 1024), b("lmI", 256, 1024))
-        ts(b("aF", 2, 3), b("mI", 0, 1), 2.0, OP.mult, 1.0, OP.add)
-        ms(b("cst", 0, 128), 976.0)
-        ms(b("cst", 128, 384), 128.0)
-        ms(one, 1.0)
-        ms(b("a16", 0, 8), 0.0)
-        cp(b("bi8", 0, 8), b("bo32", 0, 128, 16))
-
-    def inverse(c, k):
-        w, v, off = b("rf", 0, 4096), b("vals", 512 * k, 512 * k + 512), b("lm16", 256 * c + 32 * k, 256 * c + 32 * k + 32)
-        emit("s", lambda: g.scalar.activation(w[0].indirect(off[0]), v[0], AF.Silu), [v, off], [w])
-        if k == 7:
-            dma("g", [(b("rr", 4096 * c, 4096 * c + 4096), w)])
+        else:
+            ts(b("diffp", a, 4096, 16), p, 0.5, OP.mult)
+        apart[0] = False
 
     ZSRC = [(("zin0", 0), ("zin0", 128)), (("zr1", 0), ("zin1", 0)), (("zr2", 0), ("zin2", 0)), (("zr3", 0), ("zc0", 0))]
-    TILE = ("psA", "psB", "psD")
-    pieces = [0]
 
-    def round_steps(t):
+    def one_round(t):
         cc = (t % 4, (t + 1) % 4)
         zz = [b(n, lo, lo + 128) for n, lo in ZSRC[t]]
+        prefix()
+
+        for lo in range(0, 256, 256 // PIECES):
+            hi = lo + 256 // PIECES
+            bigw, offs, dif = b("big", 0, 32768), b("off16", lo, hi), b("diffp", 16 * lo, 16 * hi)
+            emit("v", lambda offs=offs, dif=dif: g.vector.tensor_copy(bigw[0].indirect(offs[0]), dif[0]), [dif, offs], [bigw],
+                 dif[4] * SCATTER * CYCLE)
+        scan(b("pE", 0, 8192), b("big", 0, 8192), b("big", 0, 8192), OP.add, OP.add)
+
+        def clear():
+            waits("g", [], [b("big", 0, 8192)])
+            g.remote_dma_fused([RemoteDMATransfer(dst_ids=[aides[k]], dma_engine_mask=1 << topo.engines(core, helper)[k],
+                                                  remote_sem=T.sem["hz%d" % t]) for k in range(2)], local_sem=T.sem.ls)
+            count["ls"] += 2
+            count["bz%d" % t] = popcount(back) + popcount(topo.mask(sweeper, core))
+            note(b("big", 0, 8192), True, "bz%d" % t, count["bz%d" % t], "net")
+
+        if t < ROUNDS - 1:
+            in_turn()
+            remote(clear, [swept, lent], [b("big", 0, 8192)], 11.0, 0.0)
+
         wrow = b("ptb", 16, 4112)
-        tile, free, tail = {}, list(TILE), []
-
-        def row():
-            dma("y", [((T.ptb[0::16, 16:4112], "ptb", 16, 4112), b("woff", 8, 264))])
-
-        def scatter(h):
-            if h == 0:
-                ts(b("smi", 0, 1), b("psC0", 402, 403), 0.5, OP.mult, -0.25, OP.add)
-            bigw, offs, dif = b("big", 0, 32768), b("off16", 128 * h, 128 * h + 128), b("diffp", 2048 * h, 2048 * h + 2048)
-            emit("v", lambda: g.vector.tensor_copy(bigw[0].indirect(offs[0]), dif[0]), [dif, offs], [bigw])
-
-        def members(q, m, k):
-            gath(q, b("wg%d" % m, BLK * k, BLK * k + BLK), wrow, b("lm16", 256 * cc[m] + 64 * k, 256 * cc[m] + 64 * k + 64))
-
-        def sums(m):
+        dma("y", [((T.ptb[0::16, 16:4112], "ptb", 16, 4112), b("woff", 8, 264))], 0.6)
+        act(b("wf", 0, 256), b("woff", 8, 264), AF.Copy, -128.0)
+        act(b("w2", 0, 256), b("woff", 8, 264), AF.Abs, -132.0)
+        act(b("w2", 0, 256), b("w2", 0, 256), AF.Copy, 4.0, -1.0)
+        for m in range(2):
+            for k in range(4):
+                gath(MEMBERS[t][4 * m + k], b("wg%d" % m, BLK * k, BLK * k + BLK), wrow, b("lm16", 256 * cc[m] + 64 * k, 256 * cc[m] + 64 * k + 64))
             for i in range(32):
                 mm(b("psC%d" % m, 384, 392), b("wg%d" % m, i, 4096, 32), b("rs8", 0, 8), i == 0, i == 31)
 
-        def centres():
-            act(b("zf32", 0, 128), zz[0], AF.Copy)
-            for k2 in range(3):
-                p = b("psA", 128 * k2, 128 * k2 + 128)
-                mm(p, b("kl", 128 * k2, 128 * k2 + 128), b("zf32", 0, 128), True, False)
-                mm(p, b("cst", 0, 128, 1, 1), b("lane", 0, 128, 1, 1), False, True)
-            mm(b("psB", 0, 128), zz[0], ident, True, True)
-            act(b("zh", 0, 64), b(ZSRC[t][0][0], ZSRC[t][0][1], ZSRC[t][0][1] + 64), AF.Copy)
-            mm(b("psB", 128, 256), zz[1], ident, True, False)
-            mm(b("psB", 128, 256), b("zh", 0, 128), nident, False, True)
-
-        def centres_end():
-            act(b("zT", 0, 256), b("psB", 0, 256), AF.Copy)
-            for h in range(2):
-                mm(b("psD", 512 * h, 512 * h + 512), b("zT", 0, 128), b("ind", 512 * h, 512 * h + 512), True, True)
-            act(b("wf", 0, 256), b("woff", 8, 264), AF.Copy, -128.0)
-
-        def repeated():
-            act(b("zrep", 0, 1024), b("psD", 0, 1024), AF.Copy, 0.0, -1.0 / 15.0)
-
-        def factors():
-            late_constants()
-            act(kl, kl, AF.Copy, 0.0, b("aF", 2, 3))
-            act(b("bok", 0, 128), b("bo32", 0, 128), AF.Copy, 0.0, 1024.0)
-
-        def next_inverse():
-            inverse(pieces[0] // 8, pieces[0] % 8)
-            pieces[0] += 1
-
-        def sequence():
-            ts(b("thf", 0, 1), b("smi", 0, 1), 4096.0, OP.min, 1.0 / 2048.0, OP.mult)
-            scan(b("pE", 0, 8192), b("big", 0, 8192), b("big", 0, 8192), OP.add, OP.add)
-            if t < ROUNDS - 1:
-                waits("g", [], [b("big", 0, 8192)])
-                rid, pid = topo.addr(helper, core)
-                g.remote_sem_update(T.sem["hz%d" % t], T.sem.ls, pid, rid, 1 << topo.engines(core, helper)[0])
-                count["ls"] += 1
-                count["bz%d" % t] = 4 * popcount(topo.mask(helper, core))
-                note("big", 0, 8192, True, "bz%d" % t, count["bz%d" % t], "net")
-
-        def places():
-            hI = b("hI", 0, 384)
-            ts(hI, b("psA", 0, 384), b("a16", 0, 1), OP.add)
+        act(b("zf32", 0, 128), zz[0], AF.Copy, 0.0, b("aF", 2, 3))
+        for bk in range(6):
+            at = 64 * bk + [x[2] for x in PARTS if x[0] <= 64 * bk][-1]
+            p = b("psA", at, at + 64)
+            mm(p, b("cst", 0, 128, 1, 2), b("lane", 0, 64, 1, 2), True, False)
+            for odd in range(2):
+                lo = 768 * odd + 128 * bk
+                mm(p, b("kl", lo, lo + 128), b("zf32", odd, 128, 2), False, odd == 1)
+        mm(b("psB", 0, 128), zz[0], ident, True, True)
+        zh, cut = zz[0], 8 * LANES[t]
+        if cut < BLK:
+            lo = 128 * (LANES[t] > 64)
+            zh = b("zh", lo, lo + 128)
+            act(b("zh", lo, lo + LANES[t]), b(ZSRC[t][0][0], ZSRC[t][0][1], ZSRC[t][0][1] + LANES[t]), AF.Copy)
+        mm(b("psB", 128, 256), zz[1], ident, True, False)
+        mm(b("psB", 128, 256), zh, nident, False, True)
+        act(b("zT", 0, 256), b("psB", 0, 256), AF.Copy)
+        for lo in range(0, cut, 512):
+            hi = min(cut, lo + 512)
+            mm(b("psD", lo, hi), b("zT", 0, 128), b("ind", lo, hi), True, True)
+        zrep = b("zrep", 0, cut)
+        act(zrep, b("psD", 0, cut), AF.Copy, 0.0, -1.0 / 15.0)
+        for lo, hi, at in PARTS:
+            hI = b("hI", lo, hi)
+            ts(hI, b("psA", lo + at, hi + at), b("a16", 0, 1), OP.add)
             ts(hI, hI, 4, OP.arith_shift_right, 4095, OP.bitwise_and)
             ts(hI, hI, b("thf", 0, 1), OP.mult, -4095.5 + 1.0 / 4096.0, OP.add)
-            ts(b("pos16", 0, 384), hI, 4095.0, OP.add)
+            ts(b("pos16", lo, hi), hI, 4095.0, OP.add)
 
-        def finished():
-            dma("y", [(T.yz[:, 128:256], b("zf1", 0, 128)), (T.yz[:, 256:384], b("zf2", 0, 128))])
-
-        def gather(bk):
-            o, win, off, zr = b("big", OP_ + bk * BLK, OP_ + bk * BLK + BLK), b("pE", 0, 8192), b("pos16", 64 * bk, 64 * bk + 64), b("zrep", 0, BLK)
-            if bk % 2:
-                gath("s", o, win, off)
-            else:
-                emit("v", lambda: g.vector.tensor_tensor(o[0], win[0].indirect(off[0]), zr[0], OP.subtract), [win, off, zr], [o])
-
-        def fill(bk, m):
-            tile[bk, m] = free.pop(0)
+        nets = [b("big", OP_ + bk * BLK, OP_ + bk * BLK + BLK) for bk in range(6)]
+        for bk in range(6):
+            at, win = nets[bk][2], b("pE", 0, 8192)
+            net, off = b("big", at, at + cut), b("pos16", 64 * bk, 64 * bk + cut // 16)
+            emit("v", lambda net=net, off=off: g.vector.tensor_tensor(net[0], win[0].indirect(off[0]), zrep[0], OP.subtract),
+                 [win, off, zrep], [net], cut * GATHER * CYCLE)
+            if cut < BLK:
+                gath("s", b("big", at + cut, at + BLK), win, b("pos16", 64 * bk + cut // 16, 64 * bk + 64))
+            ps = BLK * (bk % 3) if cut == BLK else 1536 * (bk % 2)
             for h in range(2):
-                p = b(tile[bk, m], 512 * h, 512 * h + 512)
-                rep = b("ind", BLK * (bk % 2) + 512 * h, BLK * (bk % 2) + 512 * h + 512)
-                mm(p, id15, b("big", OP_ + bk * BLK + 512 * h, OP_ + bk * BLK + 512 * h + 512), True, False)
-                mm(p, b("zT", 128 * m, 128 * m + 128), rep, False, True)
+                p = b("psT", ps + 512 * h, ps + 512 * h + 512)
+                mm(p, id15, b("big", at + 512 * h, at + 512 * h + 512), True, False)
+                mm(p, b("zT", 128, 256), b("ind", 512 * h, 512 * h + 512), False, True)
+            for m in range(2):
+                lo, how = (OI0, OI1)[m] + BLK * bk, TESTS[t][2 * bk + m]
+                near, p = b("big", lo, lo + BLK), b("psT", ps, ps + BLK)
+                both, over = how == "D", OI2 + BLK * (bk % 2)
+                if both:
+                    ts(near, net, -68.0, OP.is_ge)
+                    ts(b("big", over, over + BLK), net, 68.0, OP.is_gt, -1.0, OP.mult)
+                elif m == 0:
+                    act(b("big", lo, lo + cut), net, AF.Abs, 0.0, 15.0)
+                    near = b("big", lo, lo + cut)
+                    if cut < BLK:
+                        p, rest = b("psT", ps + BLK, ps + 2 * BLK - cut), b("big", lo + cut, lo + BLK)
+                        mm(p, id15, b("big", at + cut, at + BLK), True, False)
+                        mm(p, b("zT", 0, 128), b("ind", cut, BLK), False, True)
+                        if how == "T":
+                            ts(rest, p, BIG, OP.add, BIG, OP.is_equal)
+                        else:
+                            act(rest, p, AF.Abs)
+                            near = b("big", lo, lo + BLK)
+                    ts(near, near, 1024.0, OP.is_le)
+                elif how == "A":
+                    act(near, p, AF.Abs)
+                    ts(near, near, 1024.0, OP.is_le)
+                else:
+                    ts(near, p, BIG, OP.add, BIG, OP.is_equal)
+                for a in range(8):
+                    p = b("psC%d" % m, 8 * bk + a, 384, 48)
+                    mm(p, b("big", lo + a, lo + BLK, 8), b("bi8", 0, 8), True, not both, a > 0)
+                    if both:
+                        mm(p, b("big", over + a, over + BLK, 8), b("bi8", 0, 8), False, True)
+        tail = TILE
 
-        def ring(m, bk):
-            base = (OI0, OI1)[m] + BLK * (bk % 4)
-            return b("big", base, base + BLK)
+        ends, folded = [], nets[:FOLD[t]]
+        for part in range(2):
+            home = b(*landing(t, part))
 
-        def absolute(bk, m):
-            if (bk, m) in tile:
-                act(ring(m, bk), b(tile[bk, m], 0, 1024), AF.Abs)
-                free.append(tile[bk, m])
-            else:
-                act(ring(m, bk), b("big", OP_ + bk * BLK, OP_ + bk * BLK + BLK), AF.Abs, 0.0, 15.0)
-
-        def compare(bk, m):
-            ts(ring(m, bk), ring(m, bk), 1024.0, OP.is_le)
-
-        def test(bk, m):
-            ts(ring(m, bk), b(tile[bk, m], 0, 1024), BIG, OP.add, BIG, OP.is_equal)
-            free.append(tile[bk, m])
-
-        def counts(k2, m):
-            base = (OI0, OI1)[m] + 2048 * (k2 % 2)
-            for a in range(16):
-                mm(b("psC%d" % m, 16 * k2 + a, 384, 48), b("big", base + a, base + 2048, 16), b("bi8", 0, 8), True, True)
-
-        def fold():
-            thirds = [b("big", OP_ + 2048 * k2, OP_ + 2048 * k2 + 2048) for k2 in range(3)]
-            waits("g", thirds, [b("pE", 0, 4096)])
-            mask = topo.mask(core, helper)
-            rid, pid = topo.addr(helper, core)
-            for part in range(2):
-                at, name = 4096 * t + 2048 * part, "%d%d" % (t, part)
-                g.remote_dma_fused([RemoteDMATransfer(dst_ids=[DstId(rid=rid, pnc=pid)], dma_engine_mask=mask, remote_sem=T.sem["h" + name],
-                                                      srcs=[x[0] for x in thirds], dsts=[T.big[:, at:at + 2048]], alu_op=2 + part)],
+            def fold(part=part, home=home):
+                at, name = BLK * (2 * t + part), "%d%d" % (t, part)
+                waits("g", folded, [home])
+                g.remote_dma_fused([RemoteDMATransfer(dst_ids=[DstId(rid=hrid, pnc=hpid)], dma_engine_mask=there, remote_sem=T.sem["h" + name],
+                                                      srcs=[x[0] for x in folded], dsts=[T.big[:, at:at + BLK]], alu_op=2 + part)],
                                    local_sem=T.sem["lf%d" % t])
-                count["b" + name] = popcount(topo.mask(helper, core))
-                note("pE", 2048 * part, 2048 * part + 2048, True, "b" + name, count["b" + name], "net")
-            count["lf%d" % t] = 2 * popcount(mask)
-            note("big", OP_, OP_ + 6144, False, "lf%d" % t, count["lf%d" % t], "net")
+                count["b" + name] = popcount(back)
+                note(home, True, "b" + name, count["b" + name], "net")
+                count["lf%d" % t] = 2 * popcount(there)
+                note(b("big", OP_, OP_ + BLK * FOLD[t]), False, "lf%d" % t, count["lf%d" % t], "net")
 
-        def extremes(part):
-            d, o = b("pE", 2048 * part, 2048 * part + 2048), b("pE", 4096 + 2048 * part, 6144 + 2048 * part)
-            if part == 0:
-                scan(o, b("mkx", 0, 2048), d, OP.min, OP.max)
-            else:
-                scan(o, b("mkn", 0, 2048), d, OP.max, OP.min)
-
-        def best(m):
-            scan(b("am%d" % m, 0, 384), b("amk", 0, 384), b("psC%d" % m, 0, 384), OP.min, OP.max)
-
-        def words(m):
-            if m == 0:
-                tail.append(free.pop(0))
-                tail.extend(x for x in TILE if x != tail[0])
-            p = b(tail[0], 512 + 8 * m, 520 + 8 * m)
-            mm(p, b("crep", 0, 128), b("xs", 16 + 8 * m, 24 + 8 * m), True, True)
-            tt(b("bw", 8 * m, 8 * m + 8), p, b("bi8", 0, 8), OP.mult)
-
-        def marks(m):
-            lo = 768 * m
-            mm(b(tail[0], lo, lo + 256), b("one", 0, 128, 1, 1), b("cst", 128, 384, 1, 1), True, False)
-            for ch in range(32):
-                at = 4096 * cc[m] + 128 * ch
-                mm(b(tail[0], lo + ch, lo + 256, 32), b("rr", at, at + 128), b("bw", 8 * m, 8 * m + 8), False, ch == 31)
-
-        def rounded(m):
-            act(b("r%d" % m, 0, 256), b(tail[0], 768 * m, 768 * m + 256), AF.Copy, 2.0 ** -9)
-
-        def marked(m):
-            tt(b("mk", 256 * m, 256 * m + 256), b("r%d" % m, 0, 256), b(tail[0], 768 * m, 768 * m + 256), OP.is_gt)
-
-        def turn():
-            for h in range(2):
-                for m in range(2):
-                    mm(b(tail[0], 256 + 128 * h, 384 + 128 * h), b("mk", 256 * m + h, 256 * m + 256, 2), id15, m == 0, m == 1)
-
-        def double():
-            p = b(tail[0], 256, 512)
-            tt(p, p, b("w2", 0, 256), OP.min)
-            tt(b("w1", 0, 256), p, b("wf", 0, 256), OP.max)
-
-        def choices():
-            mm(b(tail[1], 0, 128, 1, 32), b("xs", 0, 32), ident, True, True)
-            act(b("xT", 0, 128, 1, 32), b(tail[1], 0, 128, 1, 32), AF.Copy, 0.0, b("sgn", 0, 1, 1, 32))
-
-        def spread():
-            xT = b("xT", 0, 128, 1, 32)
-            for m in range(2):
-                mm(b(tail[2], 128 * m, 128 * m + 128), b("em", 128 * m, 128 * m + 128, 1, 32), xT, True, True)
-            for k in range(4):
-                mm(b(tail[1], 128, 256), b("em", 128 * k, 128 * k + 128, 1, 32), xT, k == 0, k == 3)
-
-        def heavy():
-            total(b("a16", 0, 1), b(tail[1], 128, 256), 16.0)
-            act(b("yab", t, t + 1), b("a16", 0, 1), AF.Copy, 0.0, 0.0625)
-
-        def middle():
-            for m in range(2):
-                terms = ((n2id, zz[m]), (b("p2id", 0, 128), b("zh", 0, 128)), (ident, b("pE", 4111, 6144, 16)),
-                         (ident, b("pE", 6159, 8192, 16)))
-                for k, (l, x) in enumerate(terms):
-                    mm(b(tail[2], 512 + 128 * m, 640 + 128 * m), l, x, k == 0, k == 3)
-
-        def quarter():
-            ts(b("q01", 0, 256), b(tail[2], 512, 768), 0.25, OP.mult, -0.375, OP.add)
-
-        def move():
-            tt(b("e01", 0, 256), b("q01", 0, 256), b(tail[2], 0, 256), OP.mult)
-            for m in range(2):
-                mm(b(tail[1], 512 + 128 * m, 640 + 128 * m), ident, b("e01", 128 * m, 128 * m + 128), True, False)
-                mm(b(tail[1], 512 + 128 * m, 640 + 128 * m), ident, zz[m], False, True)
-
-        def hand_over():
-            act(b("zo%d" % t, 0, 256), b(tail[1], 512, 768), AF.Copy)
-            for kind in (("u0", "c0"), ("u1", "f1"), ("u2", "f2"), ("f3",))[t]:
-                send(kind)
+            in_turn()
+            remote(fold, folded + [lent], [home], 5.5, 0.8 * FOLD[t])
+            mask, keep, take = (b("mkx", 0, BLK), OP.min, OP.max) if part == 0 else (b("mkn", 0, BLK), OP.max, OP.min)
+            end = None
+            for k, x in enumerate(nets[FOLD[t]:] + [home]):
+                lo = BLK * (2 + 2 * k + part)
+                scan(b("pE", lo, lo + BLK), mask, x, keep, take)
+                if end:
+                    tt(b("mx", 128 * part, 128 * part + 128), end, b("pE", lo + 7, lo + BLK, 8), take)
+                end = b("mx", 128 * part, 128 * part + 128) if end else b("pE", lo + 7, lo + BLK, 8)
+            ends.append(end)
 
         m0, m1 = b("am0", 47, 384, 48), b("am1", 47, 384, 48)
+        ts(b("thr", 0, 8), b("psC0", 384, 392), 4143.5, OP.is_lt, 11.5, OP.mult)
+        ts(b("thr", 16, 24), b("psC1", 384, 392), 4143.5, OP.is_lt)
+        for m in range(2):
+            scan(b("am%d" % m, 0, 384), b("amk", 0, 384), b("psC%d" % m, 0, 384), OP.min, OP.max)
+        tt(b("xs", 16, 24), m0, b("thr", 0, 8), OP.is_lt)
+        ts(b("xs", 0, 8), m0, 11.5, OP.is_lt)
+        ts(b("thr", 8, 16), m0, 11.5, OP.is_ge, 11.5, OP.mult)
+        tt(b("thr", 24, 32), b("thr", 8, 16), b("thr", 16, 24), OP.mult)
+        tt(b("xs", 8, 16), m1, b("thr", 8, 16), OP.is_lt)
+        tt(b("xs", 24, 32), m1, b("thr", 24, 32), OP.is_lt)
 
-        def light(m):
-            if m == 0:
-                ts(b("thr", 0, 8), b("psC0", 384, 392), 4143.5, OP.is_lt, 11.5, OP.mult)
-                best(0)
-                tt(b("xs", 16, 24), m0, b("thr", 0, 8), OP.is_lt)
+        for m in range(2):
+            p, lo = b("psC%d" % m, 392, 400), 768 * m
+            mm(p, b("crep", 0, 128), b("xs", 16 + 8 * m, 24 + 8 * m), True, True)
+            tt(b("bw", 8 * m, 8 * m + 8), p, b("bi8", 0, 8), OP.mult)
+            p = b(tail[0], lo, lo + 256)
+            mm(p, b("one", 0, 128, 1, 1), b("cst", 128, 384, 1, 1), True, False)
+            for ch in range(32):
+                at = SLOT[cc[m]] + 128 * ch
+                mm(b(tail[0], lo + ch, lo + 256, 32), b("rr", at, at + 128), b("bw", 8 * m, 8 * m + 8), False, ch == 31)
+            if ROUNDER[m] == "s":
+                r = b("r%d" % m, 0, 256)
+                act(r, p, AF.Copy, 2.0 ** -9)
             else:
-                ts(b("thr", 16, 24), b("psC1", 384, 392), 4143.5, OP.is_lt)
-                best(1)
-                tt(b("thr", 24, 32), b("thr", 8, 16), b("thr", 16, 24), OP.mult)
-                tt(b("xs", 8, 16), m1, b("thr", 8, 16), OP.is_lt)
-                tt(b("xs", 24, 32), m1, b("thr", 24, 32), OP.is_lt)
+                r = b("hI", 0, 256)
+                ts(r, p, 2.0 ** -9, OP.add)
+            tt(b("mk", 256 * m, 256 * m + 256), r, p, OP.is_gt)
+        for h in range(2):
+            for m in range(2):
+                mm(b(tail[0], 256 + 128 * h, 384 + 128 * h), b("mk", 256 * m + h, 256 * m + 256, 2), id15, m == 0, m == 1)
+        p = b(tail[0], 256, 512)
+        tt(p, p, b("w2", 0, 256), OP.min)
+        red(b("smv", 0, 1), p)
+        tt(b("w1", 0, 256), p, b("wf", 0, 256), OP.add)
+        mm(b("psC0", 400, 401), b("bok", 0, 128), b("smv", 5, 6), True, False)
+        mm(b("psC0", 400, 401), b("bok", 0, 128), b("smv", 0, 1), False, True)
+        ts(b("smv", 2, 3), b("psC0", 400, 401), 128.0, OP.max, 256.5, OP.min)
+        ts(b("smv", 3, 4), b("psC0", 400, 401), 0.0, OP.is_lt, 0.5, OP.max)
+        ts(b("woff", 8, 264), b("w1", 0, 256), b("smv", 2, 3), OP.add, b("smv", 3, 4), OP.mult)
 
-        def first():
-            ts(b("xs", 0, 8), m0, 11.5, OP.is_lt)
-            ts(b("thr", 8, 16), m0, 11.5, OP.is_ge, 11.5, OP.mult)
-            ts(b("w2", 0, 256), b("wf", 0, 256), 2.0, OP.mult, 8.0, OP.min)
+        xT = b("xT", 0, 128, 1, 32)
+        mm(b(tail[1], 0, 128, 1, 32), b("xs", 0, 32), ident, True, True)
+        act(xT, b(tail[1], 0, 128, 1, 32), AF.Copy, 0.0, b("sgn", 0, 1, 1, 32))
+        for m in range(2):
+            mm(b(tail[2], 128 * m, 128 * m + 128), b("em", 128 * m, 128 * m + 128, 1, 32), xT, True, True)
+        for k in range(4):
+            mm(b(tail[1], 128, 256), b("em", 128 * k, 128 * k + 128, 1, 32), xT, k == 0, k == 3)
+        total(b("a16", 0, 1), b(tail[1], 128, 256), 16.0)
+        act(b("yab", t, t + 1), b("a16", 0, 1), AF.Copy, 0.0, 0.0625)
 
-        def whole():
-            red(b("smv", 0, 1), b("w1", 0, 258))
-            mm(b("psC0", 400, 401), b("bok", 0, 128), b("smv", 0, 1), True, True)
+        for m in range(2):
+            terms = [(n2id, zz[m]), (b("p2id", 0, 128), zh)] * (m == 1 or cut < BLK) + [(ident, x) for x in ends]
+            for k, (l, x) in enumerate(terms):
+                mm(b(tail[2], 512 + 128 * m, 640 + 128 * m), l, x, k == 0, k == len(terms) - 1)
+        for m in range(2):
+            lo, p = 128 * m, b(tail[2], 128 * m, 128 * m + 128)
+            ts(b("q01", lo, lo + 128), b(tail[2], 512 + lo, 640 + lo), 0.25, OP.mult, -0.375, OP.add)
+            tt(p, b("q01", lo, lo + 128), p, OP.mult)
+            tt(b("zo%d" % t, lo, lo + 128), zz[m], p, OP.add)
+        for kind in (("u0", "c0"), ("u1", "f1"), ("u2", "f2"), ("f3", "f0"))[t]:
+            send(kind)
 
-        def halve():
-            ts(b("smv", 2, 3), b("psC0", 400, 401), 128.0, OP.max, 256.5, OP.min)
-            ts(b("smv", 3, 4), b("psC0", 400, 401), 0.0, OP.is_lt, 0.5, OP.max)
-            ts(b("woff", 8, 264), b("w1", 0, 256), b("smv", 2, 3), OP.add, b("smv", 3, 4), OP.mult)
-
-        def prefix():
-            prefix_scan()
-            prefix_sums()
-
-        return {"row": row, "sc": scatter, "rest": rest_of_setup, "seq": sequence, "pos": places, "fin": finished, "i": next_inverse,
-                "ms": lambda m, k: members("s", m, k), "mv": lambda m, k: members("v", m, k), "sum": sums, "cen": centres,
-                "cend": centres_end, "rep": repeated, "factors": factors, "g": gather, "f": fill, "A": absolute, "C": compare,
-                "T": test, "c": counts, "x": extremes, "L": light, "first": first, "w": words, "k": marks, "r": rounded,
-                "d": marked, "turn": turn, "dbl": double, "fold": fold, "cho": choices, "spr": spread, "hea": heavy,
-                "hand": hand_over, "mid": middle, "q": quarter, "move": move, "whole": whole, "halve": halve, "pre": prefix,
-                "end": prefix_end}
-
-    steps = [round_steps(t) for t in range(ROUNDS)]
     for t in range(ROUNDS):
-        for word in ORDER[t].split():
-            name = word.lstrip("-").rstrip("0123456789")
-            steps[t - word.count("-")][name](*[int(x) for x in word.lstrip("-")[len(name):]])
+        one_round(t)
+        if t == 1:
+            narrowed(3)
 
     ts(b("ywb", 0, 256), b("woff", 8, 264), -128.0, OP.add)
-    dma("y", [(T.yw[:], b("ywb", 0, 256))])
-    dma("y", [(T.ya[:], (T.yab[0::16, 0:4], "yab", 0, 4))])
-    dma("s", [(T.yz[:, 384:512], b("zf3", 0, 128)), (T.yz[:, 0:128], b("zf3", 128, 256))])
+    dma("y", [(T.yz[:, 128:256], b("zf1", 0, 128)), (T.yz[:, 256:384], b("zf2", 0, 128))], 0.8)
+    dma("y", [(T.yw[:], b("ywb", 0, 256))], 0.7)
+    dma("y", [(T.ya[:], (T.yab[0::16, 0:4], "yab", 0, 4))], 0.1)
+    dma("s", [(T.yz[:, 384:512], b("zf3", 0, 128))], 0.4)
+    dma("y", [(T.yz[:, 0:128], b("zf0", 0, 128))], 0.4)
+
+    if not PLAN:
+        PLAN.extend(plan(calls))
+    for i in PLAN:
+        for issue in calls[i][1]:
+            issue()
     for sem, val in count.items():
         if waited["g"].get(sem, 0) < val:
             g.wait_ge(T.sem[sem], val)

@@ -7,33 +7,43 @@ AF = ActivationFunctionType
 NR = 8
 ROUNDS = 4
 BLK = 1024
-OP_, OI0, OI1, OI2 = 8192, 14336, 20480, 26624
+WIN = 16384
+OP_, OI0, OI1, OI2 = 20480, 4096, 10240, 26624
 BIG = 1.5 * 2.0 ** 34
 ROUND = 1.5 * 2.0 ** 23
-PIECES = 2
-FILLS = 2
+SEG = 50
+FAR = 512.0
+FILLS = 4
 CUTS = ((0, 2, 4, 6, 8), (0, 2, 4, 6, 8), (0, 1, 2, 3, 4, 5, 6, 7, 8), (0, 1, 2, 3, 4, 5, 6, 7, 8))
 FIRST = 11.0
-TAKEN = ()
-WEIGHT = (1.0, 1.0, 1.0, 1.0)
+TAKEN = ((1, 6),)
+WEIGHT = (1.5, 1.0, 1.2, 1.0)
 SHARE = 5
-TESTS = ("ATATATATATAT", "ATAAATAAATAA", "TATATATATATA", "TATATATATATA")
-LANES = (128, 128, 64, 64)
-FOLD = (6, 6, 6, 4)
-MEMBERS = ("ssssssvv", "ssssssss", "ssssssss", "ssssssss")
-CYCLE, COLUMN = np.array([0.83e-3, 0.83e-3, 1.1e-3, 0.95e-3]), np.array([0.52e-3, 0.52e-3, 0.7e-3, 0.6e-3])
-GATHER, SCATTER = np.array([1.1, 1.4, 1.6, 2.0]), np.array([1.8, 3.0, 5.0, 2.2])
+TESTS = ("DTDTDTDTASAS", "ASASASATASAS", "ASASASATASAS", "ASASASATASAS")
+FOLD = ((5, 6), (5, 6), (5, 6), (4, 5))
+SHARES = ((1, 2), (1, 2), (1, 2), (1, 2))
+SOURCE = 0.6
+FILLED = ("2^16", "-2^16", "2048", "3/8")
+REPEATER = "gggg"
+EAGER = (0, 1, 2, 3)
+SUMMED = ()
+MEMBERS = ("ssssssss", "ssssssss", "ssssssss", "ssssssss")
+CYCLE, COLUMN = np.array([0.83e-3, 0.85e-3, 1.05e-3, 0.95e-3]), np.array([0.44e-3, 0.44e-3, 0.55e-3, 0.52e-3])
+GATHER, SCATTER = np.array([1.15, 1.5, 1.6, 1.9]), np.array([2.0, 2.8, 4.6, 2.2])
 CALL, WAKE = {"v": 0.06, "s": 0.1, "t": 0.006, "g": 0.15, "y": 0.05}, 0.06
 WAKES = (0.06, 0.06, 0.12, 0.1)
-ROUNDER = "ss"
-PARTS = ((0, 384, 0),)
+LOADS = "zl01w23"
+HALVES = False
 SEED = 6
-SWAPS = 18000
+SWAPS = 60000
 SLACK = 0.0015
 SHAKE = 8.0
 REACH = 12.0
+STRIDE = 40
+ASIDE = 4
+MEAN = 0.2
 PASSES = 30
-CASES = (0, 1)
+CASES = (0, 1, 2, 3)
 
 MSG = [
     ("i01", "z0s", 0, 256, -1, "zin0", 0), ("i2", "z0s", 256, 384, -2, "zin1", 1), ("i3", "z0s", 384, 512, -3, "zin2", 1),
@@ -42,24 +52,24 @@ MSG = [
     ("u2", "zo2", 128, 256, -1, "zr3", 0), ("f2", "zo2", 0, 128, 3, "zf2", 1),
     ("f3", "zo3", 0, 128, 4, "zf3", 1), ("f0", "zo3", 128, 256, 4, "zf0", 0)]
 
-_B, _F, _I, _U = "bfloat16", "float32", "int32", "uint16"
+_B, _F, _I, _U, _H = "bfloat16", "float32", "int32", "uint16", "float16"
 SCRATCH = {}
 for _n, _w, _d in [
         ("big", 32768, _B), ("ptb", 4112, _B), ("diffp", 4096, _B), ("pE", 8192, _B), ("zeros", 1024, _B),
-        ("wg0", 4096, _B), ("wg1", 4096, _B), ("rf", 8192, _F), ("vals", 4096, _F), ("rr", 12288, _B),
-        ("ind", 1024, _B), ("mkx", 1024, _B), ("mkn", 1024, _B), ("amk", 384, _B),
-        ("lmI", 1024, _I), ("lm16", 1024, _U), ("pat", 256, _F), ("mI", 16, _I), ("mF", 16, _F),
-        ("zero", 128, _B), ("one", 128, _B), ("ident", 128, _B), ("nident", 128, _B), ("id15", 128, _B), ("n2id", 128, _B),
-        ("p2id", 128, _B), ("zrep", 1024, _B), ("zh", 256, _B),
-        ("bo32", 128, _F), ("lt32", 128, _F), ("one32", 128, _F), ("bi8", 8, _B), ("rs8", 8, _B), ("sgn", 8, _F),
-        ("cst", 384, _B), ("lane", 64, _B), ("crep", 128, _B), ("em", 512, _B), ("bw", 16, _B), ("bok", 128, _F),
-        ("kl", 1536, _F), ("aF", 8, _F),
-        ("m128", 272, _F), ("wt", 256, _B), ("woff", 272, _B), ("ex", 264, _F), ("off16", 256, _U), ("w2", 256, _B), ("wf", 256, _B),
-        ("mk", 512, _B), ("w1", 264, _B), ("r0", 256, _B), ("r1", 256, _B),
-        ("smv", 8, _F), ("smi", 8, _I), ("a16", 8, _F), ("thf", 8, _F), ("yab", 4, _F), ("ywb", 256, _F),
-        ("jk", 128, _B), ("zf32", 128, _F), ("zT", 256, _B), ("hI", 384, _I), ("pos16", 384, _U),
-        ("am0", 384, _B), ("am1", 384, _B), ("thr", 32, _F), ("xs", 32, _B), ("xT", 128, _B),
-        ("q01", 256, _I), ("mx", 256, _B),
+        ("wg0", 4096, _B), ("wg1", 4096, _B), ("rf", 8192, _F), ("vals", 2048, _F), ("rr", 12288, _B),
+        ("ind", 1024, _B), ("mkx", 1024, _B), ("mkn", 1024, _B), ("amk", 8 * SEG, _B),
+        ("lmI", 1024, _I), ("lm16", 1024, _U), ("pat", 256, _F), ("mI", 8, _I), ("aF", 8, _F),
+        ("zero", 128, _B), ("one", 128, _B), ("none", 128, _B), ("ident", 128, _B), ("nident", 128, _B), ("id15", 128, _B),
+        ("hid", 128, _B), ("qid", 128, _B), ("zrep", 1024, _B), ("row", 1536, _B), ("kc", 8, _B),
+        ("bo32", 128, _B), ("boq", 128, _B), ("lt32", 128, _B), ("lth", 128, _B), ("one32", 8, _F),
+        ("bi8", 8, _B), ("bis", 8, _B), ("rs8", 8, _B), ("sgn", 8, _F),
+        ("cst", 512, _B), ("lane", 64, _B), ("crep", 128, _B), ("em", 512, _B), ("bw", 16, _B),
+        ("kl", 768, _F), ("uw", 24, _B), ("uu", 128, _F), ("dA", 128, _B),
+        ("m128", 272, _B), ("wt", 256, _B), ("woff", 272, _B), ("ex", 264, _H), ("yy", 256, _F), ("off16", 256, _U),
+        ("wcap", 256, _B), ("mk", 512, _B), ("w1", 256, _B), ("r0", 256, _B), ("r1", 256, _B),
+        ("smv", 16, _F), ("a16", 8, _F), ("yab", 4, _F), ("ywb", 256, _F),
+        ("jk", 136, _B), ("zT", 256, _B), ("hI", 256, _I), ("pos16", 384, _U),
+        ("am0", 8 * SEG, _B), ("am1", 8 * SEG, _B), ("xs", 32, _B), ("xT", 128, _B), ("zs", 256, _B), ("mx", 256, _B),
         ("z0s", 512, _B), ("zin0", 256, _B), ("zin1", 128, _B), ("zin2", 128, _B), ("zr1", 128, _B), ("zr2", 128, _B),
         ("zr3", 128, _B), ("zc0", 128, _B), ("zf1", 128, _B), ("zf2", 128, _B), ("zf3", 128, _B), ("zf0", 128, _B),
         ("zo0", 256, _B), ("zo1", 256, _B), ("zo2", 256, _B), ("zo3", 256, _B)]:
@@ -71,8 +81,8 @@ for _n, _w in [("psT", 3072), ("psC0", 512), ("psC1", 512)]:
     SCRATCH[_n] = ("psum", [128, _w], _F)
 
 SEMAPHORES = ["kv", "ks", "kt", "kg", "ls"] + ["d%d" % i for i in range(40)] + ["m_" + m[0] for m in MSG] + ["q_" + m[0] for m in MSG]
-SEMAPHORES += [x + "%d%d" % (t, part) for x in "hb" for t in range(ROUNDS) for part in range(2)]
-SEMAPHORES += ["hz"] + ["lf%d" % t for t in range(ROUNDS)] + [x + "z%d" % t for x in "hb" for t in range(ROUNDS - 1)]
+SEMAPHORES += [x + "%d%d" % (t, part) for x in "hb" for t in range(ROUNDS) for part in range(sum(SHARES[t]))]
+SEMAPHORES += ["hz"] + ["lf%d" % t for t in range(ROUNDS)] + [x + "%d" % t for x in ("hz", "ba", "bb") for t in range(ROUNDS - 1)]
 PLAN = []
 
 
@@ -91,9 +101,8 @@ def helpers_of(src, cores, T, topo):
     return sorted(idle, key=lambda x: topo.die(x) != topo.die(src))[:2]
 
 
-def landing(t, part):
-    name, lo = ("pE", 0) if FOLD[t] == 6 else ("big", OI2 + 2 * BLK)
-    return name, lo + BLK * part, lo + BLK * part + BLK
+def folds(t):
+    return [(part, lo, lo + BLK // SHARES[t][part]) for part in range(2) for lo in range(0, BLK, BLK // SHARES[t][part])]
 
 
 def mask_for(src, dst, far_src, far_dst, topo):
@@ -125,17 +134,17 @@ def rank_program(g, core, T, topo):
             for k in range(4):
                 g.sync.dma_start(T.pE[:, BLK * k:BLK * k + BLK], T.zeros[:]).then_inc(T.sem.d0, 16)
             g.wait_ge(T.sem.d0, 64)
-            half = 4096 * pair.index(core)
+            half = WIN * pair.index(core)
             for t in range(ROUNDS):
                 if t < ROUNDS - 1:
                     g.wait_ge(T.sem["hz%d" % t], 1)
-                    g.remote_dma(T.big[:, half:half + 4096], T.pE[:, 0:4096], T.sem["bz%d" % t], T.sem.ls, pid, rid, topo.mask(core, src))
+                    g.remote_dma(T.big[:, half:half + 4096], T.pE[:, 0:4096], T.sem["b%s%d" % ("ab"[pair.index(core)], t)], T.sem.ls,
+                                 pid, rid, topo.mask(core, src))
                     sent += popcount(topo.mask(core, src))
-                for part in range(2 if core == pair[0] else 0):
-                    at, name = BLK * (2 * t + part), "%d%d" % (t, part)
+                for piece, (part, lo, hi) in enumerate(folds(t) if core == pair[0] else []):
+                    at, to, name = BLK * (2 * t + part), 4096 + BLK * part, "%d%d" % (t, piece)
                     g.wait_ge(T.sem["h" + name], popcount(topo.mask(src, core)))
-                    buf, lo, hi = landing(t, part)
-                    g.remote_dma(T[buf][:, lo:hi], T.big[:, at:at + BLK], T.sem["b" + name], T.sem.ls, pid, rid,
+                    g.remote_dma(T.pE[:, to + lo:to + hi], T.big[:, at + lo:at + hi], T.sem["b" + name], T.sem.ls, pid, rid,
                                  topo.mask(core, src))
                     sent += popcount(topo.mask(core, src))
     for kind, sbuf, lo, hi, off, land, which in MSG:
@@ -151,9 +160,9 @@ def rank_program(g, core, T, topo):
         g.wait_ge(T.sem.ls, sent)
 
 
-def plan(calls):
+def plan(calls, follows):
     n = len(calls)
-    before, after, seen = [set() for _ in calls], [[] for _ in calls], {}
+    before, after, seen, soft = [set() for _ in calls], [[] for _ in calls], {}, set()
     for i, c in enumerate(calls):
         for write, xs in ((False, c[2]), (True, c[3])):
             for x in xs:
@@ -165,6 +174,9 @@ def plan(calls):
                 old = [e for e in seen.get(x[1], []) if not (write and not c[6] and x[2] <= e[0] and e[1] <= x[3])]
                 seen[x[1]] = old + [(x[2], x[3], write, i)]
         before[i] -= {k for j in before[i] if not calls[j][5] + calls[j][7] for k in before[j] if not calls[k][5] + calls[k][7]}
+        if i in follows and follows[i] not in before[i]:
+            before[i].add(follows[i])
+            soft.add((follows[i], i))
         for j in before[i]:
             after[j].append(i)
     times = [[float((c[4] + 0.0 * CYCLE)[case]) for c in calls] for case in range(len(CYCLE))]
@@ -175,37 +187,53 @@ def plan(calls):
              for c in calls]
 
     def gap(j, k):
-        return 0.0 if calls[k][0] == "-" or calls[j][0] == calls[k][0] == "t" else WAKE + late[j]
+        return 0.0 if calls[k][0] == "-" or calls[j][0] == calls[k][0] == "t" or (j, k) in soft else WAKE + late[j]
 
     late = [c[5] + c[7] for c in calls]
     edges = [[(j, gap(j, i) > 0.0) for j in sorted(before[i])] for i in range(n)]
 
-    def replay(order, time):
-        wake = WAKES[times.index(time)]
-        done, free, held, engines = [0.0] * n, {}, {}, (0.0, -1)
-        for i in order:
-            q = calls[i][0]
-            at, cause[i] = free.get(q, (0.0, -1))
-            for j, waits in edges[i]:
-                x = done[j] + late[j] + wake if waits else done[j]
-                if x >= at:
-                    at, cause[i] = x, j
-            for k in banks[i]:
-                if k in held and held[k][1] != q and held[k][0] > at:
-                    at, cause[i] = held[k][0], held[k][2]
-            done[i] = at + time[i]
-            free[q] = (done[i], i)
-            if calls[i][7]:
-                if engines[0] > done[i]:
-                    cause[i] = engines[1]
-                engines = (max(engines[0], done[i]) + calls[i][7], i)
-                late[i] = engines[0] - done[i] + calls[i][5]
-            for k in banks[i]:
-                held[k] = (done[i] + wake, q, i)
-        cause[n] = max(order[-24:], key=lambda i: done[i] + late[i])
-        return done[cause[n]] + late[cause[n]]
+    rooms_of = sorted({k for x in banks for k in x})
+    facts = [("vstgy-".index(c[0]), [j for j, waits in edges[i] if waits], [j for j, waits in edges[i] if not waits],
+              [6 + rooms_of.index(k) for k in banks[i]], c[5], c[7]) for i, c in enumerate(calls)]
 
-    cause = [-1] * (n + 1)
+    def replay(order, case, old=None, start=0):
+        time, wake = times[case], WAKES[case]
+        if old is None:
+            done, seen, cause, marks = [0.0] * n, [0.0] * n, [-1] * n, []
+            free, engines, start = [(0.0, -1, -1)] * (6 + len(rooms_of)), (0.0, -1), 0
+        else:
+            start = start // STRIDE
+            done, seen, cause, marks = old[1][:], old[2][:], old[3][:], old[4][:start]
+            free, engines = old[4][start]
+            free, start = free[:], start * STRIDE
+        for lo in range(start, n, STRIDE):
+            marks.append((free[:], engines))
+            for i in order[lo:lo + STRIDE]:
+                q, hard, easy, held, away, busy = facts[i]
+                at, why, who = free[q]
+                for j in hard:
+                    if seen[j] >= at:
+                        at, why = seen[j], j
+                for j in easy:
+                    if done[j] >= at:
+                        at, why = done[j], j
+                for k in held:
+                    x = free[k]
+                    if x[0] > at and x[2] != q:
+                        at, why = x[0], x[1]
+                done[i] = at = at + time[i]
+                free[q] = (at, i, q)
+                if busy:
+                    if engines[0] > at:
+                        why, at = engines[1], engines[0]
+                    at += busy
+                    engines = (at, i)
+                cause[i] = why
+                seen[i] = at = at + away + wake
+                for k in held:
+                    free[k] = (at, i, q)
+        last = max(order[-24:], key=lambda i: seen[i])
+        return seen[last] + MEAN * sum(seen) / n, done, seen, cause, marks, last
 
     def sweep(forward, rank, times):
         pre, post = (before, after) if forward else (after, before)
@@ -239,7 +267,7 @@ def plan(calls):
     share = [w / sum(x) for w, x in zip(WEIGHT, times)]
 
     def worth(order):
-        return sum(share[case] * replay(order, times[case]) for case in reversed(range(len(times))))
+        return sum(share[case] * replay(order, case)[0] for case in range(len(times)))
 
     best, seed = None, SEED
     for k in range(PASSES):
@@ -254,37 +282,51 @@ def plan(calls):
             seed = (seed * 1103515245 + 12345) % 2 ** 31
             way.append(x + SHAKE * (seed / 2 ** 31 - 0.5) * (abs(x - lo) < REACH))
 
-    def chain(order, case):
-        span, pairs, i = share[case] * replay(order, times[case]), [], cause[n]
+    def chain(state):
+        pairs, i, cause = [], state[5], state[3]
         while cause[i] >= 0:
             if cause[i] not in before[i]:
                 pairs.append((cause[i], i))
             i = cause[i]
-        return span, pairs
+        return pairs
 
     cases = range(len(times))
     now = best
-    chains = [chain(now[1], case) for case in cases]
+    states = [replay(now[1], case) for case in cases]
+    chains = [chain(x) for x in states]
     for k in range(SWAPS):
         order, case, slack = now[1], k % len(times), SLACK * (1.0 - k / SWAPS)
-        pairs = chains[case][1]
+        pairs = chains[case]
         seed = (seed * 1103515245 + 12345) % 2 ** 31
         j, i = pairs[(seed >> 8) % len(pairs)]
+        if (seed >> 3) % 16 < ASIDE:
+            i = (seed >> 8) % n
+            j = states[case][3][i]
+            if j < 0 or j in before[i]:
+                continue
         a, z = order.index(j), order.index(i)
-        between, ahead = order[a:z + 1], {i}
-        for x in reversed(between):
-            if x in ahead:
-                ahead |= before[x]
-        if j in ahead:
+        between = order[a:z + 1]
+        if seed >> 7 & 1:
+            ahead = {i}
+            for x in reversed(between):
+                if x in ahead:
+                    ahead |= before[x]
+        else:
+            behind = {j}
+            for x in between:
+                if x in behind:
+                    behind.update(after[x])
+            ahead = set(between) - behind
+        if j in ahead or i not in ahead:
             continue
         order = order[:a] + [x for x in between if x in ahead] + [x for x in between if x not in ahead] + order[z + 1:]
-        first = chain(order, case)
-        if first[0] > chains[case][0] + slack:
+        first = replay(order, case, states[case], a)
+        if share[case] * (first[0] - states[case][0]) > slack:
             continue
-        tried = [first if x == case else chain(order, x) for x in cases]
-        span = sum(x[0] for x in tried)
+        tried = [first if x == case else replay(order, x, states[x], a) for x in cases]
+        span = sum(share[x] * tried[x][0] for x in cases)
         if span < now[0] + slack:
-            now, chains = (span, order), tried
+            now, states, chains = (span, order), tried, [chain(x) for x in tried]
             if span < best[0]:
                 best = now
     return best[1]
@@ -297,14 +339,14 @@ def rank_main(g, core, rank, cores, T, topo):
     waited = {q: {} for q in Q}
     hist = {}
     nd = [0, 0]
-    calls = []
+    calls, follows = [], {}
     apart = [False]
 
     def need(q, name, lo, hi, write, toks, loose):
         ps = name.startswith("ps")
         for (l, h, wr, sem, val, qq) in hist.get(name, []):
             if qq == q and qq in SEMOF:
-                if not (l < hi and lo < h) or not wr or (ps and q == "t") or (write and loose):
+                if not (l < hi and lo < h) or not (wr or write) or (ps and q == "t") or (write and wr and loose):
                     continue
             elif ps:
                 if l // 512 > (hi - 1) // 512 or lo // 512 > (h - 1) // 512:
@@ -344,8 +386,8 @@ def rank_main(g, core, rank, cores, T, topo):
     def ap(x):
         return x[0] if isinstance(x, tuple) else x
 
-    def emit(q, fn, reads, writes, time, joined=False):
-        reads = [x for x in reads if isinstance(x, tuple)]
+    def emit(q, fn, reads, writes, time, joined=False, held=()):
+        reads, writes = [x for x in reads if isinstance(x, tuple)], list(writes)
         loose = apart[0]
 
         def issue():
@@ -362,14 +404,14 @@ def rank_main(g, core, rank, cores, T, topo):
             c = calls[-1]
             assert c[0] == q
             c[1].append(issue)
-            c[2:5] = [c[2] + reads, c[3] + writes, c[4] + CALL[q] + time]
+            c[2:5] = [c[2] + reads, c[3] + writes + list(held), c[4] + CALL[q] + time]
         else:
-            calls.append([q, [issue], reads, writes, CALL[q] + time, 0.0, loose, 0.0])
+            calls.append([q, [issue], reads, writes + list(held), CALL[q] + time, 0.0, loose, 0.0])
 
-    def dma(q, pairs, busy):
+    def dma(q, pairs, busy, behind=()):
         sem = "d%d" % nd[0]
         nd[0] += 1
-        reads, writes = [i for o, i in pairs if isinstance(i, tuple)], [o for o, i in pairs if isinstance(o, tuple)]
+        reads, writes = [i for o, i in pairs if isinstance(i, tuple)] + list(behind), [o for o, i in pairs if isinstance(o, tuple)]
 
         def issue():
             waits(q, reads, writes)
@@ -388,7 +430,7 @@ def rank_main(g, core, rank, cores, T, topo):
         nd[1] += 1
 
     def narrow(*xs):
-        return 0.5 if all(SCRATCH[x[1]][2] in (_B, _U) for x in xs) else 1.0
+        return 0.5 if all(SCRATCH[x[1]][2] in (_B, _U, _H) for x in xs) else 1.0
 
     def cycles(k):
         return max(k, 64) * CYCLE
@@ -415,15 +457,20 @@ def rank_main(g, core, rank, cores, T, topo):
         emit("v", lambda: g.vector.tensor_tensor_scan(o[0], d0[0], d1[0], 0.0, op0, op1), [d0, d1], [o], cycles(o[4] * narrow(o, d0, d1)))
 
     def act(o, x, func, bias=0.0, scale=1.0):
-        emit("s", lambda: g.scalar.activation(o[0], x[0], func, bias=bias, scale=ap(scale)), [x, scale], [o], o[4] * CYCLE)
+        emit("s", lambda: g.scalar.activation(o[0], x[0], func, bias=ap(bias), scale=ap(scale)), [x, scale, bias], [o], o[4] * CYCLE)
 
-    def total(o, x, scale):
-        j = b("jk", 0, 128)
-        emit("s", lambda: g.scalar.activation(j[0], x[0], AF.Copy, scale=scale, accum_out=o[0]), [x], [j, o], x[4] * CYCLE)
+    def total(o, x, bias, scale):
+        j = b("jk", 0, x[4])
+        emit("s", lambda: g.scalar.activation(j[0], x[0], AF.Copy, bias=bias, scale=scale, accum_out=o[0]), [x], [j, o], x[4] * CYCLE)
 
-    def mm(o, l, r, start, stop, joined=False):
+    def mm(o, l, r, start, stop, joined=False, held=False):
+        bank = [(None, o[1], o[2] // 512 * 512, o[2] // 512 * 512 + 512)] if held else []
         emit("t", lambda: g.tensor.matmul(o[0], l[0], r[0], start, stop), [l, r], [o],
-             max(64, r[4]) * COLUMN * (4 if SCRATCH[l[1]][2] == _F else 1), joined or not start)
+             max(64, r[4]) * COLUMN * (4 if SCRATCH[l[1]][2] == _F else 1), joined or not (start or held), bank)
+
+    def group(terms, held=False):
+        for k, x in enumerate(terms):
+            mm(x[0], x[1], x[2], k == 0, k == len(terms) - 1, k > 0 and len(x) == 3, held)
 
     def asel(o, i, pattern, op, base, cm, fill=0.0):
         emit("g", lambda: g.affine_select(o[0], i[0], pattern, op, fill, base, cm), [i], [o], 2 * o[4] * CYCLE)
@@ -470,50 +517,94 @@ def rank_main(g, core, rank, cores, T, topo):
     aides = [DstId(rid=topo.addr(x, core)[0], pnc=topo.addr(x, core)[1]) for x in (helper, sweeper)]
     there, back = topo.mask(core, helper), topo.mask(helper, core)
 
-    zero, one, one32 = b("zero", 0, 128), b("one", 0, 128), b("one32", 0, 128)
-    ident, nident, id15, n2id = b("ident", 0, 128), b("nident", 0, 128), b("id15", 0, 128), b("n2id", 0, 128)
-    dma("y", [(b("wt", 0, 256), T.w0[:])], 0.5)
-    dma("s", [(b("lmI", 0, 256), T.lm[:, 0:256])], 0.7)
+    zero, one = b("zero", 0, 128), b("one", 0, 128)
+    ident, nident, id15, none = b("ident", 0, 128), b("nident", 0, 128), b("id15", 0, 128), b("none", 0, 128)
+    hid, qid, boq = b("hid", 0, 128), b("qid", 0, 128), b("boq", 0, 128)
+    loads = {"w": (b("wt", 0, 256), T.w0[:], 0.5), "l": (b("lmI", 0, 256), T.lm[:, 0:256], 0.7), "z": (b("z0s", 0, 256), T.z0[:, 0:256], 0.5)}
     for k in range(4):
-        dma("y", [(b("ptb", 16 + 1024 * k, 1040 + 1024 * k), T.pt[:, 1024 * k:1024 * k + 1024])], 1.05)
-    dma("y", [(b("z0s", 0, 512), T.z0[:])], 0.7)
-    dma("y", [(b("lmI", 256, 1024), T.lm[:, 256:1024])], 1.4)
-    iota(b("mI", 0, 16), [[-1, 16]], 16, 1, False)
-    ms(zero, 0.0)
-    ms(one32, 1.0)
-    for lo in range(8):
-        ms(b("pat", 32 * lo, 32 * lo + 32), 2.0 ** (13 - lo))
-    ts(b("mI", 0, 16), b("mI", 0, 16), 15, OP.bitwise_and)
-    ts(b("mF", 0, 16), b("mI", 0, 16), 0.0, OP.is_equal)
+        loads[str(k)] = (b("ptb", 16 + 1024 * k, 1040 + 1024 * k), T.pt[:, 1024 * k:1024 * k + 1024], 1.05)
+    for k, x in enumerate(LOADS):
+        if k:
+            follows[len(calls)] = len(calls) - 1
+        dma("y", [loads[x][:2]], loads[x][2])
+    dma("y", [(b("lmI", 256, 512), T.lm[:, 256:512])], 0.7, [b("ptb", 16, 4112)])
+    dma("y", [(b("z0s", 256, 512), T.z0[:, 256:512]), (b("lmI", 512, 1024), T.lm[:, 512:1024])], 1.5, [b("lmI", 256, 512)])
+    iota(b("mI", 0, 1), [[0, 1]], 0, 1, False)
+    iota(b("pat", 0, 256), [[1, 16], [0, 16]], 0, 0)
+    iota(zero, [[0, 128]], 0, 0)
+    ts(b("mI", 0, 1), b("mI", 0, 1), 15, OP.bitwise_and)
+    cp(b("aF", 0, 1), b("mI", 0, 1))
+    ts(b("vals", 0, 256), b("pat", 0, 256), b("aF", 0, 1), OP.is_equal, 2.0 ** 13, OP.mult)
+    for k in range(3):
+        act(b("vals", 256 << k, 512 << k), b("vals", 0, 256 << k), AF.Copy, 0.0, 0.5 ** (1 << k))
     ms(b("ptb", 0, 16), 0.0)
     ms(b("m128", 0, 272), -128.0)
     ms(b("woff", 0, 8), 128.0)
-    ms(b("cst", 128, 384), 128.0)
+    ms(b("cst", 0, 512), 128.0)
     ms(one, 1.0)
-    ms(b("a16", 0, 8), 0.0)
-    for k in range(FILLS):
-        iota(b("big", BLK * k, BLK * k + BLK), [[0, BLK]], 0, 0)
-    for k in range(FILLS, 8, 2):
-        ms(b("big", BLK * k, BLK * min(k + 2, 8)), 0.0, [b("mF", 0, 16), b("pat", 0, 256), zero])
+    ms(b("zeros", 0, BLK), 0.0)
+    parts = [WIN * (k // 4) + BLK * (k % 4) for k in range(8)]
+    for lo in parts[:8 - FILLS:2]:
+        ms(b("big", lo, lo + 2 * BLK), 0.0, [b("vals", 0, 256)])
+    if FILLS:
+        dma("y", [(b("big", lo, lo + BLK), b("zeros", 0, BLK)) for lo in parts[8 - FILLS:]], 0.8 * FILLS, [b("ptb", 16, 4112)])
 
     asel(ident, zero, [[-1, 128]], OP.not_equal, 0, 1, 1.0)
     asel(nident, zero, [[-1, 128]], OP.not_equal, 0, 1, -1.0)
-    asel(b("lt32", 0, 128), one32, [[-16, 8], [0, 16]], OP.is_ge, 0, 1)
+    asel(b("lt32", 0, 128), one, [[-16, 8], [0, 16]], OP.is_ge, 0, 1)
     asel(b("bo32", 0, 128), b("lt32", 0, 128), [[16, 8], [0, 16]], OP.is_ge, 15, -1)
     asel(b("lt32", 0, 128), b("bo32", 0, 128), [[1, 128]], OP.is_ge, -1, -1)
+    asel(b("lth", 0, 128), b("lt32", 0, 128), [[-1, 128]], OP.not_equal, 0, 1, 0.5)
+    act(boq, b("bo32", 0, 128), AF.Copy, 0.0, 2.0 ** -12)
     for kind in ("i01", "i2", "i3"):
         send(kind)
-    kl = b("kl", 0, 768)
+
+    rows = {}
+
+    def row(name, first, second=None):
+        k = 1 if second is None else 2
+        rows[name] = x = b("row", 128 * len(rows), 128 * len(rows) + 128, 1, k)
+        if name in FILLED:
+            ms(x, float(first if k == 1 else second))
+            if k == 2:
+                ms(b("row", x[2], x[3], 1, 1), float(first))
+        elif first == int(first) and abs(first) < 2 ** 23:
+            iota(x, [[0, 128]], int(first), 0 if k == 1 else int(second - first))
+        elif k == 1:
+            asel(x, b("zero", 0, 128, 1, 1), [[0, 128]], OP.is_gt, 0, 0, first)
+        else:
+            iota(x, [[0, 128]], int(second), 0)
+            asel(x, x, [[0, 128]], OP.not_equal, 0, 1, first)
+
+    def cst(k, rows=1):
+        return b("cst", 0, k, 1, rows)
+
+    asel(b("kc", 0, 1, 1, 1), b("zero", 0, 1, 1, 1), [[0, 1]], OP.is_gt, 0, 0, -2.0 ** -13)
+    iota(b("kc", 2, 3, 1, 1), [[0, 1]], int(ROUND / 2048), 0)
+    row("mid", 255 * 256)
+    row("lanes-", -1952, -1)
+    row("lanes+", 1952, -15)
+    row("2^16", 1.5 * 2.0 ** 32)
+    row("-2^16", -1.5 * 2.0 ** 32)
+    row("16", 1.5 * 2.0 ** 20)
+    row("sum", -4096, -36)
+    row("2048", 2.0 ** 28, -16)
+    row("1", ROUND / 128)
+    row("-1", -ROUND / 128)
+    row("3/8", -3.0 / 1024)
+    odd = b("row", 1408, 1536, 1, 1)
+    iota(odd, [[0, 8], [int(-61 * FAR), 2], [0, 8]], int(2 * FAR), 0)
+    iota(b("lane", 0, 64, 1, 2), [[1, 64]], 0, 0)
+    asel(b("lane", 0, 64, 1, 2), b("lane", 0, 64, 1, 2), [[0, 64]], OP.not_equal, -1, 1, 0.5)
+    iota(none, [[0, 128]], -1, 0)
+    uw = b("uw", 1, 17, 2)
+    iota(b("uw", 0, 18), [[0, 18]], 0, 0)
+    iota(uw, [[-32, 8]], 1, 2)
+    asel(uw, uw, [[-32, 8]], OP.is_ge, 1, 2)
+    asel(uw, uw, [[32, 8]], OP.is_ge, 30, -2)
+    kl = b("kl", 0, 768, 1, 16)
     iota(kl, [[40, 6], [0, 16], [5, 8]], 17, 0)
-    asel(kl, kl, [[0, 6], [-16, 8], [0, 16]], OP.is_ge, 0, 1)
-    asel(kl, kl, [[0, 6], [16, 8], [0, 16]], OP.is_ge, 15, -1)
-    asel(b("kl", 768, 1536), kl, [[0, 48], [1, 16]], OP.is_ge, -8, 0)
-    asel(kl, kl, [[0, 48], [-1, 16]], OP.is_ge, 7, 0)
-    iota(b("cst", 0, 128), [[0, 8], [976, 2], [0, 8]], 0, 0)
-    asel(b("cst", 0, 128), b("cst", 0, 128), [[0, 128]], OP.not_equal, 0, 1, 1952.0)
-    iota(b("lane", 0, 64), [[1, 64]], 0, 0)
-    asel(b("lane", 0, 64), b("lane", 0, 64), [[0, 64]], OP.not_equal, -1, 1, 1.0)
-    iota(b("zeros", 0, BLK), [[0, BLK]], 0, 0)
+    asel(kl, kl, [[0, 6], [-1, 16], [0, 8]], OP.is_equal, 0, 1)
 
     def lend_zeros():
         waits("g", [b("zeros", 0, BLK)], [])
@@ -531,26 +622,31 @@ def rank_main(g, core, rank, cores, T, topo):
     asel(b("ind", 0, BLK), b("zeros", 0, BLK), [[-1, 128], [0, 8]], OP.not_equal, 0, 1, -15.0)
     asel(id15, zero, [[-1, 128]], OP.not_equal, 0, 1, 15.0)
     asel(b("rs8", 0, 8), b("zero", 0, 8), [[-16, 8]], OP.not_equal, 0, 1, 1.0)
-    iota(b("zh", 0, 256), [[0, 256]], 0, 0)
-    iota(b("mkx", 0, BLK), [[0, 128], [1024, 8]], -512, 0)
-    iota(b("mkn", 0, BLK), [[0, 128], [-1024, 8]], 512, 0)
-    asel(b("p2id", 0, 128), zero, [[-1, 128]], OP.not_equal, 0, 1, 2.0)
-    iota(b("amk", 0, 384), [[0, 8], [16, 48]], 0, 0)
-    asel(n2id, zero, [[-1, 128]], OP.not_equal, 0, 1, -2.0)
+    iota(b("mkx", 0, 256), [[0, 32], [1024, 8]], -512, 0)
+    iota(b("mkn", 0, 256), [[0, 32], [-1024, 8]], 512, 0)
+    dma("y", [(b(x, lo, lo + 256), b(x, 0, 256)) for x in ("mkx", "mkn") for lo in range(256, BLK, 256)], 1.8)
+    asel(hid, zero, [[-1, 128]], OP.not_equal, 0, 1, 0.5)
+    asel(qid, zero, [[-1, 128]], OP.not_equal, 0, 1, 0.25)
+    iota(b("amk", 0, 8 * SEG), [[0, 8], [16, SEG]], 0, 0)
+    power = b("aF", 2, 3)
     for lo in range(8):
-        asel(b("crep", 0, 128), zero if lo == 0 else b("crep", 0, 128), [[0, 8], [-8, 16]], OP.not_equal, -lo, 1, 2.0 ** (lo - 14))
-    asel(b("em", 0, 512), b("zeros", 0, 512), [[-8, 4], [-1, 8], [0, 16]], OP.not_equal, 0, 1, 1.0)
-    asel(b("sgn", 0, 1), b("one32", 0, 1), [[0, 1]], OP.is_ge, 15, -1, -1.0)
+        asel(power, power if lo else b("aF", 0, 1), [[0, 1]], OP.is_ge, 16 * lo - 1, -1, 2.0 ** (lo - 14))
+    iota(b("jk", 0, 128), [[0, 8], [1, 16]], 0, 0)
+    ts(b("crep", 0, 128), b("jk", 0, 128), b("aF", 0, 1), OP.is_equal, power, OP.mult)
+    asel(b("em", 0, 512, 1, 32), b("zeros", 0, 512, 1, 32), [[-8, 4], [-1, 8], [0, 16]], OP.not_equal, 0, 1, 1.0)
+    for k, (first, second) in enumerate(((-FAR / 2, FAR), (FAR / 2, 0))):
+        iota(b("sgn", k, k + 1), [[0, 1]], int(first), 0)
+        asel(b("sgn", k, k + 1), b("sgn", k, k + 1), [[0, 1]], OP.is_ge, 15, -1, float(second))
 
-    ts(b("aF", 2, 3), b("mI", 0, 1), 2.0, OP.mult, 1.0, OP.add)
-    act(b("bok", 0, 128), b("bo32", 0, 128), AF.Copy, 0.0, 1024.0)
-    cp(b("bi8", 0, 8), b("bo32", 0, 128, 16))
+    act(b("bi8", 0, 8), b("bo32", 0, 128, 16), AF.Copy)
+    act(b("bis", 0, 8), b("bo32", 0, 128, 16), AF.Copy, 0.0, -372.0)
     for c in range(4):
-        cp(b("lm16", 256 * c, 256 * c + 256), b("lmI", 256 * c, 256 * c + 256))
+        for h in range(2):
+            cp(b("lm16", 256 * c + 128 * h, 256 * c + 128 * h + 128), b("lmI", 256 * c + h, 256 * c + 256, 2))
     ts(b("woff", 8, 264), b("wt", 0, 256), 128.0, OP.add)
+    mm(b("psC1", 408, 409), odd, b("one", 0, 1, 1, 1), True, True)
+    act(b("a16", 0, 1), b("psC1", 408, 409), AF.Copy, 32.0, -16.0 / FAR)
 
-    for a in range(16):
-        act(b("vals", 256 * a, 256 * a + 256), b("pat", 0, 256), AF.Copy, 0.0, b("mF", a, a + 1))
     SLOT = (0, 4096, 8192, 4096)
 
     def narrowed(c):
@@ -558,7 +654,7 @@ def rank_main(g, core, rank, cores, T, topo):
 
     for c in range(4):
         for lo, hi in zip(CUTS[c], CUTS[c][1:]):
-            w, v = b("rf", 4096 * (c % 2), 4096 * (c % 2) + 4096), b("vals", 512 * lo, 512 * hi)
+            w, v = b("rf", 4096 * (c % 2), 4096 * (c % 2) + 4096), b("vals", 512 * (lo % 4), 512 * (lo % 4 + hi - lo))
             off = b("lm16", 256 * c + 32 * lo, 256 * c + 32 * hi)
             if (c, lo) in TAKEN:
                 emit("v", lambda w=w, v=v, off=off: g.vector.tensor_copy(w[0].indirect(off[0]), v[0]), [v, off], [w], v[4] * SCATTER * CYCLE)
@@ -570,26 +666,34 @@ def rank_main(g, core, rank, cores, T, topo):
 
     def prefix():
         scan(b("ex", 0, 257), b("m128", 0, 257), b("woff", 7, 264), OP.add, OP.add)
-        mm(b("psC0", 401, 402), b("lt32", 0, 128), b("ex", 256, 257), True, True)
-        mm(b("psC0", 402, 403), b("bo32", 0, 128), b("ex", 256, 257), True, True)
-        ts(b("off16", 0, 256), b("ex", 0, 256), b("psC0", 401, 402), OP.add)
-        act(b("smv", 5, 6), b("ex", 256, 257), AF.Copy, -7168.5 / 16.0)
-        x = b("thf", 1, 2)
-        act(x, b("psC0", 402, 403), AF.Copy, -0.25, 0.5)
-        act(x, x, AF.Copy, ROUND)
-        act(x, x, AF.Relu, ROUND + 4096.0, -1.0)
-        act(b("thf", 0, 1), x, AF.Copy, 2.0, -1.0 / 2048.0)
+        rowsum, th, inv, q, at, half = [b("ex", 256, 257)] + [b("smv", k, k + 1) for k in (2, 4, 6, 8, 10)]
+        p = b("psC0", 408, 409)
+        group([(p, b("one", 0, 128, 1, 1), b("kc", 0, 1, 1, 1)), (p, boq, rowsum), (p, b("one", 0, 128, 1, 1), b("kc", 2, 3, 1, 1))])
+        mm(b("psC1", 409, 410), b("lth", 0, 128), rowsum, True, True)
+        mm(b("psC1", 410, 411), b("lt32", 0, 128), rowsum, True, True)
+        ts(th, p, -ROUND / 2048, OP.add, 2.0, OP.min)
+        emit("v", lambda: g.vector.reciprocal(inv[0], th[0]), [th], [inv], 0.14)
+        act(half, th, AF.Copy, -2.0 ** -12, 0.5)
+        ts(q, b("psC1", 409, 410), inv, OP.mult, ROUND, OP.add)
+        ts(at, q, -ROUND, OP.add, th, OP.mult)
+        ts(at, at, b("psC1", 410, 411), OP.subtract, half, OP.subtract)
+        for par in range(2):
+            y = b("yy", 128 * par, 128 * par + 128)
+            ts(y, b("ex", par, 256, 2), at, OP.subtract, inv, OP.mult)
+            ts(b("off16", 128 * par, 128 * par + 128), y, q, OP.add, -ROUND, OP.add)
 
     banks = (("psB", 0), ("psB", 512), ("psD", 0), ("psD", 512), ("psA", 0), ("psA", 512))
     for a in range(16):
-        p = b(banks[a % 6][0], banks[a % 6][1], banks[a % 6][1] + 256)
-        mm(p, ident, b("ptb", 16 + 256 * a, 272 + 256 * a), True, False)
-        mm(p, nident, b("ptb", 15 + 256 * a, 271 + 256 * a), False, True)
+        name, at = banks[a % 6]
+        for par in range(2):
+            p, lo = b(name, at + 128 * par, at + 128 * par + 128), 16 + 256 * a + par
+            mm(p, ident, b("ptb", lo, lo + 255, 2), True, False, par == 1)
+            mm(p, nident, b("ptb", lo - 1, lo + 254, 2), False, True)
         apart[0] = True
         if a < SHARE:
-            act(b("diffp", a, 4096, 16), p, AF.Copy, 0.0, 0.5)
+            act(b("diffp", a, 4096, 16), b(name, at, at + 256), AF.Copy)
         else:
-            ts(b("diffp", a, 4096, 16), p, 0.5, OP.mult)
+            cp(b("diffp", a, 4096, 16), b(name, at, at + 256))
         apart[0] = False
 
     ZSRC = [(("zin0", 0), ("zin0", 128)), (("zr1", 0), ("zin1", 0)), (("zr2", 0), ("zin2", 0)), (("zr3", 0), ("zc0", 0))]
@@ -599,197 +703,213 @@ def rank_main(g, core, rank, cores, T, topo):
         zz = [b(n, lo, lo + 128) for n, lo in ZSRC[t]]
         prefix()
 
-        for lo in range(0, 256, 256 // PIECES):
-            hi = lo + 256 // PIECES
-            bigw, offs, dif = b("big", 0, 32768), b("off16", lo, hi), b("diffp", 16 * lo, 16 * hi)
-            emit("v", lambda offs=offs, dif=dif: g.vector.tensor_copy(bigw[0].indirect(offs[0]), dif[0]), [dif, offs], [bigw],
+        zeroed = [b("big", WIN * par, WIN * par + 4096) for par in range(2)]
+        for par in range(2):
+            bigw, offs, dif = b("big", WIN * par, WIN * par + WIN), b("off16", 128 * par, 128 * par + 128), b("diffp", 2048 * par, 2048 * par + 2048)
+            emit("v", lambda bigw=bigw, offs=offs, dif=dif: g.vector.tensor_copy(bigw[0].indirect(offs[0]), dif[0]), [dif, offs], [bigw],
                  dif[4] * SCATTER * CYCLE)
-        scan(b("pE", 0, 8192), b("big", 0, 8192), b("big", 0, 8192), OP.add, OP.add)
+        scan(b("pE", 0, 4096), zeroed[0], zeroed[1], OP.add, OP.add)
 
         def clear():
-            waits("g", [], [b("big", 0, 8192)])
+            waits("g", [], zeroed)
             g.remote_dma_fused([RemoteDMATransfer(dst_ids=[aides[k]], dma_engine_mask=1 << topo.engines(core, helper)[k],
                                                   remote_sem=T.sem["hz%d" % t]) for k in range(2)], local_sem=T.sem.ls)
             count["ls"] += 2
-            count["bz%d" % t] = popcount(back) + popcount(topo.mask(sweeper, core))
-            note(b("big", 0, 8192), True, "bz%d" % t, count["bz%d" % t], "net")
+            for x, name, who in zip(zeroed, ("ba%d" % t, "bb%d" % t), (helper, sweeper)):
+                count[name] = popcount(topo.mask(who, core))
+                note(x, True, name, count[name], "net")
 
         if t < ROUNDS - 1:
             in_turn()
-            remote(clear, [swept, lent], [b("big", 0, 8192)], 11.0, 0.0)
+            remote(clear, [swept, lent], zeroed, 11.0, 0.0)
 
-        wrow = b("ptb", 16, 4112)
-        dma("y", [((T.ptb[0::16, 16:4112], "ptb", 16, 4112), b("woff", 8, 264))], 0.6)
-        act(b("wf", 0, 256), b("woff", 8, 264), AF.Copy, -128.0)
-        act(b("w2", 0, 256), b("woff", 8, 264), AF.Abs, -132.0)
-        act(b("w2", 0, 256), b("w2", 0, 256), AF.Copy, 4.0, -1.0)
+        wrow, woff = b("ptb", 16, 4112), b("woff", 8, 264)
+        dma("y", [((T.ptb[0::16, 16:4112], "ptb", 16, 4112), woff)], 0.6)
+        act(b("wcap", 0, 256), woff, AF.Relu, 264.0, -2.0)
+        act(b("wcap", 0, 256), b("wcap", 0, 256), AF.Copy, 8.0, -1.0)
+        members = []
         for m in range(2):
             for k in range(4):
+                members += [len(calls)] * (MEMBERS[t][4 * m + k] == "s")
                 gath(MEMBERS[t][4 * m + k], b("wg%d" % m, BLK * k, BLK * k + BLK), wrow, b("lm16", 256 * cc[m] + 64 * k, 256 * cc[m] + 64 * k + 64))
-            for i in range(32):
-                mm(b("psC%d" % m, 384, 392), b("wg%d" % m, i, 4096, 32), b("rs8", 0, 8), i == 0, i == 31)
+            apart[0] = True
+            p = b("psC%d" % m, SEG - 1, 8 * SEG, SEG)
+            group([(p, rows["sum"], b("one", 0, 8, 1, 2))] +
+                  [(p, b("wg%d" % m, 2048 * (i // 16) + i % 16, 2048 * (i // 16) + 2048, 16), b("rs8", 0, 8)) for i in range(32)])
+            if m == 0:
+                mm(b("psC0", SEG - 2, 8 * SEG, SEG), b("one", 0, 128, 1, 1), b("zero", 0, 8, 1, 1), True, True)
+            apart[0] = False
 
-        act(b("zf32", 0, 128), zz[0], AF.Copy, 0.0, b("aF", 2, 3))
-        for bk in range(6):
-            at = 64 * bk + [x[2] for x in PARTS if x[0] <= 64 * bk][-1]
-            p = b("psA", at, at + 64)
-            mm(p, b("cst", 0, 128, 1, 2), b("lane", 0, 64, 1, 2), True, False)
-            for odd in range(2):
-                lo = 768 * odd + 128 * bk
-                mm(p, b("kl", lo, lo + 128), b("zf32", odd, 128, 2), False, odd == 1)
-        mm(b("psB", 0, 128), zz[0], ident, True, True)
-        zh, cut = zz[0], 8 * LANES[t]
-        if cut < BLK:
-            lo = 128 * (LANES[t] > 64)
-            zh = b("zh", lo, lo + 128)
-            act(b("zh", lo, lo + LANES[t]), b(ZSRC[t][0][0], ZSRC[t][0][1], ZSRC[t][0][1] + LANES[t]), AF.Copy)
-        mm(b("psB", 128, 256), zz[1], ident, True, False)
-        mm(b("psB", 128, 256), zh, nident, False, True)
-        act(b("zT", 0, 256), b("psB", 0, 256), AF.Copy)
-        for lo in range(0, cut, 512):
-            hi = min(cut, lo + 512)
-            mm(b("psD", lo, hi), b("zT", 0, 128), b("ind", lo, hi), True, True)
-        zrep = b("zrep", 0, cut)
-        act(zrep, b("psD", 0, cut), AF.Copy, 0.0, -1.0 / 15.0)
-        for lo, hi, at in PARTS:
-            hI = b("hI", lo, hi)
-            ts(hI, b("psA", lo + at, hi + at), b("a16", 0, 1), OP.add)
-            ts(hI, hI, 4, OP.arith_shift_right, 4095, OP.bitwise_and)
-            ts(hI, hI, b("thf", 0, 1), OP.mult, -4095.5 + 1.0 / 4096.0, OP.add)
-            ts(b("pos16", lo, hi), hI, 4095.0, OP.add)
+        zname, zlo = ZSRC[t][0]
+        u = b("psA", 512, 576, 1, 16)
+        group([(u, b("uw", 1 - par, 17 - par), b(zname, zlo + par, zlo + 128, 2)) for par in range(2)])
+        act(b("uu", 0, 64, 1, 16), u, AF.Copy, 0.0, -1.0)
+        act(b("uu", 64, 128, 1, 16), u, AF.Copy)
+        act(b("dA", 0, 128), ident, AF.Copy, 0.0, b("a16", 0, 1))
+        p, terms = b("psA", 0, 384), []
+        for k, (first, ones) in enumerate((("mid", none), ("-2^16", one))):
+            terms += [(p, rows[first], cst(384))]
+            terms += [(b("psA", 64 * bk, 64 * bk + 64), rows["lanes" + "-+"[k]], b("lane", 0, 64, 1, 2)) for bk in range(6)]
+            terms += [(b("psA", lo, lo + 128), b("dA", 0, 128), ones) + (True,) * (lo + k == 0) for lo in range(0, 384, 128)]
+            terms += [(b("psA", 64 * bk, 64 * bk + 64), b("kl", 128 * bk, 128 * bk + 128, 1, 16), b("uu", 64 * k, 64 * k + 64, 1, 16))
+                      + (True,) * (bk == 0) for bk in range(6)]
+            terms += [(p, rows[("2^16", "16")[k]], cst(384))]
+        group(terms, True)
+        ts(b("pos16", 0, 384), p, -(1.5 * 2.0 ** 27 + 127 * 65536.0), OP.add, 0.0625, OP.mult)
+
+        group([(b("psB", 128, 256), zz[1], ident), (b("psB", 128, 256), zz[0], nident)])
+        if REPEATER[t] == "g":
+            act(b("zT", 128, 256), b("psB", 128, 256), AF.Copy)
+            apart[0] = True
+            for a in range(8):
+                asel(b("zrep", a, BLK, 8), zz[0], [[0, 128]], OP.is_ge, 0, 0)
+            apart[0] = False
+        else:
+            mm(b("psB", 0, 128), zz[0], ident, True, True)
+            act(b("zT", 0, 256), b("psB", 0, 256), AF.Copy)
+            for lo in range(0, BLK, 512):
+                mm(b("psD", lo, lo + 512), b("zT", 0, 128), b("ind", lo, lo + 512), True, True)
+            act(b("zrep", 0, BLK), b("psD", 0, BLK), AF.Copy, 0.0, -1.0 / 15.0)
 
         nets = [b("big", OP_ + bk * BLK, OP_ + bk * BLK + BLK) for bk in range(6)]
-        for bk in range(6):
-            at, win = nets[bk][2], b("pE", 0, 8192)
-            net, off = b("big", at, at + cut), b("pos16", 64 * bk, 64 * bk + cut // 16)
+        turn, win, zrep = 0, b("pE", 0, 4096), b("zrep", 0, BLK)
+        for bk, net in enumerate(nets):
+            off = b("pos16", 64 * bk, 64 * bk + 64)
+            if bk:
+                follows[len(calls)] = len(calls) - 1
+            if bk < max(FOLD[t]):
+                gathered = len(calls)
             emit("v", lambda net=net, off=off: g.vector.tensor_tensor(net[0], win[0].indirect(off[0]), zrep[0], OP.subtract),
-                 [win, off, zrep], [net], cut * GATHER * CYCLE)
-            if cut < BLK:
-                gath("s", b("big", at + cut, at + BLK), win, b("pos16", 64 * bk + cut // 16, 64 * bk + 64))
-            ps = BLK * (bk % 3) if cut == BLK else 1536 * (bk % 2)
-            for h in range(2):
-                p = b("psT", ps + 512 * h, ps + 512 * h + 512)
-                mm(p, id15, b("big", at + 512 * h, at + 512 * h + 512), True, False)
-                mm(p, b("zT", 128, 256), b("ind", 512 * h, 512 * h + 512), False, True)
+                 [win, off, zrep], [net], BLK * GATHER * CYCLE)
+        tested = len(calls)
+        for bk in range(6):
+            at = nets[bk][2]
             for m in range(2):
                 lo, how = (OI0, OI1)[m] + BLK * bk, TESTS[t][2 * bk + m]
-                near, p = b("big", lo, lo + BLK), b("psT", ps, ps + BLK)
-                both, over = how == "D", OI2 + BLK * (bk % 2)
-                if both:
-                    ts(near, net, -68.0, OP.is_ge)
-                    ts(b("big", over, over + BLK), net, 68.0, OP.is_gt, -1.0, OP.mult)
-                elif m == 0:
-                    act(b("big", lo, lo + cut), net, AF.Abs, 0.0, 15.0)
-                    near = b("big", lo, lo + cut)
-                    if cut < BLK:
-                        p, rest = b("psT", ps + BLK, ps + 2 * BLK - cut), b("big", lo + cut, lo + BLK)
-                        mm(p, id15, b("big", at + cut, at + BLK), True, False)
-                        mm(p, b("zT", 0, 128), b("ind", cut, BLK), False, True)
-                        if how == "T":
-                            ts(rest, p, BIG, OP.add, BIG, OP.is_equal)
-                        else:
-                            act(rest, p, AF.Abs)
-                            near = b("big", lo, lo + BLK)
-                    ts(near, near, 1024.0, OP.is_le)
-                elif how == "A":
-                    act(near, p, AF.Abs)
-                    ts(near, near, 1024.0, OP.is_le)
-                else:
-                    ts(near, p, BIG, OP.add, BIG, OP.is_equal)
+                both, over, grain = how == "D", OI2 + BLK * (bk % 2), BLK
+                if how.islower():
+                    how, grain = how.upper(), 512
+                if m == 1 or how in "ST":
+                    ps, turn = BLK * (turn % 3), turn + 1
+                    for h in range(2):
+                        p = b("psT", ps + 512 * h, ps + 512 * h + 512)
+                        group([(p, id15, b("big", at + 512 * h, at + 512 * h + 512))] +
+                              [(p, b("zT", 128, 256), b("ind", 512 * h, 512 * h + 512))] * m + [(p, rows["2048"], cst(512, 2))] * (how == "S"))
+                for x in range(0, BLK, grain):
+                    near, net = b("big", lo + x, lo + x + grain), b("big", at + x, at + x + grain)
+                    p = b("psT", ps + x, ps + x + grain) if m == 1 or how in "ST" else net
+                    if both:
+                        ts(near, net, -68.0, OP.is_ge)
+                        ts(b("big", over, over + BLK), net, 68.0, OP.is_gt, -1.0, OP.mult)
+                    elif how == "A":
+                        act(near, p, AF.Abs)
+                        ts(near, near, 1024.0 if m else 68.0, OP.is_le)
+                    elif how == "S":
+                        act(near, p, AF.Silu, -2.0 ** 27, 2.0 ** -8)
+                    else:
+                        ts(near, p, BIG, OP.add, BIG, OP.is_equal)
+                apart[0] = True
                 for a in range(8):
-                    p = b("psC%d" % m, 8 * bk + a, 384, 48)
-                    mm(p, b("big", lo + a, lo + BLK, 8), b("bi8", 0, 8), True, not both, a > 0)
+                    p = b("psC%d" % m, 8 * bk + a, 8 * SEG, SEG)
+                    mm(p, b("big", lo + a, lo + BLK, 8), b("bis" if how == "S" else "bi8", 0, 8), True, not both, a > 0)
                     if both:
                         mm(p, b("big", over + a, over + BLK, 8), b("bi8", 0, 8), False, True)
-        tail = TILE
+                apart[0] = False
 
-        ends, folded = [], nets[:FOLD[t]]
-        for part in range(2):
-            home = b(*landing(t, part))
+        if t in EAGER:
+            follows.update({i: gathered for i in range(tested, len(calls)) if calls[i][0] == "v"})
+        if t in SUMMED:
+            follows.update({i: members[-1] for i in range(tested, len(calls)) if calls[i][0] == "s"})
+            follows.update(zip(members[1:], members))
 
-            def fold(part=part, home=home):
-                at, name = BLK * (2 * t + part), "%d%d" % (t, part)
+        for piece, (part, lo, hi) in enumerate(folds(t)):
+            home = b("pE", 4096 + BLK * part + lo, 4096 + BLK * part + hi)
+            folded = [b("big", x[2] + lo, x[2] + hi) for x in nets[:FOLD[t][part]]]
+
+            def fold(piece=piece, part=part, home=home, folded=folded):
+                at, name = 2 * BLK * t + home[2] - 4096, "%d%d" % (t, piece)
                 waits("g", folded, [home])
                 g.remote_dma_fused([RemoteDMATransfer(dst_ids=[DstId(rid=hrid, pnc=hpid)], dma_engine_mask=there, remote_sem=T.sem["h" + name],
-                                                      srcs=[x[0] for x in folded], dsts=[T.big[:, at:at + BLK]], alu_op=2 + part)],
+                                                      srcs=[x[0] for x in folded], dsts=[T.big[:, at:at + home[4]]], alu_op=2 + part)],
                                    local_sem=T.sem["lf%d" % t])
                 count["b" + name] = popcount(back)
                 note(home, True, "b" + name, count["b" + name], "net")
-                count["lf%d" % t] = 2 * popcount(there)
-                note(b("big", OP_, OP_ + BLK * FOLD[t]), False, "lf%d" % t, count["lf%d" % t], "net")
+                count["lf%d" % t] = len(folds(t)) * popcount(there)
+                note(b("big", OP_, OP_ + BLK * FOLD[t][part]), False, "lf%d" % t, count["lf%d" % t], "net")
 
             in_turn()
-            remote(fold, folded + [lent], [home], 5.5, 0.8 * FOLD[t])
-            mask, keep, take = (b("mkx", 0, BLK), OP.min, OP.max) if part == 0 else (b("mkn", 0, BLK), OP.max, OP.min)
+            remote(fold, folded + [lent], [home], 4.7 + 0.8 * (hi - lo) / BLK, SOURCE * len(folded) * (hi - lo) / BLK)
+        ends = []
+        for part in range(2):
+            mask, keep, take = ("mkx", OP.min, OP.max) if part == 0 else ("mkn", OP.max, OP.min)
             end = None
-            for k, x in enumerate(nets[FOLD[t]:] + [home]):
-                lo = BLK * (2 + 2 * k + part)
-                scan(b("pE", lo, lo + BLK), mask, x, keep, take)
+            for k, x in enumerate(nets[FOLD[t][part]:] + [None]):
+                name, lo = ("wg%d" % part, BLK * k) if x else ("pE", 6144 + BLK * part)
+                if x:
+                    scan(b(name, lo, lo + BLK), b(mask, 0, BLK), x, keep, take)
+                else:
+                    for x, y in [f[1:] for f in folds(t) if f[0] == part]:
+                        scan(b(name, lo + x, lo + y), b(mask, x, y), b(name, lo + x - 2048, lo + y - 2048), keep, take)
                 if end:
-                    tt(b("mx", 128 * part, 128 * part + 128), end, b("pE", lo + 7, lo + BLK, 8), take)
-                end = b("mx", 128 * part, 128 * part + 128) if end else b("pE", lo + 7, lo + BLK, 8)
+                    tt(b("mx", 128 * part, 128 * part + 128), end, b(name, lo + 7, lo + BLK, 8), take)
+                end = b("mx", 128 * part, 128 * part + 128) if end else b(name, lo + 7, lo + BLK, 8)
             ends.append(end)
 
-        m0, m1 = b("am0", 47, 384, 48), b("am1", 47, 384, 48)
-        ts(b("thr", 0, 8), b("psC0", 384, 392), 4143.5, OP.is_lt, 11.5, OP.mult)
-        ts(b("thr", 16, 24), b("psC1", 384, 392), 4143.5, OP.is_lt)
+        free = [BLK * ((turn + k // 2) % 3) + 512 * (k % 2) for k in range(6)]
+        wnew = b("psT", free[0], free[0] + 256)
+        mm(wnew, b("none", 0, 128, 1, 1), cst(256), True, False, False, True)
+        mm(wnew, ident, woff, False, False, True, True)
         for m in range(2):
-            scan(b("am%d" % m, 0, 384), b("amk", 0, 384), b("psC%d" % m, 0, 384), OP.min, OP.max)
-        tt(b("xs", 16, 24), m0, b("thr", 0, 8), OP.is_lt)
-        ts(b("xs", 0, 8), m0, 11.5, OP.is_lt)
-        ts(b("thr", 8, 16), m0, 11.5, OP.is_ge, 11.5, OP.mult)
-        tt(b("thr", 24, 32), b("thr", 8, 16), b("thr", 16, 24), OP.mult)
-        tt(b("xs", 8, 16), m1, b("thr", 8, 16), OP.is_lt)
-        tt(b("xs", 24, 32), m1, b("thr", 24, 32), OP.is_lt)
-
-        for m in range(2):
-            p, lo = b("psC%d" % m, 392, 400), 768 * m
+            name = "psC%d" % m
+            scan(b("am%d" % m, 0, 8 * SEG), b("amk", 0, 8 * SEG), b(name, 0, 8 * SEG), OP.min, OP.max)
+            chosen = b("am%d" % m, SEG - 2, 8 * SEG, SEG)
+            if m == 0:
+                apart[0] = True
+                act(b("psC1", SEG - 2, 8 * SEG, SEG), chosen, AF.Copy, 23.0, -1.0)
+                apart[0] = False
+            ts(b("xs", 16 + 8 * m, 24 + 8 * m), b("am%d" % m, SEG - 1, 8 * SEG, SEG), 11.5, OP.is_lt)
+            act(b("xs", 8 * m, 8 * m + 8), chosen, AF.Sign, 11.5, -1.0)
+            p = b("psC%d" % (1 - m), 400, 408)
             mm(p, b("crep", 0, 128), b("xs", 16 + 8 * m, 24 + 8 * m), True, True)
             tt(b("bw", 8 * m, 8 * m + 8), p, b("bi8", 0, 8), OP.mult)
-            p = b(tail[0], lo, lo + 256)
-            mm(p, b("one", 0, 128, 1, 1), b("cst", 128, 384, 1, 1), True, False)
-            for ch in range(32):
-                at = SLOT[cc[m]] + 128 * ch
-                mm(b(tail[0], lo + ch, lo + 256, 32), b("rr", at, at + 128), b("bw", 8 * m, 8 * m + 8), False, ch == 31)
-            if ROUNDER[m] == "s":
-                r = b("r%d" % m, 0, 256)
+            where = [(name, 0), (name, 128)] if m == 0 or not HALVES else [(name, 0), ("psT", free[4])]
+            for part in ([0, 1],) if where[1][1] == 128 else ([0], [1]):
+                x, lo = where[part[0]]
+                p = b(x, lo, lo + 128 * len(part))
+                terms = [(b(x, where[h][1] + a, where[h][1] + 128, 16), b("rr", SLOT[cc[m]] + 256 * a + 128 * h, SLOT[cc[m]] + 256 * a + 128 * h + 128),
+                          b("bw", 8 * m, 8 * m + 8)) for h in part for a in range(16)]
+                group([(p, b("one", 0, 128, 1, 1), cst(p[4])), terms[0] + (True,)] + terms[1:], True)
+                r, mark = b("r%d" % m, 128 * part[0], 128 * part[0] + p[4]), b("mk", 256 * m + 128 * part[0], 256 * m + 128 * part[0] + p[4])
                 act(r, p, AF.Copy, 2.0 ** -9)
-            else:
-                r = b("hI", 0, 256)
-                ts(r, p, 2.0 ** -9, OP.add)
-            tt(b("mk", 256 * m, 256 * m + 256), r, p, OP.is_gt)
-        for h in range(2):
-            for m in range(2):
-                mm(b(tail[0], 256 + 128 * h, 384 + 128 * h), b("mk", 256 * m + h, 256 * m + 256, 2), id15, m == 0, m == 1)
-        p = b(tail[0], 256, 512)
-        tt(p, p, b("w2", 0, 256), OP.min)
-        red(b("smv", 0, 1), p)
-        tt(b("w1", 0, 256), p, b("wf", 0, 256), OP.add)
-        mm(b("psC0", 400, 401), b("bok", 0, 128), b("smv", 5, 6), True, False)
-        mm(b("psC0", 400, 401), b("bok", 0, 128), b("smv", 0, 1), False, True)
-        ts(b("smv", 2, 3), b("psC0", 400, 401), 128.0, OP.max, 256.5, OP.min)
-        ts(b("smv", 3, 4), b("psC0", 400, 401), 0.0, OP.is_lt, 0.5, OP.max)
-        ts(b("woff", 8, 264), b("w1", 0, 256), b("smv", 2, 3), OP.add, b("smv", 3, 4), OP.mult)
+                tt(mark, r, p, OP.is_gt)
+                for h in part:
+                    mm(b("psT", free[0] + 128 * h, free[0] + 128 * h + 128), b("mk", 256 * m + 128 * h, 256 * m + 128 * h + 128), id15,
+                       False, m + h == 2, h > part[0], True)
+        tt(b("w1", 0, 256), wnew, b("wcap", 0, 256), OP.min)
+        scan(b("ex", 0, 256), b("zeros", 0, 256), b("w1", 0, 256), OP.add, OP.add)
+        mm(b("psC0", 411, 412), boq, b("ex", 255, 256), True, True)
+        ts(b("smv", 12, 13), b("psC0", 411, 412), 7168.5 / 4096, OP.is_lt, 0.5, OP.max)
+        ts(woff, b("w1", 0, 256), b("smv", 12, 13), OP.mult, 128.25, OP.add)
 
-        xT = b("xT", 0, 128, 1, 32)
-        mm(b(tail[1], 0, 128, 1, 32), b("xs", 0, 32), ident, True, True)
-        act(xT, b(tail[1], 0, 128, 1, 32), AF.Copy, 0.0, b("sgn", 0, 1, 1, 32))
-        for m in range(2):
-            mm(b(tail[2], 128 * m, 128 * m + 128), b("em", 128 * m, 128 * m + 128, 1, 32), xT, True, True)
-        for k in range(4):
-            mm(b(tail[1], 128, 256), b("em", 128 * k, 128 * k + 128, 1, 32), xT, k == 0, k == 3)
-        total(b("a16", 0, 1), b(tail[1], 128, 256), 16.0)
+        xT, em = b("xT", 0, 128, 1, 32), [b("em", 128 * k, 128 * k + 128, 1, 32) for k in range(4)]
+        mm(b("psT", free[1], free[1] + 128, 1, 32), b("xs", 0, 32), ident, True, True)
+        act(xT, b("psT", free[1], free[1] + 128, 1, 32), AF.Identity, b("sgn", 1, 2, 1, 32), b("sgn", 0, 1, 1, 32))
+        group([(b("psT", free[1] + 128, free[1] + 256), x, xT) for x in em])
+        mm(b("psT", free[1] + 256, free[1] + 257), odd, b("one", 0, 1, 1, 1), True, True, True)
+        total(b("a16", 0, 1), b("psT", free[1] + 128, free[1] + 257), 32.0, -16.0 / FAR)
         act(b("yab", t, t + 1), b("a16", 0, 1), AF.Copy, 0.0, 0.0625)
 
+        halves = [[b("psT", free[k] + 128 * m, free[k] + 128 * m + 128) for m in range(2)] for k in (2, 3)]
         for m in range(2):
-            terms = [(n2id, zz[m]), (b("p2id", 0, 128), zh)] * (m == 1 or cut < BLK) + [(ident, x) for x in ends]
-            for k, (l, x) in enumerate(terms):
-                mm(b(tail[2], 512 + 128 * m, 640 + 128 * m), l, x, k == 0, k == len(terms) - 1)
-        for m in range(2):
-            lo, p = 128 * m, b(tail[2], 128 * m, 128 * m + 128)
-            ts(b("q01", lo, lo + 128), b(tail[2], 512 + lo, 640 + lo), 0.25, OP.mult, -0.375, OP.add)
-            tt(p, b("q01", lo, lo + 128), p, OP.mult)
-            tt(b("zo%d" % t, lo, lo + 128), zz[m], p, OP.add)
+            mm(halves[0][m], nident, zz[m], True, False, m == 1)
+            mm(halves[0][m], em[m], xT, False, True)
+        act(b("zs", 0, 256), b("psT", free[2], free[2] + 256), AF.Copy, FAR, -1.0)
+        p = b("psT", free[3], free[3] + 256)
+        group([(p, rows["3/8"], cst(256)), (halves[1][0], ident, zz[0]), (halves[1][1], hid, zz[0]), (halves[1][1], hid, zz[1]),
+               (halves[1][0], em[0], xT, True), (halves[1][1], em[1], xT)] +
+              [(halves[1][m], qid, x) + (True,) * (m == 0) for x in ends for m in range(2)] +
+              [(p, rows["1"], cst(256)), (p, rows["-1"], cst(256))], True)
+        tt(b("zo%d" % t, 0, 256), p, b("zs", 0, 256), OP.min)
         for kind in (("u0", "c0"), ("u1", "f1"), ("u2", "f2"), ("f3", "f0"))[t]:
             send(kind)
 
@@ -806,7 +926,7 @@ def rank_main(g, core, rank, cores, T, topo):
     dma("y", [(T.yz[:, 0:128], b("zf0", 0, 128))], 0.4)
 
     if not PLAN:
-        PLAN.extend(plan(calls))
+        PLAN.extend(plan(calls, follows))
     for i in PLAN:
         for issue in calls[i][1]:
             issue()

import numpy as np
from concourse.bass import DstId, RemoteDMATransfer
from concourse.mybir import dt, AluOpType, AxisListType, ActivationFunctionType

OP = AluOpType
AF = ActivationFunctionType
NR = 8
ROUNDS = 4
BLK = 1024
WIN = 16384
OP_, OI0, OI1, OI2 = 20480, 4096, 10240, 26624
BIG = 1.5 * 2.0 ** 34
ROUND = 1.5 * 2.0 ** 23
SEG = 50
FAR = 512.0
FILLS = 4
CUTS = ((0, 2, 4, 6, 8), (0, 2, 4, 6, 8), (0, 1, 2, 3, 4, 5, 6, 7, 8), (0, 1, 2, 3, 4, 5, 6, 7, 8))
FIRST = 11.0
TAKEN = ((1, 6),)
WEIGHT = (1.5, 1.0, 1.2, 1.0)
SHARE = 5
TESTS = ("DTDTDTDTASAS", "ASASASATASAS", "ASASASATASAS", "ASASASATASAS")
FOLD = ((5, 6), (5, 6), (5, 6), (4, 5))
SHARES = ((1, 2), (1, 2), (1, 2), (1, 2))
SOURCE = 0.6
FILLED = ("2^16", "-2^16", "2048", "3/8")
REPEATER = "gggg"
EAGER = (0, 1, 2, 3)
SUMMED = ()
MEMBERS = ("ssssssss", "ssssssss", "ssssssss", "ssssssss")
CYCLE, COLUMN = np.array([0.83e-3, 0.85e-3, 1.05e-3, 0.95e-3]), np.array([0.44e-3, 0.44e-3, 0.55e-3, 0.52e-3])
GATHER, SCATTER = np.array([1.15, 1.5, 1.6, 1.9]), np.array([2.0, 2.8, 4.6, 2.2])
CALL, WAKE = {"v": 0.06, "s": 0.1, "t": 0.006, "g": 0.15, "y": 0.05}, 0.06
WAKES = (0.06, 0.06, 0.12, 0.1)
LOADS = "zl01w23"
HALVES = False
SEED = 6
SWAPS = 60000
SLACK = 0.0015
SHAKE = 8.0
REACH = 12.0
STRIDE = 40
ASIDE = 4
MEAN = 0.2
PASSES = 30
CASES = (0, 1, 2, 3)

MSG = [
    ("i01", "z0s", 0, 256, -1, "zin0", 0), ("i2", "z0s", 256, 384, -2, "zin1", 1), ("i3", "z0s", 384, 512, -3, "zin2", 1),
    ("u0", "zo0", 128, 256, -1, "zr1", 0), ("c0", "zo0", 0, 128, -3, "zc0", 1),
    ("u1", "zo1", 128, 256, -1, "zr2", 0), ("f1", "zo1", 0, 128, 2, "zf1", 1),
    ("u2", "zo2", 128, 256, -1, "zr3", 0), ("f2", "zo2", 0, 128, 3, "zf2", 1),
    ("f3", "zo3", 0, 128, 4, "zf3", 1), ("f0", "zo3", 128, 256, 4, "zf0", 0)]

_B, _F, _I, _U, _H = "bfloat16", "float32", "int32", "uint16", "float16"
SCRATCH = {}
for _n, _w, _d in [
        ("big", 32768, _B), ("ptb", 4112, _B), ("diffp", 4096, _B), ("pE", 8192, _B), ("zeros", 1024, _B),
        ("wg0", 4096, _B), ("wg1", 4096, _B), ("rf", 8192, _F), ("vals", 2048, _F), ("rr", 12288, _B),
        ("ind", 1024, _B), ("mkx", 1024, _B), ("mkn", 1024, _B), ("amk", 8 * SEG, _B),
        ("lmI", 1024, _I), ("lm16", 1024, _U), ("pat", 256, _F), ("mI", 8, _I), ("aF", 8, _F),
        ("zero", 128, _B), ("one", 128, _B), ("none", 128, _B), ("ident", 128, _B), ("nident", 128, _B), ("id15", 128, _B),
        ("hid", 128, _B), ("qid", 128, _B), ("zrep", 1024, _B), ("row", 1536, _B), ("kc", 8, _B),
        ("bo32", 128, _B), ("boq", 128, _B), ("lt32", 128, _B), ("lth", 128, _B), ("one32", 8, _F),
        ("bi8", 8, _B), ("bis", 8, _B), ("rs8", 8, _B), ("sgn", 8, _F),
        ("cst", 512, _B), ("lane", 64, _B), ("crep", 128, _B), ("em", 512, _B), ("bw", 16, _B),
        ("kl", 768, _F), ("uw", 24, _B), ("uu", 128, _F), ("dA", 128, _B),
        ("m128", 272, _B), ("wt", 256, _B), ("woff", 272, _B), ("ex", 264, _H), ("yy", 256, _F), ("off16", 256, _U),
        ("wcap", 256, _B), ("mk", 512, _B), ("w1", 256, _B), ("r0", 256, _B), ("r1", 256, _B),
        ("smv", 16, _F), ("a16", 8, _F), ("yab", 4, _F), ("ywb", 256, _F),
        ("jk", 136, _B), ("zT", 256, _B), ("hI", 256, _I), ("pos16", 384, _U),
        ("am0", 8 * SEG, _B), ("am1", 8 * SEG, _B), ("xs", 32, _B), ("xT", 128, _B), ("zs", 256, _B), ("mx", 256, _B),
        ("z0s", 512, _B), ("zin0", 256, _B), ("zin1", 128, _B), ("zin2", 128, _B), ("zr1", 128, _B), ("zr2", 128, _B),
        ("zr3", 128, _B), ("zc0", 128, _B), ("zf1", 128, _B), ("zf2", 128, _B), ("zf3", 128, _B), ("zf0", 128, _B),
        ("zo0", 256, _B), ("zo1", 256, _B), ("zo2", 256, _B), ("zo3", 256, _B)]:
    SCRATCH[_n] = ("sbuf", [128, _w], _d)
for _m in MSG:
    SCRATCH["y_" + _m[0]] = ("sbuf", [128, _m[3] - _m[2]], _B)
TILE = ("psA", "psB", "psD")
for _n, _w in [("psT", 3072), ("psC0", 512), ("psC1", 512)]:
    SCRATCH[_n] = ("psum", [128, _w], _F)

SEMAPHORES = ["kv", "ks", "kt", "kg", "ls"] + ["d%d" % i for i in range(40)] + ["m_" + m[0] for m in MSG] + ["q_" + m[0] for m in MSG]
SEMAPHORES += [x + "%d%d" % (t, part) for x in "hb" for t in range(ROUNDS) for part in range(sum(SHARES[t]))]
SEMAPHORES += ["hz"] + ["lf%d" % t for t in range(ROUNDS)] + [x + "%d" % t for x in ("hz", "ba", "bb") for t in range(ROUNDS - 1)]
PLAN = []


def relay_of(src, dst, which, T, topo):
    if topo.may_write(src, dst):
        return None
    c = [x for x in topo.cores_of(src) if x != src and T.rank_of(x) is None and topo.may_write(x, dst) and topo.may_write(src, x)]
    near = [x for x in c if topo.die(x) == topo.die(src)]
    c = near if near else c
    return c[which % len(c)]


def helpers_of(src, cores, T, topo):
    busy = [x for x in topo.cores_of(src) if all(topo.may_write(x, y) for y in cores if y != x)]
    idle = [x for x in topo.cores_of(src) if T.rank_of(x) is None and x not in busy]
    return sorted(idle, key=lambda x: topo.die(x) != topo.die(src))[:2]


def folds(t):
    return [(part, lo, lo + BLK // SHARES[t][part]) for part in range(2) for lo in range(0, BLK, BLK // SHARES[t][part])]


def mask_for(src, dst, far_src, far_dst, topo):
    m = 0
    ok = topo.engines(src, dst)
    for e in topo.engines(far_src, far_dst):
        if e in ok:
            m |= 1 << e
    return m


def popcount(m):
    return bin(m).count("1")


def rank_program(g, core, T, topo):
    rank = T.rank_of(core)
    cores = list(T.cores)
    if rank is not None:
        rank_main(g, core, rank, cores, T, topo)
        return
    sent = 0
    for src in cores:
        pair = helpers_of(src, cores, T, topo)
        if core in pair:
            rid, pid = topo.addr(src, core)
            g.wait_ge(T.sem.hz, popcount(topo.mask(src, core)))
            g.sync.wait_ge(T.sem.hz, popcount(topo.mask(src, core)))
            for k in range(4):
                g.sync.dma_start(T.pE[:, BLK * k:BLK * k + BLK], T.zeros[:]).then_inc(T.sem.d0, 16)
            g.wait_ge(T.sem.d0, 64)
            half = WIN * pair.index(core)
            for t in range(ROUNDS):
                if t < ROUNDS - 1:
                    g.wait_ge(T.sem["hz%d" % t], 1)
                    g.remote_dma(T.big[:, half:half + 4096], T.pE[:, 0:4096], T.sem["b%s%d" % ("ab"[pair.index(core)], t)], T.sem.ls,
                                 pid, rid, topo.mask(core, src))
                    sent += popcount(topo.mask(core, src))
                for piece, (part, lo, hi) in enumerate(folds(t) if core == pair[0] else []):
                    at, to, name = BLK * (2 * t + part), 4096 + BLK * part, "%d%d" % (t, piece)
                    g.wait_ge(T.sem["h" + name], popcount(topo.mask(src, core)))
                    g.remote_dma(T.pE[:, to + lo:to + hi], T.big[:, at + lo:at + hi], T.sem["b" + name], T.sem.ls, pid, rid,
                                 topo.mask(core, src))
                    sent += popcount(topo.mask(core, src))
    for kind, sbuf, lo, hi, off, land, which in MSG:
        for r in range(NR):
            src, dst = cores[r], cores[(r + off) % NR]
            if relay_of(src, dst, which, T, topo) == core:
                m = mask_for(core, dst, core, dst, topo)
                g.wait_ge(T.sem["q_" + kind], popcount(mask_for(src, core, core, dst, topo)))
                rid, pid = topo.addr(dst, core)
                g.remote_dma(T[land][:], T["y_" + kind][:], T.sem["m_" + kind], T.sem.ls, pid, rid, m)
                sent += popcount(m)
    if sent:
        g.wait_ge(T.sem.ls, sent)


def plan(calls, follows):
    n = len(calls)
    before, after, seen, soft = [set() for _ in calls], [[] for _ in calls], {}, set()
    for i, c in enumerate(calls):
        for write, xs in ((False, c[2]), (True, c[3])):
            for x in xs:
                for lo, hi, wr, j in seen.get(x[1], []):
                    if lo < x[3] and x[2] < hi and (wr or write) and j != i and not (wr and write and c[6] and calls[j][6]):
                        before[i].add(j)
        for write, xs in ((False, c[2]), (True, c[3])):
            for x in xs:
                old = [e for e in seen.get(x[1], []) if not (write and not c[6] and x[2] <= e[0] and e[1] <= x[3])]
                seen[x[1]] = old + [(x[2], x[3], write, i)]
        before[i] -= {k for j in before[i] if not calls[j][5] + calls[j][7] for k in before[j] if not calls[k][5] + calls[k][7]}
        if i in follows and follows[i] not in before[i]:
            before[i].add(follows[i])
            soft.add((follows[i], i))
        for j in before[i]:
            after[j].append(i)
    times = [[float((c[4] + 0.0 * CYCLE)[case]) for c in calls] for case in range(len(CYCLE))]
    way = [0.0] * n
    for i in range(n - 1, -1, -1):
        way[i] = times[1][i] + calls[i][5] + max([way[k] + WAKE for k in after[i]], default=0.0)
    banks = [sorted({(x[1], k) for x in c[2] + c[3] if x[1].startswith("ps") for k in range(x[2] // 512, (x[3] - 1) // 512 + 1)})
             for c in calls]

    def gap(j, k):
        return 0.0 if calls[k][0] == "-" or calls[j][0] == calls[k][0] == "t" or (j, k) in soft else WAKE + late[j]

    late = [c[5] + c[7] for c in calls]
    edges = [[(j, gap(j, i) > 0.0) for j in sorted(before[i])] for i in range(n)]

    rooms_of = sorted({k for x in banks for k in x})
    facts = [("vstgy-".index(c[0]), [j for j, waits in edges[i] if waits], [j for j, waits in edges[i] if not waits],
              [6 + rooms_of.index(k) for k in banks[i]], c[5], c[7]) for i, c in enumerate(calls)]

    def replay(order, case, old=None, start=0):
        time, wake = times[case], WAKES[case]
        if old is None:
            done, seen, cause, marks = [0.0] * n, [0.0] * n, [-1] * n, []
            free, engines, start = [(0.0, -1, -1)] * (6 + len(rooms_of)), (0.0, -1), 0
        else:
            start = start // STRIDE
            done, seen, cause, marks = old[1][:], old[2][:], old[3][:], old[4][:start]
            free, engines = old[4][start]
            free, start = free[:], start * STRIDE
        for lo in range(start, n, STRIDE):
            marks.append((free[:], engines))
            for i in order[lo:lo + STRIDE]:
                q, hard, easy, held, away, busy = facts[i]
                at, why, who = free[q]
                for j in hard:
                    if seen[j] >= at:
                        at, why = seen[j], j
                for j in easy:
                    if done[j] >= at:
                        at, why = done[j], j
                for k in held:
                    x = free[k]
                    if x[0] > at and x[2] != q:
                        at, why = x[0], x[1]
                done[i] = at = at + time[i]
                free[q] = (at, i, q)
                if busy:
                    if engines[0] > at:
                        why, at = engines[1], engines[0]
                    at += busy
                    engines = (at, i)
                cause[i] = why
                seen[i] = at = at + away + wake
                for k in held:
                    free[k] = (at, i, q)
        last = max(order[-24:], key=lambda i: seen[i])
        return seen[last] + MEAN * sum(seen) / n, done, seen, cause, marks, last

    def sweep(forward, rank, times):
        pre, post = (before, after) if forward else (after, before)
        done, busy, left, placed = [0.0] * n, {}, [len(x) for x in pre], []
        ready = {i: 0.0 if forward else late[i] for i in range(n) if not left[i]}
        while ready:
            i = max(ready, key=lambda k: (rank[k], -k))
            at, time, moved = ready.pop(i), times[i], True
            rooms = [busy.setdefault(k, []) for k in banks[i] + [calls[i][0]]]
            while moved:
                moved = False
                for room in rooms:
                    k = len(room)
                    while k and room[k - 1][1] > at:
                        k -= 1
                    while k < len(room) and room[k][0] < at + time:
                        at, moved, k = room[k][1], True, k + 1
            done[i] = at + time
            for room in rooms:
                k = len(room)
                while k and room[k - 1][0] > at:
                    k -= 1
                room.insert(k, (at, done[i]))
            placed.append((at, len(placed), i))
            for k in post[i]:
                left[k] -= 1
                if not left[k]:
                    ready[k] = max(done[j] + (gap(j, k) if forward else gap(k, j)) for j in pre[k])
        return [i for at, k, i in sorted(placed)], done

    share = [w / sum(x) for w, x in zip(WEIGHT, times)]

    def worth(order):
        return sum(share[case] * replay(order, case)[0] for case in range(len(times)))

    best, seed = None, SEED
    for k in range(PASSES):
        for _ in range(2):
            order, done = sweep(True, way, times[CASES[k % len(CASES)]])
            span = worth(order)
            way = sweep(False, done, times[CASES[k % len(CASES)]])[1]
            if best is None or span < best[0]:
                best = (span, order, way)
        way, lo = [], max(best[2]) * (k * 0.382 % 1.0)
        for x in best[2]:
            seed = (seed * 1103515245 + 12345) % 2 ** 31
            way.append(x + SHAKE * (seed / 2 ** 31 - 0.5) * (abs(x - lo) < REACH))

    def chain(state):
        pairs, i, cause = [], state[5], state[3]
        while cause[i] >= 0:
            if cause[i] not in before[i]:
                pairs.append((cause[i], i))
            i = cause[i]
        return pairs

    cases = range(len(times))
    now = best
    states = [replay(now[1], case) for case in cases]
    chains = [chain(x) for x in states]
    for k in range(SWAPS):
        order, case, slack = now[1], k % len(times), SLACK * (1.0 - k / SWAPS)
        pairs = chains[case]
        seed = (seed * 1103515245 + 12345) % 2 ** 31
        j, i = pairs[(seed >> 8) % len(pairs)]
        if (seed >> 3) % 16 < ASIDE:
            i = (seed >> 8) % n
            j = states[case][3][i]
            if j < 0 or j in before[i]:
                continue
        a, z = order.index(j), order.index(i)
        between = order[a:z + 1]
        if seed >> 7 & 1:
            ahead = {i}
            for x in reversed(between):
                if x in ahead:
                    ahead |= before[x]
        else:
            behind = {j}
            for x in between:
                if x in behind:
                    behind.update(after[x])
            ahead = set(between) - behind
        if j in ahead or i not in ahead:
            continue
        order = order[:a] + [x for x in between if x in ahead] + [x for x in between if x not in ahead] + order[z + 1:]
        first = replay(order, case, states[case], a)
        if share[case] * (first[0] - states[case][0]) > slack:
            continue
        tried = [first if x == case else replay(order, x, states[x], a) for x in cases]
        span = sum(share[x] * tried[x][0] for x in cases)
        if span < now[0] + slack:
            now, states, chains = (span, order), tried, [chain(x) for x in tried]
            if span < best[0]:
                best = now
    return best[1]


def rank_main(g, core, rank, cores, T, topo):
    Q = {"v": g.vector, "s": g.scalar, "t": g.tensor, "g": g, "y": g.sync}
    SEMOF = {"v": "kv", "s": "ks", "t": "kt", "g": "kg"}
    count = {"ls": 0}
    waited = {q: {} for q in Q}
    hist = {}
    nd = [0, 0]
    calls, follows = [], {}
    apart = [False]

    def need(q, name, lo, hi, write, toks, loose):
        ps = name.startswith("ps")
        for (l, h, wr, sem, val, qq) in hist.get(name, []):
            if qq == q and qq in SEMOF:
                if not (l < hi and lo < h) or not (wr or write) or (ps and q == "t") or (write and wr and loose):
                    continue
            elif ps:
                if l // 512 > (hi - 1) // 512 or lo // 512 > (h - 1) // 512:
                    continue
            elif not (l < hi and lo < h) or not (wr or write) or (write and wr and loose):
                continue
            if toks.get(sem, 0) < val:
                toks[sem] = val

    def note(x, write, sem, val, q, loose=False):
        name, lo, hi = x[1:4]
        L = hist.get(name, [])
        if write:
            L = [e for e in L if not (lo <= e[0] and e[1] <= hi and (e[5] == q or not loose))]
        else:
            L = [e for e in L if not (not e[2] and e[5] == q and q in SEMOF and lo <= e[0] and e[1] <= hi)]
        L.append((lo, hi, write, sem, val, q))
        hist[name] = L

    def waits(q, reads, writes, loose=False):
        toks = {}
        for x in reads:
            need(q, x[1], x[2], x[3], False, toks, loose)
        for x in writes:
            need(q, x[1], x[2], x[3], True, toks, loose)
        for sem, val in toks.items():
            if waited[q].get(sem, 0) < val:
                Q[q].wait_ge(T.sem[sem], val)
                waited[q][sem] = val

    def b(name, lo, hi, step=1, rows=None):
        if name in TILE:
            name, lo, hi = "psT", lo + BLK * TILE.index(name), hi + BLK * TILE.index(name)
        cols = slice(lo, hi, step) if step != 1 else slice(lo, hi)
        return (T[name][:, cols] if rows is None else T[name][0:rows, cols], name, lo, hi, (hi - lo + step - 1) // step)

    def ap(x):
        return x[0] if isinstance(x, tuple) else x

    def emit(q, fn, reads, writes, time, joined=False, held=()):
        reads, writes = [x for x in reads if isinstance(x, tuple)], list(writes)
        loose = apart[0]

        def issue():
            waits(q, reads, writes, loose)
            sem = SEMOF[q]
            count[sem] = count.get(sem, 0) + 1
            fn().then_inc(T.sem[sem], 1)
            for x in reads:
                note(x, False, sem, count[sem], q)
            for x in writes:
                note(x, True, sem, count[sem], q, loose)

        if joined:
            c = calls[-1]
            assert c[0] == q
            c[1].append(issue)
            c[2:5] = [c[2] + reads, c[3] + writes + list(held), c[4] + CALL[q] + time]
        else:
            calls.append([q, [issue], reads, writes + list(held), CALL[q] + time, 0.0, loose, 0.0])

    def dma(q, pairs, busy, behind=()):
        sem = "d%d" % nd[0]
        nd[0] += 1
        reads, writes = [i for o, i in pairs if isinstance(i, tuple)] + list(behind), [o for o, i in pairs if isinstance(o, tuple)]

        def issue():
            waits(q, reads, writes)
            count[sem] = 16 * len(pairs)
            for o, i in pairs:
                Q[q].dma_start(ap(o), ap(i)).then_inc(T.sem[sem], 16)
            for x in reads:
                note(x, False, sem, count[sem], q + "dma")
            for x in writes:
                note(x, True, sem, count[sem], q + "dma")

        calls.append([q, [issue], reads, writes, 1.0 if q == "g" else CALL[q], 1.7, False, busy])

    def remote(issue, reads, writes, late, busy):
        calls.append(["g", [issue], reads, writes, 0.3 if nd[1] else 2.3, late, False, busy])
        nd[1] += 1

    def narrow(*xs):
        return 0.5 if all(SCRATCH[x[1]][2] in (_B, _U, _H) for x in xs) else 1.0

    def cycles(k):
        return max(k, 64) * CYCLE

    def tt(o, x, y, op):
        emit("v", lambda: g.vector.tensor_tensor(o[0], x[0], y[0], op), [x, y], [o], cycles(o[4] * (1 if "ps" in (x[1][:2], y[1][:2]) else 2)))

    def ts(o, x, s1, op0, s2=None, op1=None):
        if op1 is None:
            emit("v", lambda: g.vector.tensor_scalar(o[0], x[0], ap(s1), None, op0), [x, s1], [o], cycles(o[4] * narrow(o, x)))
        else:
            emit("v", lambda: g.vector.tensor_scalar(o[0], x[0], ap(s1), ap(s2), op0, op1), [x, s1, s2], [o], cycles(o[4] * narrow(o, x)))

    def cp(o, x):
        emit("v", lambda: g.vector.tensor_copy(o[0], x[0]), [x], [o], cycles(o[4] * narrow(o, x)))

    def ms(o, c, behind=()):
        emit("v", lambda: g.vector.memset(o[0], c), list(behind), [o], cycles(o[4] * narrow(o)))

    def red(o, x):
        emit("v", lambda: g.vector.tensor_reduce(o[0], x[0], AxisListType.X, OP.add), [x], [o], cycles(x[4]))

    def scan(o, d0, d1, op0, op1):
        emit("v", lambda: g.vector.tensor_tensor_scan(o[0], d0[0], d1[0], 0.0, op0, op1), [d0, d1], [o], cycles(o[4] * narrow(o, d0, d1)))

    def act(o, x, func, bias=0.0, scale=1.0):
        emit("s", lambda: g.scalar.activation(o[0], x[0], func, bias=ap(bias), scale=ap(scale)), [x, scale, bias], [o], o[4] * CYCLE)

    def total(o, x, bias, scale):
        j = b("jk", 0, x[4])
        emit("s", lambda: g.scalar.activation(j[0], x[0], AF.Copy, bias=bias, scale=scale, accum_out=o[0]), [x], [j, o], x[4] * CYCLE)

    def mm(o, l, r, start, stop, joined=False, held=False):
        bank = [(None, o[1], o[2] // 512 * 512, o[2] // 512 * 512 + 512)] if held else []
        emit("t", lambda: g.tensor.matmul(o[0], l[0], r[0], start, stop), [l, r], [o],
             max(64, r[4]) * COLUMN * (4 if SCRATCH[l[1]][2] == _F else 1), joined or not (start or held), bank)

    def group(terms, held=False):
        for k, x in enumerate(terms):
            mm(x[0], x[1], x[2], k == 0, k == len(terms) - 1, k > 0 and len(x) == 3, held)

    def asel(o, i, pattern, op, base, cm, fill=0.0):
        emit("g", lambda: g.affine_select(o[0], i[0], pattern, op, fill, base, cm), [i], [o], 2 * o[4] * CYCLE)

    def iota(o, pattern, base, cm, flag=True):
        if flag:
            emit("g", lambda: g.iota(o[0], pattern, base, cm, allow_small_or_imprecise_dtypes=True), [], [o], 2 * o[4] * CYCLE)
        else:
            emit("g", lambda: g.iota(o[0], pattern, base, cm), [], [o], 2 * o[4] * CYCLE)

    def gath(q, o, win, off):
        if q == "s":
            emit("s", lambda: g.scalar.activation(o[0], win[0].indirect(off[0]), AF.Copy), [win, off], [o], o[4] * GATHER * CYCLE)
        else:
            emit("v", lambda: g.vector.tensor_copy(o[0], win[0].indirect(off[0])), [win, off], [o], o[4] * GATHER * CYCLE)

    for kind, sbuf, lo, hi, off, land, which in MSG:
        src = cores[(rank - off) % NR]
        rel = relay_of(src, core, which, T, topo)
        far = src if rel is None else rel
        count["m_" + kind] = popcount(mask_for(far, core, far, core, topo))
        note(b(land, 0, hi - lo), True, "m_" + kind, count["m_" + kind], "net")

    def send(kind):
        k, sbuf, lo, hi, off, land, which = [m for m in MSG if m[0] == kind][0]
        dst = cores[(rank + off) % NR]
        rel = relay_of(core, dst, which, T, topo)
        src = b(sbuf, lo, hi)

        def issue():
            waits("g", [src], [])
            if rel is None:
                m, to, out, sem = mask_for(core, dst, core, dst, topo), dst, T[land][:], "m_" + kind
            else:
                m, to, out, sem = mask_for(core, rel, rel, dst, topo), rel, T["y_" + kind][:], "q_" + kind
            rid, pid = topo.addr(to, core)
            g.remote_dma(out, src[0], T.sem[sem], T.sem.ls, pid, rid, m)
            count["ls"] += popcount(m)

        remote(issue, [src], [b(land, 0, hi - lo)], FIRST if kind[0] == "i" else 5.5, 0.8)

    helper, sweeper = helpers_of(core, cores, T, topo)
    hrid, hpid = topo.addr(helper, core)
    aides = [DstId(rid=topo.addr(x, core)[0], pnc=topo.addr(x, core)[1]) for x in (helper, sweeper)]
    there, back = topo.mask(core, helper), topo.mask(helper, core)

    zero, one = b("zero", 0, 128), b("one", 0, 128)
    ident, nident, id15, none = b("ident", 0, 128), b("nident", 0, 128), b("id15", 0, 128), b("none", 0, 128)
    hid, qid, boq = b("hid", 0, 128), b("qid", 0, 128), b("boq", 0, 128)
    loads = {"w": (b("wt", 0, 256), T.w0[:], 0.5), "l": (b("lmI", 0, 256), T.lm[:, 0:256], 0.7), "z": (b("z0s", 0, 256), T.z0[:, 0:256], 0.5)}
    for k in range(4):
        loads[str(k)] = (b("ptb", 16 + 1024 * k, 1040 + 1024 * k), T.pt[:, 1024 * k:1024 * k + 1024], 1.05)
    for k, x in enumerate(LOADS):
        if k:
            follows[len(calls)] = len(calls) - 1
        dma("y", [loads[x][:2]], loads[x][2])
    dma("y", [(b("lmI", 256, 512), T.lm[:, 256:512])], 0.7, [b("ptb", 16, 4112)])
    dma("y", [(b("z0s", 256, 512), T.z0[:, 256:512]), (b("lmI", 512, 1024), T.lm[:, 512:1024])], 1.5, [b("lmI", 256, 512)])
    iota(b("mI", 0, 1), [[0, 1]], 0, 1, False)
    iota(b("pat", 0, 256), [[1, 16], [0, 16]], 0, 0)
    iota(zero, [[0, 128]], 0, 0)
    ts(b("mI", 0, 1), b("mI", 0, 1), 15, OP.bitwise_and)
    cp(b("aF", 0, 1), b("mI", 0, 1))
    ts(b("vals", 0, 256), b("pat", 0, 256), b("aF", 0, 1), OP.is_equal, 2.0 ** 13, OP.mult)
    for k in range(3):
        act(b("vals", 256 << k, 512 << k), b("vals", 0, 256 << k), AF.Copy, 0.0, 0.5 ** (1 << k))
    ms(b("ptb", 0, 16), 0.0)
    ms(b("m128", 0, 272), -128.0)
    ms(b("woff", 0, 8), 128.0)
    ms(b("cst", 0, 512), 128.0)
    ms(one, 1.0)
    ms(b("zeros", 0, BLK), 0.0)
    parts = [WIN * (k // 4) + BLK * (k % 4) for k in range(8)]
    for lo in parts[:8 - FILLS:2]:
        ms(b("big", lo, lo + 2 * BLK), 0.0, [b("vals", 0, 256)])
    if FILLS:
        dma("y", [(b("big", lo, lo + BLK), b("zeros", 0, BLK)) for lo in parts[8 - FILLS:]], 0.8 * FILLS, [b("ptb", 16, 4112)])

    asel(ident, zero, [[-1, 128]], OP.not_equal, 0, 1, 1.0)
    asel(nident, zero, [[-1, 128]], OP.not_equal, 0, 1, -1.0)
    asel(b("lt32", 0, 128), one, [[-16, 8], [0, 16]], OP.is_ge, 0, 1)
    asel(b("bo32", 0, 128), b("lt32", 0, 128), [[16, 8], [0, 16]], OP.is_ge, 15, -1)
    asel(b("lt32", 0, 128), b("bo32", 0, 128), [[1, 128]], OP.is_ge, -1, -1)
    asel(b("lth", 0, 128), b("lt32", 0, 128), [[-1, 128]], OP.not_equal, 0, 1, 0.5)
    act(boq, b("bo32", 0, 128), AF.Copy, 0.0, 2.0 ** -12)
    for kind in ("i01", "i2", "i3"):
        send(kind)

    rows = {}

    def row(name, first, second=None):
        k = 1 if second is None else 2
        rows[name] = x = b("row", 128 * len(rows), 128 * len(rows) + 128, 1, k)
        if name in FILLED:
            ms(x, float(first if k == 1 else second))
            if k == 2:
                ms(b("row", x[2], x[3], 1, 1), float(first))
        elif first == int(first) and abs(first) < 2 ** 23:
            iota(x, [[0, 128]], int(first), 0 if k == 1 else int(second - first))
        elif k == 1:
            asel(x, b("zero", 0, 128, 1, 1), [[0, 128]], OP.is_gt, 0, 0, first)
        else:
            iota(x, [[0, 128]], int(second), 0)
            asel(x, x, [[0, 128]], OP.not_equal, 0, 1, first)

    def cst(k, rows=1):
        return b("cst", 0, k, 1, rows)

    asel(b("kc", 0, 1, 1, 1), b("zero", 0, 1, 1, 1), [[0, 1]], OP.is_gt, 0, 0, -2.0 ** -13)
    iota(b("kc", 2, 3, 1, 1), [[0, 1]], int(ROUND / 2048), 0)
    row("mid", 255 * 256)
    row("lanes-", -1952, -1)
    row("lanes+", 1952, -15)
    row("2^16", 1.5 * 2.0 ** 32)
    row("-2^16", -1.5 * 2.0 ** 32)
    row("16", 1.5 * 2.0 ** 20)
    row("sum", -4096, -36)
    row("2048", 2.0 ** 28, -16)
    row("1", ROUND / 128)
    row("-1", -ROUND / 128)
    row("3/8", -3.0 / 1024)
    odd = b("row", 1408, 1536, 1, 1)
    iota(odd, [[0, 8], [int(-61 * FAR), 2], [0, 8]], int(2 * FAR), 0)
    iota(b("lane", 0, 64, 1, 2), [[1, 64]], 0, 0)
    asel(b("lane", 0, 64, 1, 2), b("lane", 0, 64, 1, 2), [[0, 64]], OP.not_equal, -1, 1, 0.5)
    iota(none, [[0, 128]], -1, 0)
    uw = b("uw", 1, 17, 2)
    iota(b("uw", 0, 18), [[0, 18]], 0, 0)
    iota(uw, [[-32, 8]], 1, 2)
    asel(uw, uw, [[-32, 8]], OP.is_ge, 1, 2)
    asel(uw, uw, [[32, 8]], OP.is_ge, 30, -2)
    kl = b("kl", 0, 768, 1, 16)
    iota(kl, [[40, 6], [0, 16], [5, 8]], 17, 0)
    asel(kl, kl, [[0, 6], [-1, 16], [0, 8]], OP.is_equal, 0, 1)

    def lend_zeros():
        waits("g", [b("zeros", 0, BLK)], [])
        g.remote_dma_fused([RemoteDMATransfer(dst_ids=aides, dma_engine_mask=there, remote_sem=T.sem.hz, srcs=[T.zeros[:]],
                                              dsts=[T.zeros[:], T.zeros[:]])], local_sem=T.sem.ls)
        count["ls"] += popcount(there)

    lent = (None, "lent", 0, 1)
    swept = (None, "swept", 0, 1)
    remote(lend_zeros, [b("zeros", 0, BLK)], [swept], 8.0, 2.0)

    def in_turn():
        calls.append(["-", [], [], [lent], 0.0, 0.0, False, 0.0])

    asel(b("ind", 0, BLK), b("zeros", 0, BLK), [[-1, 128], [0, 8]], OP.not_equal, 0, 1, -15.0)
    asel(id15, zero, [[-1, 128]], OP.not_equal, 0, 1, 15.0)
    asel(b("rs8", 0, 8), b("zero", 0, 8), [[-16, 8]], OP.not_equal, 0, 1, 1.0)
    iota(b("mkx", 0, 256), [[0, 32], [1024, 8]], -512, 0)
    iota(b("mkn", 0, 256), [[0, 32], [-1024, 8]], 512, 0)
    dma("y", [(b(x, lo, lo + 256), b(x, 0, 256)) for x in ("mkx", "mkn") for lo in range(256, BLK, 256)], 1.8)
    asel(hid, zero, [[-1, 128]], OP.not_equal, 0, 1, 0.5)
    asel(qid, zero, [[-1, 128]], OP.not_equal, 0, 1, 0.25)
    iota(b("amk", 0, 8 * SEG), [[0, 8], [16, SEG]], 0, 0)
    power = b("aF", 2, 3)
    for lo in range(8):
        asel(power, power if lo else b("aF", 0, 1), [[0, 1]], OP.is_ge, 16 * lo - 1, -1, 2.0 ** (lo - 14))
    iota(b("jk", 0, 128), [[0, 8], [1, 16]], 0, 0)
    ts(b("crep", 0, 128), b("jk", 0, 128), b("aF", 0, 1), OP.is_equal, power, OP.mult)
    asel(b("em", 0, 512, 1, 32), b("zeros", 0, 512, 1, 32), [[-8, 4], [-1, 8], [0, 16]], OP.not_equal, 0, 1, 1.0)
    for k, (first, second) in enumerate(((-FAR / 2, FAR), (FAR / 2, 0))):
        iota(b("sgn", k, k + 1), [[0, 1]], int(first), 0)
        asel(b("sgn", k, k + 1), b("sgn", k, k + 1), [[0, 1]], OP.is_ge, 15, -1, float(second))

    act(b("bi8", 0, 8), b("bo32", 0, 128, 16), AF.Copy)
    act(b("bis", 0, 8), b("bo32", 0, 128, 16), AF.Copy, 0.0, -372.0)
    for c in range(4):
        for h in range(2):
            cp(b("lm16", 256 * c + 128 * h, 256 * c + 128 * h + 128), b("lmI", 256 * c + h, 256 * c + 256, 2))
    ts(b("woff", 8, 264), b("wt", 0, 256), 128.0, OP.add)
    mm(b("psC1", 408, 409), odd, b("one", 0, 1, 1, 1), True, True)
    act(b("a16", 0, 1), b("psC1", 408, 409), AF.Copy, 32.0, -16.0 / FAR)

    SLOT = (0, 4096, 8192, 4096)

    def narrowed(c):
        dma("g", [(b("rr", SLOT[c], SLOT[c] + 4096), b("rf", 4096 * (c % 2), 4096 * (c % 2) + 4096))], 3.5)

    for c in range(4):
        for lo, hi in zip(CUTS[c], CUTS[c][1:]):
            w, v = b("rf", 4096 * (c % 2), 4096 * (c % 2) + 4096), b("vals", 512 * (lo % 4), 512 * (lo % 4 + hi - lo))
            off = b("lm16", 256 * c + 32 * lo, 256 * c + 32 * hi)
            if (c, lo) in TAKEN:
                emit("v", lambda w=w, v=v, off=off: g.vector.tensor_copy(w[0].indirect(off[0]), v[0]), [v, off], [w], v[4] * SCATTER * CYCLE)
            else:
                emit("s", lambda w=w, v=v, off=off: g.scalar.activation(w[0].indirect(off[0]), v[0], AF.Silu), [v, off],
                     [w, (None, "class after class", 0, 1)], v[4] * SCATTER * CYCLE)
        if c < 3:
            narrowed(c)

    def prefix():
        scan(b("ex", 0, 257), b("m128", 0, 257), b("woff", 7, 264), OP.add, OP.add)
        rowsum, th, inv, q, at, half = [b("ex", 256, 257)] + [b("smv", k, k + 1) for k in (2, 4, 6, 8, 10)]
        p = b("psC0", 408, 409)
        group([(p, b("one", 0, 128, 1, 1), b("kc", 0, 1, 1, 1)), (p, boq, rowsum), (p, b("one", 0, 128, 1, 1), b("kc", 2, 3, 1, 1))])
        mm(b("psC1", 409, 410), b("lth", 0, 128), rowsum, True, True)
        mm(b("psC1", 410, 411), b("lt32", 0, 128), rowsum, True, True)
        ts(th, p, -ROUND / 2048, OP.add, 2.0, OP.min)
        emit("v", lambda: g.vector.reciprocal(inv[0], th[0]), [th], [inv], 0.14)
        act(half, th, AF.Copy, -2.0 ** -12, 0.5)
        ts(q, b("psC1", 409, 410), inv, OP.mult, ROUND, OP.add)
        ts(at, q, -ROUND, OP.add, th, OP.mult)
        ts(at, at, b("psC1", 410, 411), OP.subtract, half, OP.subtract)
        for par in range(2):
            y = b("yy", 128 * par, 128 * par + 128)
            ts(y, b("ex", par, 256, 2), at, OP.subtract, inv, OP.mult)
            ts(b("off16", 128 * par, 128 * par + 128), y, q, OP.add, -ROUND, OP.add)

    banks = (("psB", 0), ("psB", 512), ("psD", 0), ("psD", 512), ("psA", 0), ("psA", 512))
    for a in range(16):
        name, at = banks[a % 6]
        for par in range(2):
            p, lo = b(name, at + 128 * par, at + 128 * par + 128), 16 + 256 * a + par
            mm(p, ident, b("ptb", lo, lo + 255, 2), True, False, par == 1)
            mm(p, nident, b("ptb", lo - 1, lo + 254, 2), False, True)
        apart[0] = True
        if a < SHARE:
            act(b("diffp", a, 4096, 16), b(name, at, at + 256), AF.Copy)
        else:
            cp(b("diffp", a, 4096, 16), b(name, at, at + 256))
        apart[0] = False

    ZSRC = [(("zin0", 0), ("zin0", 128)), (("zr1", 0), ("zin1", 0)), (("zr2", 0), ("zin2", 0)), (("zr3", 0), ("zc0", 0))]

    def one_round(t):
        cc = (t % 4, (t + 1) % 4)
        zz = [b(n, lo, lo + 128) for n, lo in ZSRC[t]]
        prefix()

        zeroed = [b("big", WIN * par, WIN * par + 4096) for par in range(2)]
        for par in range(2):
            bigw, offs, dif = b("big", WIN * par, WIN * par + WIN), b("off16", 128 * par, 128 * par + 128), b("diffp", 2048 * par, 2048 * par + 2048)
            emit("v", lambda bigw=bigw, offs=offs, dif=dif: g.vector.tensor_copy(bigw[0].indirect(offs[0]), dif[0]), [dif, offs], [bigw],
                 dif[4] * SCATTER * CYCLE)
        scan(b("pE", 0, 4096), zeroed[0], zeroed[1], OP.add, OP.add)

        def clear():
            waits("g", [], zeroed)
            g.remote_dma_fused([RemoteDMATransfer(dst_ids=[aides[k]], dma_engine_mask=1 << topo.engines(core, helper)[k],
                                                  remote_sem=T.sem["hz%d" % t]) for k in range(2)], local_sem=T.sem.ls)
            count["ls"] += 2
            for x, name, who in zip(zeroed, ("ba%d" % t, "bb%d" % t), (helper, sweeper)):
                count[name] = popcount(topo.mask(who, core))
                note(x, True, name, count[name], "net")

        if t < ROUNDS - 1:
            in_turn()
            remote(clear, [swept, lent], zeroed, 11.0, 0.0)

        wrow, woff = b("ptb", 16, 4112), b("woff", 8, 264)
        dma("y", [((T.ptb[0::16, 16:4112], "ptb", 16, 4112), woff)], 0.6)
        act(b("wcap", 0, 256), woff, AF.Relu, 264.0, -2.0)
        act(b("wcap", 0, 256), b("wcap", 0, 256), AF.Copy, 8.0, -1.0)
        members = []
        for m in range(2):
            for k in range(4):
                members += [len(calls)] * (MEMBERS[t][4 * m + k] == "s")
                gath(MEMBERS[t][4 * m + k], b("wg%d" % m, BLK * k, BLK * k + BLK), wrow, b("lm16", 256 * cc[m] + 64 * k, 256 * cc[m] + 64 * k + 64))
            apart[0] = True
            p = b("psC%d" % m, SEG - 1, 8 * SEG, SEG)
            group([(p, rows["sum"], b("one", 0, 8, 1, 2))] +
                  [(p, b("wg%d" % m, 2048 * (i // 16) + i % 16, 2048 * (i // 16) + 2048, 16), b("rs8", 0, 8)) for i in range(32)])
            if m == 0:
                mm(b("psC0", SEG - 2, 8 * SEG, SEG), b("one", 0, 128, 1, 1), b("zero", 0, 8, 1, 1), True, True)
            apart[0] = False

        zname, zlo = ZSRC[t][0]
        u = b("psA", 512, 576, 1, 16)
        group([(u, b("uw", 1 - par, 17 - par), b(zname, zlo + par, zlo + 128, 2)) for par in range(2)])
        act(b("uu", 0, 64, 1, 16), u, AF.Copy, 0.0, -1.0)
        act(b("uu", 64, 128, 1, 16), u, AF.Copy)
        act(b("dA", 0, 128), ident, AF.Copy, 0.0, b("a16", 0, 1))
        p, terms = b("psA", 0, 384), []
        for k, (first, ones) in enumerate((("mid", none), ("-2^16", one))):
            terms += [(p, rows[first], cst(384))]
            terms += [(b("psA", 64 * bk, 64 * bk + 64), rows["lanes" + "-+"[k]], b("lane", 0, 64, 1, 2)) for bk in range(6)]
            terms += [(b("psA", lo, lo + 128), b("dA", 0, 128), ones) + (True,) * (lo + k == 0) for lo in range(0, 384, 128)]
            terms += [(b("psA", 64 * bk, 64 * bk + 64), b("kl", 128 * bk, 128 * bk + 128, 1, 16), b("uu", 64 * k, 64 * k + 64, 1, 16))
                      + (True,) * (bk == 0) for bk in range(6)]
            terms += [(p, rows[("2^16", "16")[k]], cst(384))]
        group(terms, True)
        ts(b("pos16", 0, 384), p, -(1.5 * 2.0 ** 27 + 127 * 65536.0), OP.add, 0.0625, OP.mult)

        group([(b("psB", 128, 256), zz[1], ident), (b("psB", 128, 256), zz[0], nident)])
        if REPEATER[t] == "g":
            act(b("zT", 128, 256), b("psB", 128, 256), AF.Copy)
            apart[0] = True
            for a in range(8):
                asel(b("zrep", a, BLK, 8), zz[0], [[0, 128]], OP.is_ge, 0, 0)
            apart[0] = False
        else:
            mm(b("psB", 0, 128), zz[0], ident, True, True)
            act(b("zT", 0, 256), b("psB", 0, 256), AF.Copy)
            for lo in range(0, BLK, 512):
                mm(b("psD", lo, lo + 512), b("zT", 0, 128), b("ind", lo, lo + 512), True, True)
            act(b("zrep", 0, BLK), b("psD", 0, BLK), AF.Copy, 0.0, -1.0 / 15.0)

        nets = [b("big", OP_ + bk * BLK, OP_ + bk * BLK + BLK) for bk in range(6)]
        turn, win, zrep = 0, b("pE", 0, 4096), b("zrep", 0, BLK)
        for bk, net in enumerate(nets):
            off = b("pos16", 64 * bk, 64 * bk + 64)
            if bk:
                follows[len(calls)] = len(calls) - 1
            if bk < max(FOLD[t]):
                gathered = len(calls)
            emit("v", lambda net=net, off=off: g.vector.tensor_tensor(net[0], win[0].indirect(off[0]), zrep[0], OP.subtract),
                 [win, off, zrep], [net], BLK * GATHER * CYCLE)
        tested = len(calls)
        for bk in range(6):
            at = nets[bk][2]
            for m in range(2):
                lo, how = (OI0, OI1)[m] + BLK * bk, TESTS[t][2 * bk + m]
                both, over, grain = how == "D", OI2 + BLK * (bk % 2), BLK
                if how.islower():
                    how, grain = how.upper(), 512
                if m == 1 or how in "ST":
                    ps, turn = BLK * (turn % 3), turn + 1
                    for h in range(2):
                        p = b("psT", ps + 512 * h, ps + 512 * h + 512)
                        group([(p, id15, b("big", at + 512 * h, at + 512 * h + 512))] +
                              [(p, b("zT", 128, 256), b("ind", 512 * h, 512 * h + 512))] * m + [(p, rows["2048"], cst(512, 2))] * (how == "S"))
                for x in range(0, BLK, grain):
                    near, net = b("big", lo + x, lo + x + grain), b("big", at + x, at + x + grain)
                    p = b("psT", ps + x, ps + x + grain) if m == 1 or how in "ST" else net
                    if both:
                        ts(near, net, -68.0, OP.is_ge)
                        ts(b("big", over, over + BLK), net, 68.0, OP.is_gt, -1.0, OP.mult)
                    elif how == "A":
                        act(near, p, AF.Abs)
                        ts(near, near, 1024.0 if m else 68.0, OP.is_le)
                    elif how == "S":
                        act(near, p, AF.Silu, -2.0 ** 27, 2.0 ** -8)
                    else:
                        ts(near, p, BIG, OP.add, BIG, OP.is_equal)
                apart[0] = True
                for a in range(8):
                    p = b("psC%d" % m, 8 * bk + a, 8 * SEG, SEG)
                    mm(p, b("big", lo + a, lo + BLK, 8), b("bis" if how == "S" else "bi8", 0, 8), True, not both, a > 0)
                    if both:
                        mm(p, b("big", over + a, over + BLK, 8), b("bi8", 0, 8), False, True)
                apart[0] = False

        if t in EAGER:
            follows.update({i: gathered for i in range(tested, len(calls)) if calls[i][0] == "v"})
        if t in SUMMED:
            follows.update({i: members[-1] for i in range(tested, len(calls)) if calls[i][0] == "s"})
            follows.update(zip(members[1:], members))

        for piece, (part, lo, hi) in enumerate(folds(t)):
            home = b("pE", 4096 + BLK * part + lo, 4096 + BLK * part + hi)
            folded = [b("big", x[2] + lo, x[2] + hi) for x in nets[:FOLD[t][part]]]

            def fold(piece=piece, part=part, home=home, folded=folded):
                at, name = 2 * BLK * t + home[2] - 4096, "%d%d" % (t, piece)
                waits("g", folded, [home])
                g.remote_dma_fused([RemoteDMATransfer(dst_ids=[DstId(rid=hrid, pnc=hpid)], dma_engine_mask=there, remote_sem=T.sem["h" + name],
                                                      srcs=[x[0] for x in folded], dsts=[T.big[:, at:at + home[4]]], alu_op=2 + part)],
                                   local_sem=T.sem["lf%d" % t])
                count["b" + name] = popcount(back)
                note(home, True, "b" + name, count["b" + name], "net")
                count["lf%d" % t] = len(folds(t)) * popcount(there)
                note(b("big", OP_, OP_ + BLK * FOLD[t][part]), False, "lf%d" % t, count["lf%d" % t], "net")

            in_turn()
            remote(fold, folded + [lent], [home], 4.7 + 0.8 * (hi - lo) / BLK, SOURCE * len(folded) * (hi - lo) / BLK)
        ends = []
        for part in range(2):
            mask, keep, take = ("mkx", OP.min, OP.max) if part == 0 else ("mkn", OP.max, OP.min)
            end = None
            for k, x in enumerate(nets[FOLD[t][part]:] + [None]):
                name, lo = ("wg%d" % part, BLK * k) if x else ("pE", 6144 + BLK * part)
                if x:
                    scan(b(name, lo, lo + BLK), b(mask, 0, BLK), x, keep, take)
                else:
                    for x, y in [f[1:] for f in folds(t) if f[0] == part]:
                        scan(b(name, lo + x, lo + y), b(mask, x, y), b(name, lo + x - 2048, lo + y - 2048), keep, take)
                if end:
                    tt(b("mx", 128 * part, 128 * part + 128), end, b(name, lo + 7, lo + BLK, 8), take)
                end = b("mx", 128 * part, 128 * part + 128) if end else b(name, lo + 7, lo + BLK, 8)
            ends.append(end)

        free = [BLK * ((turn + k // 2) % 3) + 512 * (k % 2) for k in range(6)]
        wnew = b("psT", free[0], free[0] + 256)
        mm(wnew, b("none", 0, 128, 1, 1), cst(256), True, False, False, True)
        mm(wnew, ident, woff, False, False, True, True)
        for m in range(2):
            name = "psC%d" % m
            scan(b("am%d" % m, 0, 8 * SEG), b("amk", 0, 8 * SEG), b(name, 0, 8 * SEG), OP.min, OP.max)
            chosen = b("am%d" % m, SEG - 2, 8 * SEG, SEG)
            if m == 0:
                apart[0] = True
                act(b("psC1", SEG - 2, 8 * SEG, SEG), chosen, AF.Copy, 23.0, -1.0)
                apart[0] = False
            ts(b("xs", 16 + 8 * m, 24 + 8 * m), b("am%d" % m, SEG - 1, 8 * SEG, SEG), 11.5, OP.is_lt)
            act(b("xs", 8 * m, 8 * m + 8), chosen, AF.Sign, 11.5, -1.0)
            p = b("psC%d" % (1 - m), 400, 408)
            mm(p, b("crep", 0, 128), b("xs", 16 + 8 * m, 24 + 8 * m), True, True)
            tt(b("bw", 8 * m, 8 * m + 8), p, b("bi8", 0, 8), OP.mult)
            where = [(name, 0), (name, 128)] if m == 0 or not HALVES else [(name, 0), ("psT", free[4])]
            for part in ([0, 1],) if where[1][1] == 128 else ([0], [1]):
                x, lo = where[part[0]]
                p = b(x, lo, lo + 128 * len(part))
                terms = [(b(x, where[h][1] + a, where[h][1] + 128, 16), b("rr", SLOT[cc[m]] + 256 * a + 128 * h, SLOT[cc[m]] + 256 * a + 128 * h + 128),
                          b("bw", 8 * m, 8 * m + 8)) for h in part for a in range(16)]
                group([(p, b("one", 0, 128, 1, 1), cst(p[4])), terms[0] + (True,)] + terms[1:], True)
                r, mark = b("r%d" % m, 128 * part[0], 128 * part[0] + p[4]), b("mk", 256 * m + 128 * part[0], 256 * m + 128 * part[0] + p[4])
                act(r, p, AF.Copy, 2.0 ** -9)
                tt(mark, r, p, OP.is_gt)
                for h in part:
                    mm(b("psT", free[0] + 128 * h, free[0] + 128 * h + 128), b("mk", 256 * m + 128 * h, 256 * m + 128 * h + 128), id15,
                       False, m + h == 2, h > part[0], True)
        tt(b("w1", 0, 256), wnew, b("wcap", 0, 256), OP.min)
        scan(b("ex", 0, 256), b("zeros", 0, 256), b("w1", 0, 256), OP.add, OP.add)
        mm(b("psC0", 411, 412), boq, b("ex", 255, 256), True, True)
        ts(b("smv", 12, 13), b("psC0", 411, 412), 7168.5 / 4096, OP.is_lt, 0.5, OP.max)
        ts(woff, b("w1", 0, 256), b("smv", 12, 13), OP.mult, 128.25, OP.add)

        xT, em = b("xT", 0, 128, 1, 32), [b("em", 128 * k, 128 * k + 128, 1, 32) for k in range(4)]
        mm(b("psT", free[1], free[1] + 128, 1, 32), b("xs", 0, 32), ident, True, True)
        act(xT, b("psT", free[1], free[1] + 128, 1, 32), AF.Identity, b("sgn", 1, 2, 1, 32), b("sgn", 0, 1, 1, 32))
        group([(b("psT", free[1] + 128, free[1] + 256), x, xT) for x in em])
        mm(b("psT", free[1] + 256, free[1] + 257), odd, b("one", 0, 1, 1, 1), True, True, True)
        total(b("a16", 0, 1), b("psT", free[1] + 128, free[1] + 257), 32.0, -16.0 / FAR)
        act(b("yab", t, t + 1), b("a16", 0, 1), AF.Copy, 0.0, 0.0625)

        halves = [[b("psT", free[k] + 128 * m, free[k] + 128 * m + 128) for m in range(2)] for k in (2, 3)]
        for m in range(2):
            mm(halves[0][m], nident, zz[m], True, False, m == 1)
            mm(halves[0][m], em[m], xT, False, True)
        act(b("zs", 0, 256), b("psT", free[2], free[2] + 256), AF.Copy, FAR, -1.0)
        p = b("psT", free[3], free[3] + 256)
        group([(p, rows["3/8"], cst(256)), (halves[1][0], ident, zz[0]), (halves[1][1], hid, zz[0]), (halves[1][1], hid, zz[1]),
               (halves[1][0], em[0], xT, True), (halves[1][1], em[1], xT)] +
              [(halves[1][m], qid, x) + (True,) * (m == 0) for x in ends for m in range(2)] +
              [(p, rows["1"], cst(256)), (p, rows["-1"], cst(256))], True)
        tt(b("zo%d" % t, 0, 256), p, b("zs", 0, 256), OP.min)
        for kind in (("u0", "c0"), ("u1", "f1"), ("u2", "f2"), ("f3", "f0"))[t]:
            send(kind)

    for t in range(ROUNDS):
        one_round(t)
        if t == 1:
            narrowed(3)

    ts(b("ywb", 0, 256), b("woff", 8, 264), -128.0, OP.add)
    dma("y", [(T.yz[:, 128:256], b("zf1", 0, 128)), (T.yz[:, 256:384], b("zf2", 0, 128))], 0.8)
    dma("y", [(T.yw[:], b("ywb", 0, 256))], 0.7)
    dma("y", [(T.ya[:], (T.yab[0::16, 0:4], "yab", 0, 4))], 0.1)
    dma("s", [(T.yz[:, 384:512], b("zf3", 0, 128))], 0.4)
    dma("y", [(T.yz[:, 0:128], b("zf0", 0, 128))], 0.4)

    if not PLAN:
        PLAN.extend(plan(calls, follows))
    for i in PLAN:
        for issue in calls[i][1]:
            issue()
    for sem, val in count.items():
        if waited["g"].get(sem, 0) < val:
            g.wait_ge(T.sem[sem], val)
